import numpy as np
import ml_dtypes


def mxq(x, axis, fmt="e4m3"):
    dtype, down = {"e4m3": (ml_dtypes.float8_e4m3fn, 7), "e5m2": (ml_dtypes.float8_e5m2, 14)}[fmt]
    v = np.moveaxis(np.asarray(x, np.float32).astype(ml_dtypes.bfloat16).astype(np.float64), axis, -1)
    blocks = v.reshape(v.shape[:-1] + (-1, 32))
    amax = np.abs(blocks).max(-1, keepdims=True)
    byte = np.maximum(np.where(amax > 0, np.frexp(amax)[1] - 1 + 127, 0) - down, 1)
    scale = np.exp2(byte - 127.0)
    codes = (blocks / scale).astype(np.float32).astype(dtype).astype(np.float64)
    return np.moveaxis((codes * scale).reshape(v.shape), -1, axis)


WIDE = False


def mx_kscale(k):
    if not WIDE:
        return np.ones(k)
    levels = np.array([24, -24, 12, -12, 0])
    if k % 512:
        return np.exp2(np.random.permutation(np.resize(levels, k // 32))).repeat(32)
    a = np.empty((k // 512, 16))
    for p in range(k // 512):
        a[p, :8] = np.random.permutation(np.resize(levels, 8))
        for g in range(8):
            far = levels[np.abs(levels - a[p, g]) >= 10]
            a[p, g + 8] = far[np.random.randint(len(far))]
    return np.exp2(a.ravel()).repeat(32)


def f64(x):
    return np.asarray(x).astype(np.float64)


def striped(idx):
    return np.tile(idx.reshape(-1, 16).T, (8, 1)).astype(np.uint16)


def unstriped(offs):
    return offs[:16].T.reshape(-1).astype(np.int64)


E2M1 = np.array([0.0, 0.5, 1.0, 1.5, 2.0, 3.0, 4.0, 6.0, -0.0, -0.5, -1.0, -1.5, -2.0, -3.0, -4.0, -6.0])


def pack_weight(w, fmt):
    k, n = w.shape
    w = f64(np.asarray(w, np.float32).astype(ml_dtypes.bfloat16)).reshape(k // 32, 32, n)
    amax = np.abs(w).max(1)
    if fmt == "e4m3":
        byte = np.frexp(amax)[1] - 1 + 127 - 7
    else:
        mant, ex = np.frexp(amax / 6.0)
        byte = np.where(mant > 0.5, ex, ex - 1) + 127
    byte = np.clip(np.where(amax > 0, byte, 1), 1, 254)
    scaled = (w * np.exp2(127.0 - byte)[:, None, :]).reshape(k, n).astype(np.float32)
    by_word = np.ascontiguousarray(scaled.reshape(k // 512, 128, 4, n).transpose(0, 1, 3, 2))
    if fmt == "e4m3":
        words = by_word.astype(ml_dtypes.float8_e4m3fn).view(np.uint8)
    else:
        c = by_word.astype(ml_dtypes.float4_e2m1fn).view(np.uint8) & 0xF
        words = (c[..., 0::2] | (c[..., 1::2] << 4)).reshape(k // 512, 128, 2 * n)
    return np.ascontiguousarray(words), np.ascontiguousarray(byte.astype(np.uint8).reshape(k // 512, 16, n))


def unpack_weight(words, scales, fmt):
    g, _, n = scales.shape
    words = np.ascontiguousarray(words).reshape(g, 128, n, -1)
    if fmt == "e4m3":
        vals = words.view(ml_dtypes.float8_e4m3fn).astype(np.float64)
    else:
        nib = np.empty((g, 128, n, 4), np.uint8)
        nib[..., 0::2] = words & 0xF
        nib[..., 1::2] = words >> 4
        vals = E2M1[nib]
    vals = vals * np.repeat(np.exp2(scales.astype(np.float64) - 127.0), 8, axis=1)[..., None]
    return vals.transpose(0, 1, 3, 2).reshape(g * 512, n)


def pack_table4(v):
    words, scales = pack_weight(v, "e2m1")
    g, t = words.shape[0] // 2, v.shape[1]
    return np.ascontiguousarray(words.reshape(g, 2, 128, t, 2).transpose(0, 2, 3, 1, 4).reshape(g, 128, t, 4)), scales


def unpack_table4(words, scales):
    g, _, t, _ = words.shape
    return unpack_weight(words.reshape(g, 128, t, 2, 2).transpose(0, 3, 1, 2, 4).reshape(2 * g, 128, 2 * t), scales, "e2m1")


def gelu(f):
    return 0.5 * f * (1.0 + np.tanh(np.sqrt(2.0 / np.pi) * (f + 0.044715 * f**3)))


K, R, N, T, J = 1024, 512, 512, 2048, 1024


def setup_inputs():
    n = np.random.standard_normal
    s = mx_kscale(K)[:, None]
    u = mx_kscale(R)[:, None]
    wd = n((R, N)) / np.sqrt(R) / u
    wd4 = pack_weight(wd, "e2m1")
    wdrest = wd - unpack_weight(*wd4, "e2m1")
    p_tab = pack_table4(n((K, T)) * s)
    p_wu = pack_weight(n((K, R)) / np.sqrt(K) / s, "e4m3")
    p_wd8 = pack_weight(wdrest, "e4m3")
    return {
        "tab_words": p_tab[0],
        "tab_scales": p_tab[1],
        "wu_words": p_wu[0],
        "wu_scales": p_wu[1],
        "sm": (np.random.uniform(0.5, 2.0, R) * u[:, 0]).astype(np.float32),
        "wd4_words": wd4[0],
        "wd4_scales": wd4[1],
        "wd8_words": p_wd8[0],
        "wd8_scales": p_wd8[1],
        "b": (0.3 * n(N)).astype(np.float32),
        "wgo": np.tile(np.random.uniform(0.5, 2.0, J), (128, 1)).astype(np.float32),
        "offs": striped(np.random.permutation(T)[:J]),
    }


def reference(tab_words, tab_scales, wu_words, wu_scales, sm, wd4_words, wd4_scales, wd8_words, wd8_scales, b, wgo, offs):
    idx = unstriped(offs)
    tab_ = unpack_table4(tab_words, tab_scales)[:, idx]
    wu_ = unpack_weight(wu_words, wu_scales, "e4m3")
    a = wu_.T @ tab_
    h = f64(sm)[:, None] * gelu(a)
    h_ = mxq(h, 0, "e4m3")
    wd4_ = unpack_weight(wd4_words, wd4_scales, "e2m1")
    wd8_ = unpack_weight(wd8_words, wd8_scales, "e4m3")
    y = wd4_.T @ h_ + wd8_.T @ h_
    out = np.zeros((N, T))
    out[:, idx] = f64(wgo)[0] * (y + f64(b)[:, None])
    return out

@@ -1,0 +1,229 @@
+from contextlib import ExitStack
+
+import concourse.mybir as mybir
+
+K, R, N, T, J = 1024, 512, 512, 2048, 1024
+FLOPS = 2 * K * R * J + 2 * 2 * R * N * J
+
+F32 = mybir.dt.float32
+BF16 = mybir.dt.bfloat16
+I32 = mybir.dt.int32
+U32 = mybir.dt.uint32
+U16 = mybir.dt.uint16
+U8 = mybir.dt.uint8
+FP8X4 = mybir.dt.float8_e4m3fn_x4
+FP4X4 = mybir.dt.float4_e2m1fn_x4
+ACT = mybir.ActivationFunctionType
+MULT = mybir.AluOpType.mult
+
+P = 128
+PACK = 4
+PASSES = K // (P * PACK)
+CHUNK = 256
+CHUNKS = J // CHUNK
+HALF = 128
+BLOCKS = N // P
+ROWS0 = 96
+
+
+def tile_list_modp_gelu_res_noneb_kernel(
+    tc, tab_words, tab_scales, wu_words, wu_scales, sm, wd4_words, wd4_scales, wd8_words, wd8_scales, b, wgo, offs, out
+):
+    nc = tc.nc
+    with ExitStack() as ctx:
+        lists = ctx.enter_context(tc.tile_pool(name="lists", bufs=1))
+        pool = ctx.enter_context(tc.tile_pool(name="pool", bufs=1))
+        placed = ctx.enter_context(tc.tile_pool(name="placed", bufs=1))
+        psum = ctx.enter_context(tc.psum_pool(name="psum", bufs=1))
+
+        def sbuf(shape, dtype, name, tag=None):
+            return pool.tile(shape, dtype, name=name, tag=tag or name, align_bytes=64)
+
+        offsets = lists.tile([P, J // 16], U16, name="offsets")
+        nc.sync.dma_start(offsets[:], offs)
+
+        wu_sc_raw = sbuf([P, PASSES, R], U8, "wu_sc_raw")
+        nc.gpsimd.memset(wu_sc_raw[:].bitcast(I32), 0)
+        tab_sc = sbuf([P, T], U8, "tab_sc")
+        nc.gpsimd.memset(tab_sc[0:ROWS0, :].bitcast(I32), 0)
+        nc.sync.dma_start(tab_sc[ROWS0:P, :].bitcast(I32), tab_scales.rearrange("a q t -> (a q) t").bitcast(I32))
+        for q in range(4):
+            nc.scalar.dma_start(
+                wu_sc_raw[32 * q : 32 * q + 4, :, :].bitcast(I32),
+                wu_scales[:, 4 * q : 4 * q + 4, :].rearrange("a r n -> r a n").bitcast(I32),
+            )
+        wu_raw = sbuf([P, PASSES, R], U32, "wu_raw")
+        nc.sync.dma_start(wu_raw[:].bitcast(I32), wu_words.rearrange("a p r i -> p a (r i)").bitcast(I32))
+        tab = sbuf([P, T], U32, "tab")
+        nc.sync.dma_start(tab[:].bitcast(I32), tab_words[0].rearrange("p t i -> p (t i)").bitcast(I32))
+
+        v_sc = sbuf([P, PASSES, J], U8, "v_sc")
+        nc.vector.memset(v_sc[:].bitcast(I32), 0)
+        picked_sc = sbuf([P, J], U8, "picked_sc")
+        nc.vector.tensor_copy(picked_sc[:], tab_sc[:].indirect(offsets[:]))
+        for a in range(PASSES):
+            for q in range(4):
+                row = ROWS0 + 16 * a + 4 * q
+                nc.sync.dma_start(v_sc[32 * q : 32 * q + 4, a, :].bitcast(I32), picked_sc[row : row + 4, :].bitcast(I32))
+
+        wu = sbuf([P, PASSES, R], U32, "wu")
+        nc.vector.tensor_copy(
+            wu[:].rearrange("p a (t c i) -> p a c t i", t=PACK, i=4),
+            wu_raw[:].rearrange("p a (c i t) -> p a c t i", t=PACK, i=4),
+        )
+        wu_sc = sbuf([P, PASSES, R], U8, "wu_sc")
+        nc.vector.tensor_copy(
+            wu_sc[:].rearrange("p a (t c i) -> p a c t i", t=PACK, i=16),
+            wu_sc_raw[:].rearrange("p a (c i t) -> p a c t i", t=PACK, i=16),
+        )
+
+        sm_t = sbuf([P, PACK], F32, "sm_t", tag="wu_sc_raw")[:]
+        b_t = sbuf([P, BLOCKS], F32, "b_t")[:]
+        nc.sync.dma_start(sm_t, sm.rearrange("(p t) -> p t", t=PACK))
+        wd = sbuf([P, 6 * N], U8, "wd", tag="wu_raw")
+        wd8 = wd[:, 0 : 4 * N]
+        wd4 = wd[:, 4 * N : 6 * N]
+        nc.sync.dma_start(wd8.bitcast(I32), wd8_words[0].rearrange("p n i -> p (n i)").bitcast(I32))
+        nc.sync.dma_start(wd4.bitcast(I32), wd4_words[0].bitcast(I32))
+        with nc.allow_non_contiguous_dma(reason="one bias value a partition and block"):
+            nc.gpsimd.dma_start(b_t, b.rearrange("(c p) -> p c", p=P))
+
+        h_codes = sbuf([P, J], U32, "h_codes")
+        h_sc = sbuf([P, J], U8, "h_sc")
+
+        def pick(c, tag=None):
+            picked = sbuf([P, CHUNK], U32, "picked%d" % c, tag)
+            nc.vector.tensor_copy(picked[:], tab[:].indirect(offsets[:, c * CHUNK // 16 : (c + 1) * CHUNK // 16]))
+            v = sbuf([P, PASSES, 2 * CHUNK], U8, "v%d" % c)
+            nc.vector.tensor_copy(v[:].bitcast(U16), picked[:].bitcast(U16).rearrange("p (j a) -> p a j", a=PASSES))
+            return v
+
+        def up(c, half, v, slot):
+            bank = psum.tile([P, PACK, HALF], F32, name="a_bank", tag="bank%d" % slot)
+            j0 = c * CHUNK + half * HALF
+            for t in range(PACK):
+                for a in range(PASSES):
+                    nc.tensor.matmul_mx(
+                        out=bank[:, t, :],
+                        lhsT=wu[:, a, t * P : (t + 1) * P].bitcast(FP8X4),
+                        lhsT_scale=wu_sc[:, a, t * P : (t + 1) * P],
+                        rhs=v[:, a, 2 * half * HALF : 2 * (half + 1) * HALF].bitcast(FP4X4),
+                        rhs_scale=v_sc[:, a, j0 : j0 + HALF],
+                        start=(a == 0),
+                        stop=(a == PASSES - 1),
+                    )
+            return bank
+
+        def quantise(c, woven):
+            cols = slice(c * CHUNK, (c + 1) * CHUNK)
+            nc.vector.quantize_mx(out=h_codes[:, cols].bitcast(FP8X4), scales=h_sc[:, cols], in_=woven[:])
+
+        def hidden_first(v):
+            woven = placed.tile([P, CHUNK * PACK], BF16, name="woven0", offset=4 * T - CHUNK * PACK, align_bytes=64)
+            for half in range(CHUNK // HALF):
+                bank = up(0, half, v, half)
+                g = sbuf([P, HALF, PACK], F32, "g0_%d" % half)
+                nc.scalar.activation(g[:], bank[:].rearrange("p t j -> p j t"), ACT.Gelu_apprx_tanh)
+                nc.vector.tensor_tensor(
+                    woven[:, half * HALF * PACK : (half + 1) * HALF * PACK].rearrange("p (j t) -> p j t", t=PACK),
+                    g[:],
+                    sm_t.unsqueeze(1).to_broadcast([P, HALF, PACK]),
+                    MULT,
+                )
+            quantise(0, woven)
+
+        def hidden(c, half, v, slot, woven):
+            bank = up(c, half, v, slot)
+            g = sbuf([P, PACK, HALF], F32, "g%d_%d" % (c, half))
+            nc.scalar.activation(g[:], bank[:], ACT.Gelu_apprx_tanh)
+            planes = sbuf([P, PACK * HALF], BF16, "planes%d_%d" % (c, half))
+            for t in range(PACK):
+                nc.scalar.activation(planes[:, t * HALF : (t + 1) * HALF], g[:, t, :], ACT.Copy, scale=sm_t[:, t : t + 1])
+            nc.scalar.copy(
+                woven[:, half * HALF * PACK : (half + 1) * HALF * PACK].rearrange("p (c i t) -> p c t i", t=PACK, i=4),
+                planes[:].rearrange("p (t c i) -> p c t i", t=PACK, i=4),
+            )
+            return planes
+
+        def down(block, j0, width, narrow, slot):
+            bank = psum.tile([P, width], F32, name="y_bank", tag="bank%d" % slot)
+            cols = slice(block * P, (block + 1) * P)
+            nc.tensor.matmul_mx(
+                out=bank[:],
+                lhsT=wd8[:, 4 * block * P : 4 * (block + 1) * P].bitcast(FP8X4),
+                lhsT_scale=wd8_sc[:, cols],
+                rhs=h_codes[:, j0 : j0 + width].bitcast(FP8X4),
+                rhs_scale=h_sc[:, j0 : j0 + width],
+                start=True,
+                stop=False,
+            )
+            for s in range(0, width, narrow):
+                nc.tensor.matmul_mx(
+                    out=bank[:, s : s + narrow],
+                    lhsT=wd4[:, 2 * block * P : 2 * (block + 1) * P].bitcast(FP4X4),
+                    lhsT_scale=wd4_sc[:, cols],
+                    rhs=h_codes[:, j0 + s : j0 + s + narrow].bitcast(FP8X4),
+                    rhs_scale=h_sc[:, j0 + s : j0 + s + narrow],
+                    start=False,
+                    stop=(s + narrow == width),
+                )
+            return bank
+
+        def add_bias(y, bank, block):
+            nc.scalar.activation(y, bank[:], ACT.Identity, bias=b_t[:, block : block + 1])
+
+        def scatter(page, y, j0, width):
+            nc.vector.tensor_tensor(
+                page[:].indirect(offsets[:, j0 // 16 : (j0 + width) // 16]), y, weight[:, j0 : j0 + width], MULT
+            )
+
+        picks = [pick(0)]
+        weight = sbuf([P, J], F32, "weight", tag="picked0")
+        nc.sync.dma_start(weight[:], wgo)
+        wd4_sc = sbuf([P, N], U8, "wd4_sc")
+        wd8_sc = sbuf([P, N], U8, "wd8_sc", tag="tab_sc")
+        nc.gpsimd.memset(wd8_sc[:].bitcast(I32), 0)
+        nc.gpsimd.memset(wd4_sc[:].bitcast(I32), 0)
+        for q in range(4):
+            nc.sync.dma_start(wd8_sc[32 * q : 32 * q + 4, :].bitcast(I32), wd8_scales[0, 4 * q : 4 * q + 4, :].bitcast(I32))
+            nc.gpsimd.dma_start(wd4_sc[32 * q : 32 * q + 4, :].bitcast(I32), wd4_scales[0, 4 * q : 4 * q + 4, :].bitcast(I32))
+        pages = [sbuf([P, T], F32, "page0")]
+        picks.append(pick(1))
+        hidden_first(picks[0])
+        picks.append(pick(2))
+        picks.append(pick(3, "g0_1"))
+        nc.vector.memset(pages[0][:], 0.0)
+        for i in range(2):
+            pages.append(placed.tile([P, T], F32, name="page%d" % (i + 1), offset=4 * T * i, align_bytes=64))
+            nc.gpsimd.memset(pages[i + 1][:], 0.0)
+
+        last = BLOCKS - 1
+        wovens = [None] + [sbuf([P, CHUNK * PACK], BF16, "woven%d" % c) for c in range(1, CHUNKS)]
+        hidden(1, 0, picks[1], 2, wovens[1])
+        for c in range(CHUNKS):
+            slots = [last * ((c + 1) % 2) + block for block in range(last)]
+            banks = [down(block, c * CHUNK, CHUNK, HALF, slots[block]) for block in range(last)]
+            for block in range(last - 1):
+                y = sbuf([P, CHUNK], F32, "y%d_%d" % (c, block))
+                add_bias(y[:], banks[block], block)
+                scatter(pages[block], y[:], c * CHUNK, CHUNK)
+                if c == CHUNKS - 1:
+                    nc.sync.dma_start(out[block * P : (block + 1) * P, :], pages[block][:])
+            if c + 1 < CHUNKS:
+                y = hidden(c + 1, 1, picks[c + 1], slots[0], wovens[c + 1])[:].bitcast(F32)
+                quantise(c + 1, wovens[c + 1])
+            else:
+                y = sbuf([P, CHUNK], F32, "y_end")[:]
+            add_bias(y, banks[last - 1], last - 1)
+            scatter(pages[last - 1], y, c * CHUNK, CHUNK)
+            if c + 2 < CHUNKS:
+                hidden(c + 2, 0, picks[c + 2], slots[1], wovens[c + 2])
+        nc.sync.dma_start(out[(last - 1) * P : last * P, :], pages[last - 1][:])
+
+        page = sbuf([P, T], F32, "page3", tag="woven%d" % (CHUNKS - 1))
+        nc.gpsimd.memset(page[:], 0.0)
+        y = sbuf([P, J], F32, "y_last")
+        for j0 in range(0, J, 512):
+            add_bias(y[:, j0 : j0 + 512], down(last, j0, 512, 512, 2 * last + j0 // 512), last)
+        scatter(page, y[:], 0, J)
+        nc.sync.dma_start(out[last * P : N, :], page[:])

@@ -33,7 +33,6 @@ def tile_list_modp_gelu_res_noneb_kernel(
     with ExitStack() as ctx:
         lists = ctx.enter_context(tc.tile_pool(name="lists", bufs=1))
         pool = ctx.enter_context(tc.tile_pool(name="pool", bufs=1))
-        placed = ctx.enter_context(tc.tile_pool(name="placed", bufs=1))
         psum = ctx.enter_context(tc.psum_pool(name="psum", bufs=1))
 
         def sbuf(shape, dtype, name, tag=None):
@@ -59,12 +58,22 @@ def tile_list_modp_gelu_res_noneb_kernel(
 
         v_sc = sbuf([P, PASSES, J], U8, "v_sc")
         nc.vector.memset(v_sc[:].bitcast(I32), 0)
+        pages = [sbuf([P, T], F32, "page0"), sbuf([P, T], F32, "page1")]
+        nc.vector.memset(pages[0][:], 0.0)
+        nc.vector.memset(pages[1][:, 0 : T // 2], 0.0)
         picked_sc = sbuf([P, J], U8, "picked_sc")
         nc.vector.tensor_copy(picked_sc[:], tab_sc[:].indirect(offsets[:]))
+        nc.vector.memset(pages[1][:, T // 2 : T], 0.0)
         for a in range(PASSES):
             for q in range(4):
                 row = ROWS0 + 16 * a + 4 * q
                 nc.sync.dma_start(v_sc[32 * q : 32 * q + 4, a, :].bitcast(I32), picked_sc[row : row + 4, :].bitcast(I32))
+
+        wd_sc = sbuf([P, 2, N], U8, "wd_sc", tag="tab_sc")
+        nc.gpsimd.memset(wd_sc[:].bitcast(I32), 0)
+        for q in range(4):
+            nc.sync.dma_start(wd_sc[32 * q : 32 * q + 4, 1, :].bitcast(I32), wd8_scales[0, 4 * q : 4 * q + 4, :].bitcast(I32))
+            nc.sync.dma_start(wd_sc[32 * q : 32 * q + 4, 0, :].bitcast(I32), wd4_scales[0, 4 * q : 4 * q + 4, :].bitcast(I32))
 
         wu = sbuf([P, PASSES, R], U32, "wu")
         nc.vector.tensor_copy(
@@ -77,8 +86,9 @@ def tile_list_modp_gelu_res_noneb_kernel(
             wu_sc_raw[:].rearrange("p a (c i t) -> p a c t i", t=PACK, i=16),
         )
 
-        sm_t = sbuf([P, PACK], F32, "sm_t", tag="wu_sc_raw")[:]
-        b_t = sbuf([P, BLOCKS], F32, "b_t")[:]
+        vectors = sbuf([P, 16], F32, "vectors", tag="wu_sc_raw")
+        sm_t = vectors[:, 0:PACK]
+        b_t = vectors[:, 8 : 8 + BLOCKS]
         nc.sync.dma_start(sm_t, sm.rearrange("(p t) -> p t", t=PACK))
         wd = sbuf([P, 6 * N], U8, "wd", tag="wu_raw")
         wd8 = wd[:, 0 : 4 * N]
@@ -86,7 +96,7 @@ def tile_list_modp_gelu_res_noneb_kernel(
         nc.sync.dma_start(wd8.bitcast(I32), wd8_words[0].rearrange("p n i -> p (n i)").bitcast(I32))
         nc.sync.dma_start(wd4.bitcast(I32), wd4_words[0].bitcast(I32))
         with nc.allow_non_contiguous_dma(reason="one bias value a partition and block"):
-            nc.gpsimd.dma_start(b_t, b.rearrange("(c p) -> p c", p=P))
+            nc.sync.dma_start(b_t, b.rearrange("(c p) -> p c", p=P))
 
         h_codes = sbuf([P, J], U32, "h_codes")
         h_sc = sbuf([P, J], U8, "h_sc")
@@ -119,7 +129,7 @@ def tile_list_modp_gelu_res_noneb_kernel(
             nc.vector.quantize_mx(out=h_codes[:, cols].bitcast(FP8X4), scales=h_sc[:, cols], in_=woven[:])
 
         def hidden_first(v):
-            woven = placed.tile([P, CHUNK * PACK], BF16, name="woven0", offset=4 * T - CHUNK * PACK, align_bytes=64)
+            woven = sbuf([P, CHUNK * PACK], BF16, "woven0")
             for half in range(CHUNK // HALF):
                 bank = up(0, half, v, half)
                 g = sbuf([P, HALF, PACK], F32, "g0_%d" % half)
@@ -151,7 +161,7 @@ def tile_list_modp_gelu_res_noneb_kernel(
             nc.tensor.matmul_mx(
                 out=bank[:],
                 lhsT=wd8[:, 4 * block * P : 4 * (block + 1) * P].bitcast(FP8X4),
-                lhsT_scale=wd8_sc[:, cols],
+                lhsT_scale=wd_sc[:, 1, cols],
                 rhs=h_codes[:, j0 : j0 + width].bitcast(FP8X4),
                 rhs_scale=h_sc[:, j0 : j0 + width],
                 start=True,
@@ -161,7 +171,7 @@ def tile_list_modp_gelu_res_noneb_kernel(
                 nc.tensor.matmul_mx(
                     out=bank[:, s : s + narrow],
                     lhsT=wd4[:, 2 * block * P : 2 * (block + 1) * P].bitcast(FP4X4),
-                    lhsT_scale=wd4_sc[:, cols],
+                    lhsT_scale=wd_sc[:, 0, cols],
                     rhs=h_codes[:, j0 + s : j0 + s + narrow].bitcast(FP8X4),
                     rhs_scale=h_sc[:, j0 + s : j0 + s + narrow],
                     start=False,
@@ -180,22 +190,12 @@ def tile_list_modp_gelu_res_noneb_kernel(
         picks = [pick(0)]
         weight = sbuf([P, J], F32, "weight", tag="picked0")
         nc.sync.dma_start(weight[:], wgo)
-        wd4_sc = sbuf([P, N], U8, "wd4_sc")
-        wd8_sc = sbuf([P, N], U8, "wd8_sc", tag="tab_sc")
-        nc.gpsimd.memset(wd8_sc[:].bitcast(I32), 0)
-        nc.gpsimd.memset(wd4_sc[:].bitcast(I32), 0)
-        for q in range(4):
-            nc.sync.dma_start(wd8_sc[32 * q : 32 * q + 4, :].bitcast(I32), wd8_scales[0, 4 * q : 4 * q + 4, :].bitcast(I32))
-            nc.gpsimd.dma_start(wd4_sc[32 * q : 32 * q + 4, :].bitcast(I32), wd4_scales[0, 4 * q : 4 * q + 4, :].bitcast(I32))
-        pages = [sbuf([P, T], F32, "page0")]
         picks.append(pick(1))
-        hidden_first(picks[0])
         picks.append(pick(2))
+        pages.append(sbuf([P, T], F32, "page2", tag="picked2"))
+        nc.vector.memset(pages[2][:], 0.0)
+        hidden_first(picks[0])
         picks.append(pick(3, "g0_1"))
-        nc.vector.memset(pages[0][:], 0.0)
-        for i in range(2):
-            pages.append(placed.tile([P, T], F32, name="page%d" % (i + 1), offset=4 * T * i, align_bytes=64))
-            nc.gpsimd.memset(pages[i + 1][:], 0.0)
 
         last = BLOCKS - 1
         wovens = [None] + [sbuf([P, CHUNK * PACK], BF16, "woven%d" % c) for c in range(1, CHUNKS)]
@@ -220,8 +220,7 @@ def tile_list_modp_gelu_res_noneb_kernel(
                 hidden(c + 2, 0, picks[c + 2], slots[1], wovens[c + 2])
         nc.sync.dma_start(out[(last - 1) * P : last * P, :], pages[last - 1][:])
 
-        page = sbuf([P, T], F32, "page3", tag="woven%d" % (CHUNKS - 1))
-        nc.gpsimd.memset(page[:], 0.0)
+        page = pages[0]
         y = sbuf([P, J], F32, "y_last")
         for j0 in range(0, J, 512):
             add_bias(y[:, j0 : j0 + 512], down(last, j0, 512, 512, 2 * last + j0 // 512), last)

@@ -59,11 +59,11 @@ def tile_list_modp_gelu_res_noneb_kernel(
         v_sc = sbuf([P, PASSES, J], U8, "v_sc")
         nc.vector.memset(v_sc[:].bitcast(I32), 0)
         pages = [sbuf([P, T], F32, "page0"), sbuf([P, T], F32, "page1")]
-        nc.vector.memset(pages[0][:], 0.0)
-        nc.vector.memset(pages[1][:, 0 : T // 2], 0.0)
+        nc.vector.memset(pages[0][:].bitcast(I32), 0)
+        nc.vector.memset(pages[1][:, 0 : T // 2].bitcast(I32), 0)
         picked_sc = sbuf([P, J], U8, "picked_sc")
         nc.vector.tensor_copy(picked_sc[:], tab_sc[:].indirect(offsets[:]))
-        nc.vector.memset(pages[1][:, T // 2 : T], 0.0)
+        nc.vector.memset(pages[1][:, T // 2 : T].bitcast(I32), 0)
         for a in range(PASSES):
             for q in range(4):
                 row = ROWS0 + 16 * a + 4 * q
@@ -98,8 +98,12 @@ def tile_list_modp_gelu_res_noneb_kernel(
         with nc.allow_non_contiguous_dma(reason="one bias value a partition and block"):
             nc.sync.dma_start(b_t, b.rearrange("(c p) -> p c", p=P))
 
-        h_codes = sbuf([P, J], U32, "h_codes")
+        h_first = sbuf([P, CHUNK], U32, "h_first")
+        h_rest = sbuf([P, J - CHUNK], U32, "h_rest")
         h_sc = sbuf([P, J], U8, "h_sc")
+
+        def h_codes(j0, width):
+            return (h_first[:, j0 : j0 + width] if j0 < CHUNK else h_rest[:, j0 - CHUNK : j0 - CHUNK + width]).bitcast(FP8X4)
 
         def pick(c, tag=None):
             picked = sbuf([P, CHUNK], U32, "picked%d" % c, tag)
@@ -108,8 +112,8 @@ def tile_list_modp_gelu_res_noneb_kernel(
             nc.vector.tensor_copy(v[:].bitcast(U16), picked[:].bitcast(U16).rearrange("p (j a) -> p a j", a=PASSES))
             return v
 
-        def up(c, half, v, slot):
-            bank = psum.tile([P, PACK, HALF], F32, name="a_bank", tag="bank%d" % slot)
+        def up(c, half, v):
+            bank = psum.tile([P, PACK, HALF], F32, name="a_bank", tag="a_bank", bufs=4)
             j0 = c * CHUNK + half * HALF
             for t in range(PACK):
                 for a in range(PASSES):
@@ -126,12 +130,12 @@ def tile_list_modp_gelu_res_noneb_kernel(
 
         def quantise(c, woven):
             cols = slice(c * CHUNK, (c + 1) * CHUNK)
-            nc.vector.quantize_mx(out=h_codes[:, cols].bitcast(FP8X4), scales=h_sc[:, cols], in_=woven[:])
+            nc.vector.quantize_mx(out=h_codes(c * CHUNK, CHUNK), scales=h_sc[:, cols], in_=woven[:])
 
         def hidden_first(v):
             woven = sbuf([P, CHUNK * PACK], BF16, "woven0")
             for half in range(CHUNK // HALF):
-                bank = up(0, half, v, half)
+                bank = up(0, half, v)
                 g = sbuf([P, HALF, PACK], F32, "g0_%d" % half)
                 nc.scalar.activation(g[:], bank[:].rearrange("p t j -> p j t"), ACT.Gelu_apprx_tanh)
                 nc.vector.tensor_tensor(
@@ -142,27 +146,29 @@ def tile_list_modp_gelu_res_noneb_kernel(
                 )
             quantise(0, woven)
 
-        def hidden(c, half, v, slot, woven):
-            bank = up(c, half, v, slot)
-            g = sbuf([P, PACK, HALF], F32, "g%d_%d" % (c, half))
-            nc.scalar.activation(g[:], bank[:], ACT.Gelu_apprx_tanh)
-            planes = sbuf([P, PACK * HALF], BF16, "planes%d_%d" % (c, half))
+        def hidden(c, v):
+            g = sbuf([P, PACK, CHUNK], F32, "g%d" % c, "g")
+            for half in range(CHUNK // HALF):
+                nc.scalar.activation(g[:, :, half * HALF : (half + 1) * HALF], up(c, half, v)[:], ACT.Gelu_apprx_tanh)
+            planes = sbuf([P, PACK * CHUNK], BF16, "planes%d" % c, "h_first" if c == 1 else None)
             for t in range(PACK):
-                nc.scalar.activation(planes[:, t * HALF : (t + 1) * HALF], g[:, t, :], ACT.Copy, scale=sm_t[:, t : t + 1])
+                nc.scalar.activation(planes[:, t * CHUNK : (t + 1) * CHUNK], g[:, t, :], ACT.Copy, scale=sm_t[:, t : t + 1])
+            woven = sbuf([P, CHUNK * PACK], BF16, "woven%d" % c)
             nc.scalar.copy(
-                woven[:, half * HALF * PACK : (half + 1) * HALF * PACK].rearrange("p (c i t) -> p c t i", t=PACK, i=4),
+                woven[:].rearrange("p (c i t) -> p c t i", t=PACK, i=4),
                 planes[:].rearrange("p (t c i) -> p c t i", t=PACK, i=4),
             )
+            quantise(c, woven)
             return planes
 
-        def down(block, j0, width, narrow, slot):
-            bank = psum.tile([P, width], F32, name="y_bank", tag="bank%d" % slot)
+        def down(block, j0, width, narrow):
+            bank = psum.tile([P, width], F32, name="y_bank", tag="y_bank", bufs=4)
             cols = slice(block * P, (block + 1) * P)
             nc.tensor.matmul_mx(
                 out=bank[:],
                 lhsT=wd8[:, 4 * block * P : 4 * (block + 1) * P].bitcast(FP8X4),
                 lhsT_scale=wd_sc[:, 1, cols],
-                rhs=h_codes[:, j0 : j0 + width].bitcast(FP8X4),
+                rhs=h_codes(j0, width),
                 rhs_scale=h_sc[:, j0 : j0 + width],
                 start=True,
                 stop=False,
@@ -172,7 +178,7 @@ def tile_list_modp_gelu_res_noneb_kernel(
                     out=bank[:, s : s + narrow],
                     lhsT=wd4[:, 2 * block * P : 2 * (block + 1) * P].bitcast(FP4X4),
                     lhsT_scale=wd_sc[:, 0, cols],
-                    rhs=h_codes[:, j0 + s : j0 + s + narrow].bitcast(FP8X4),
+                    rhs=h_codes(j0 + s, narrow),
                     rhs_scale=h_sc[:, j0 + s : j0 + s + narrow],
                     start=False,
                     stop=(s + narrow == width),
@@ -191,38 +197,30 @@ def tile_list_modp_gelu_res_noneb_kernel(
         weight = sbuf([P, J], F32, "weight", tag="picked0")
         nc.sync.dma_start(weight[:], wgo)
         picks.append(pick(1))
-        picks.append(pick(2))
-        pages.append(sbuf([P, T], F32, "page2", tag="picked2"))
-        nc.vector.memset(pages[2][:], 0.0)
+        pages.append(sbuf([P, T], F32, "page2", tag="picked1"))
+        nc.vector.memset(pages[2][:].bitcast(I32), 0)
         hidden_first(picks[0])
-        picks.append(pick(3, "g0_1"))
+        picks.append(pick(2, "g0_1"))
+        picks.append(pick(3, "woven0"))
+        pages.append(sbuf([P, T], F32, "page3", tag="g0_0"))
+        for s in range(0, T, T // 2):
+            nc.vector.memset(pages[3][:, s : s + T // 2].bitcast(I32), 0)
 
-        last = BLOCKS - 1
-        wovens = [None] + [sbuf([P, CHUNK * PACK], BF16, "woven%d" % c) for c in range(1, CHUNKS)]
-        hidden(1, 0, picks[1], 2, wovens[1])
         for c in range(CHUNKS):
-            slots = [last * ((c + 1) % 2) + block for block in range(last)]
-            banks = [down(block, c * CHUNK, CHUNK, HALF, slots[block]) for block in range(last)]
-            for block in range(last - 1):
-                y = sbuf([P, CHUNK], F32, "y%d_%d" % (c, block))
-                add_bias(y[:], banks[block], block)
-                scatter(pages[block], y[:], c * CHUNK, CHUNK)
+            blocks = BLOCKS if c < CHUNKS // 2 else BLOCKS - 1
+            banks = [down(block, c * CHUNK, CHUNK, HALF) for block in range(blocks)]
+            for block in range(blocks):
+                if block == blocks - 1 and c + 1 < CHUNKS:
+                    y = hidden(c + 1, picks[c + 1])[:].bitcast(F32)[:, 0:CHUNK]
+                else:
+                    y = sbuf([P, CHUNK], F32, "y%d_%d" % (c, block))[:]
+                add_bias(y, banks[block], block)
+                scatter(pages[block], y, c * CHUNK, CHUNK)
                 if c == CHUNKS - 1:
                     nc.sync.dma_start(out[block * P : (block + 1) * P, :], pages[block][:])
-            if c + 1 < CHUNKS:
-                y = hidden(c + 1, 1, picks[c + 1], slots[0], wovens[c + 1])[:].bitcast(F32)
-                quantise(c + 1, wovens[c + 1])
-            else:
-                y = sbuf([P, CHUNK], F32, "y_end")[:]
-            add_bias(y, banks[last - 1], last - 1)
-            scatter(pages[last - 1], y, c * CHUNK, CHUNK)
-            if c + 2 < CHUNKS:
-                hidden(c + 2, 0, picks[c + 2], slots[1], wovens[c + 2])
-        nc.sync.dma_start(out[(last - 1) * P : last * P, :], pages[last - 1][:])
 
-        page = pages[0]
-        y = sbuf([P, J], F32, "y_last")
-        for j0 in range(0, J, 512):
-            add_bias(y[:, j0 : j0 + 512], down(last, j0, 512, 512, 2 * last + j0 // 512), last)
-        scatter(page, y[:], 0, J)
-        nc.sync.dma_start(out[last * P : N, :], page[:])
+        last = BLOCKS - 1
+        y = sbuf([P, J // 2], F32, "y_last")
+        add_bias(y[:], down(last, J // 2, J // 2, J // 2), last)
+        scatter(pages[last], y[:], J // 2, J // 2)
+        nc.sync.dma_start(out[last * P : N, :], pages[last][:])

@@ -33,6 +33,7 @@ def tile_list_modp_gelu_res_noneb_kernel(
     with ExitStack() as ctx:
         lists = ctx.enter_context(tc.tile_pool(name="lists", bufs=1))
         pool = ctx.enter_context(tc.tile_pool(name="pool", bufs=1))
+        placed = ctx.enter_context(tc.tile_pool(name="placed", bufs=1))
         psum = ctx.enter_context(tc.psum_pool(name="psum", bufs=1))
 
         def sbuf(shape, dtype, name, tag=None):
@@ -41,7 +42,7 @@ def tile_list_modp_gelu_res_noneb_kernel(
         offsets = lists.tile([P, J // 16], U16, name="offsets")
         nc.sync.dma_start(offsets[:], offs)
 
-        wu_sc_raw = sbuf([P, PASSES, R], U8, "wu_sc_raw")
+        wu_sc_raw = placed.tile([P, PASSES, R], U8, name="wu_sc_raw", offset=0, align_bytes=64)
         nc.gpsimd.memset(wu_sc_raw[:].bitcast(I32), 0)
         tab_sc = sbuf([P, T], U8, "tab_sc")
         nc.gpsimd.memset(tab_sc[0:ROWS0, :].bitcast(I32), 0)
@@ -86,7 +87,7 @@ def tile_list_modp_gelu_res_noneb_kernel(
             wu_sc_raw[:].rearrange("p a (c i t) -> p a c t i", t=PACK, i=16),
         )
 
-        vectors = sbuf([P, 16], F32, "vectors", tag="wu_sc_raw")
+        vectors = placed.tile([P, 16], F32, name="vectors", offset=0, align_bytes=64)
         sm_t = vectors[:, 0:PACK]
         b_t = vectors[:, 8 : 8 + BLOCKS]
         nc.sync.dma_start(sm_t, sm.rearrange("(p t) -> p t", t=PACK))
@@ -105,10 +106,12 @@ def tile_list_modp_gelu_res_noneb_kernel(
         def h_codes(j0, width):
             return (h_first[:, j0 : j0 + width] if j0 < CHUNK else h_rest[:, j0 - CHUNK : j0 - CHUNK + width]).bitcast(FP8X4)
 
-        def pick(c, tag=None):
-            picked = sbuf([P, CHUNK], U32, "picked%d" % c, tag)
+        def gather(c, picked):
             nc.vector.tensor_copy(picked[:], tab[:].indirect(offsets[:, c * CHUNK // 16 : (c + 1) * CHUNK // 16]))
-            v = sbuf([P, PASSES, 2 * CHUNK], U8, "v%d" % c)
+            return picked
+
+        def part(c, picked, tag=None):
+            v = sbuf([P, PASSES, 2 * CHUNK], U8, "v%d" % c, tag)
             nc.vector.tensor_copy(v[:].bitcast(U16), picked[:].bitcast(U16).rearrange("p (j a) -> p a j", a=PASSES))
             return v
 
@@ -193,18 +196,18 @@ def tile_list_modp_gelu_res_noneb_kernel(
                 page[:].indirect(offsets[:, j0 // 16 : (j0 + width) // 16]), y, weight[:, j0 : j0 + width], MULT
             )
 
-        picks = [pick(0)]
+        picks = [part(0, gather(0, sbuf([P, CHUNK], U32, "picked0")))]
         weight = sbuf([P, J], F32, "weight", tag="picked0")
         nc.sync.dma_start(weight[:], wgo)
-        picks.append(pick(1))
+        picks.append(part(1, gather(1, sbuf([P, CHUNK], U32, "picked1"))))
         pages.append(sbuf([P, T], F32, "page2", tag="picked1"))
         nc.vector.memset(pages[2][:].bitcast(I32), 0)
+        picked2 = gather(2, placed.tile([P, CHUNK], U32, name="picked2", offset=64, align_bytes=64))
+        pages.append(sbuf([P, T], F32, "page3", tag="picked_sc"))
+        nc.vector.memset(pages[3][:].bitcast(I32), 0)
         hidden_first(picks[0])
-        picks.append(pick(2, "g0_1"))
-        picks.append(pick(3, "woven0"))
-        pages.append(sbuf([P, T], F32, "page3", tag="g0_0"))
-        for s in range(0, T, T // 2):
-            nc.vector.memset(pages[3][:, s : s + T // 2].bitcast(I32), 0)
+        picks.append(part(2, picked2, "g0_1"))
+        picks.append(part(3, gather(3, sbuf([P, CHUNK], U32, "picked3", "woven0"))))
 
         for c in range(CHUNKS):
             blocks = BLOCKS if c < CHUNKS // 2 else BLOCKS - 1

@@ -42,7 +42,7 @@ def tile_list_modp_gelu_res_noneb_kernel(
         offsets = lists.tile([P, J // 16], U16, name="offsets")
         nc.sync.dma_start(offsets[:], offs)
 
-        wu_sc_raw = placed.tile([P, PASSES, R], U8, name="wu_sc_raw", offset=0, align_bytes=64)
+        wu_sc_raw = sbuf([P, PASSES, R], U8, "wu_sc_raw")
         nc.gpsimd.memset(wu_sc_raw[:].bitcast(I32), 0)
         tab_sc = sbuf([P, T], U8, "tab_sc")
         nc.gpsimd.memset(tab_sc[0:ROWS0, :].bitcast(I32), 0)
@@ -59,12 +59,10 @@ def tile_list_modp_gelu_res_noneb_kernel(
 
         v_sc = sbuf([P, PASSES, J], U8, "v_sc")
         nc.vector.memset(v_sc[:].bitcast(I32), 0)
-        pages = [sbuf([P, T], F32, "page0"), sbuf([P, T], F32, "page1")]
+        pages = [sbuf([P, T], F32, "page0")]
         nc.vector.memset(pages[0][:].bitcast(I32), 0)
-        nc.vector.memset(pages[1][:, 0 : T // 2].bitcast(I32), 0)
         picked_sc = sbuf([P, J], U8, "picked_sc")
         nc.vector.tensor_copy(picked_sc[:], tab_sc[:].indirect(offsets[:]))
-        nc.vector.memset(pages[1][:, T // 2 : T].bitcast(I32), 0)
         for a in range(PASSES):
             for q in range(4):
                 row = ROWS0 + 16 * a + 4 * q
@@ -87,7 +85,7 @@ def tile_list_modp_gelu_res_noneb_kernel(
             wu_sc_raw[:].rearrange("p a (c i t) -> p a c t i", t=PACK, i=16),
         )
 
-        vectors = placed.tile([P, 16], F32, name="vectors", offset=0, align_bytes=64)
+        vectors = sbuf([P, 16], F32, "vectors", tag="wu_sc_raw")
         sm_t = vectors[:, 0:PACK]
         b_t = vectors[:, 8 : 8 + BLOCKS]
         nc.sync.dma_start(sm_t, sm.rearrange("(p t) -> p t", t=PACK))
@@ -199,15 +197,17 @@ def tile_list_modp_gelu_res_noneb_kernel(
         picks = [part(0, gather(0, sbuf([P, CHUNK], U32, "picked0")))]
         weight = sbuf([P, J], F32, "weight", tag="picked0")
         nc.sync.dma_start(weight[:], wgo)
-        picks.append(part(1, gather(1, sbuf([P, CHUNK], U32, "picked1"))))
-        pages.append(sbuf([P, T], F32, "page2", tag="picked1"))
-        nc.vector.memset(pages[2][:].bitcast(I32), 0)
-        picked2 = gather(2, placed.tile([P, CHUNK], U32, name="picked2", offset=64, align_bytes=64))
-        pages.append(sbuf([P, T], F32, "page3", tag="picked_sc"))
-        nc.vector.memset(pages[3][:].bitcast(I32), 0)
+        picks.append(part(1, gather(1, placed.tile([P, CHUNK], U32, name="picked1", offset=4 * T - 4 * CHUNK, align_bytes=64))))
+        picked2 = gather(2, placed.tile([P, CHUNK], U32, name="picked2", offset=4 * T - 6 * CHUNK, align_bytes=64))
+        picked3 = gather(3, placed.tile([P, CHUNK], U32, name="picked3", offset=4 * T - 2 * CHUNK, align_bytes=64))
+        pages.append(sbuf([P, T], F32, "page1", tag="picked_sc"))
+        nc.vector.memset(pages[1][:].bitcast(I32), 0)
         hidden_first(picks[0])
         picks.append(part(2, picked2, "g0_1"))
-        picks.append(part(3, gather(3, sbuf([P, CHUNK], U32, "picked3", "woven0"))))
+        picks.append(part(3, picked3, "woven0"))
+        for i in range(2):
+            pages.append(placed.tile([P, T], F32, name="page%d" % (2 + i), offset=4 * T * i, align_bytes=64))
+            nc.gpsimd.memset(pages[2 + i][:].bitcast(I32), 0)
 
         for c in range(CHUNKS):
             blocks = BLOCKS if c < CHUNKS // 2 else BLOCKS - 1

@@ -42,60 +42,65 @@ def tile_list_modp_gelu_res_noneb_kernel(
         offsets = lists.tile([P, J // 16], U16, name="offsets")
         nc.sync.dma_start(offsets[:], offs)
 
-        wu_sc_raw = sbuf([P, PASSES, R], U8, "wu_sc_raw")
-        nc.gpsimd.memset(wu_sc_raw[:].bitcast(I32), 0)
         tab_sc = sbuf([P, T], U8, "tab_sc")
         nc.gpsimd.memset(tab_sc[0:ROWS0, :].bitcast(I32), 0)
-        nc.sync.dma_start(tab_sc[ROWS0:P, :].bitcast(I32), tab_scales.rearrange("a q t -> (a q) t").bitcast(I32))
-        for q in range(4):
-            nc.scalar.dma_start(
-                wu_sc_raw[32 * q : 32 * q + 4, :, :].bitcast(I32),
-                wu_scales[:, 4 * q : 4 * q + 4, :].rearrange("a r n -> r a n").bitcast(I32),
-            )
+        nc.sync.dma_start(tab_sc[ROWS0:P, :].bitcast(I32), tab_scales.rearrange("a q t -> q a t").bitcast(I32))
+        wu_sc_raw = sbuf([P, R], U8, "wu_sc_raw")
+        nc.vector.memset(wu_sc_raw[0:ROWS0, :].bitcast(I32), 0)
+        nc.scalar.dma_start(wu_sc_raw[ROWS0:P, :].bitcast(I32), wu_scales.rearrange("a q r -> q a r").bitcast(I32))
+        stage1 = sbuf([P, J - CHUNK + N], U8, "stage1")
+        nc.scalar.dma_start(stage1[ROWS0:P:2, J - CHUNK :].bitcast(I32), wd4_scales[0].bitcast(I32))
+        nc.scalar.dma_start(stage1[ROWS0 + 1 : P : 2, J - CHUNK :].bitcast(I32), wd8_scales[0].bitcast(I32))
+        sm_t = sbuf([P, PACK], F32, "sm_t")
+        nc.scalar.dma_start(sm_t[:], sm.rearrange("(p t) -> p t", t=PACK))
+        sm_t = sm_t[:]
         wu_raw = sbuf([P, PASSES, R], U32, "wu_raw")
         nc.sync.dma_start(wu_raw[:].bitcast(I32), wu_words.rearrange("a p r i -> p a (r i)").bitcast(I32))
         tab = sbuf([P, T], U32, "tab")
         nc.sync.dma_start(tab[:].bitcast(I32), tab_words[0].rearrange("p t i -> p (t i)").bitcast(I32))
 
-        v_sc = sbuf([P, PASSES, J], U8, "v_sc")
-        nc.vector.memset(v_sc[:].bitcast(I32), 0)
+        planes0 = sbuf([P, 2, CHUNK + R], U8, "sc_planes0")
+        nc.vector.memset(planes0[:].bitcast(I32), 0)
+        planes1 = sbuf([P, 2, J - CHUNK + N], U8, "sc_planes1")
+        nc.vector.memset(planes1[:].bitcast(I32), 0)
         pages = [sbuf([P, T], F32, "page0")]
         nc.vector.memset(pages[0][:].bitcast(I32), 0)
-        picked_sc = sbuf([P, J], U8, "picked_sc")
-        nc.vector.tensor_copy(picked_sc[:], tab_sc[:].indirect(offsets[:]))
-        for a in range(PASSES):
-            for q in range(4):
-                row = ROWS0 + 16 * a + 4 * q
-                nc.sync.dma_start(v_sc[32 * q : 32 * q + 4, a, :].bitcast(I32), picked_sc[row : row + 4, :].bitcast(I32))
 
-        wd_sc = sbuf([P, 2, N], U8, "wd_sc", tag="tab_sc")
-        nc.gpsimd.memset(wd_sc[:].bitcast(I32), 0)
-        for q in range(4):
-            nc.sync.dma_start(wd_sc[32 * q : 32 * q + 4, 1, :].bitcast(I32), wd8_scales[0, 4 * q : 4 * q + 4, :].bitcast(I32))
-            nc.sync.dma_start(wd_sc[32 * q : 32 * q + 4, 0, :].bitcast(I32), wd4_scales[0, 4 * q : 4 * q + 4, :].bitcast(I32))
+        def spread(queue, planes, stage):
+            for q in range(4):
+                queue.dma_start(
+                    planes[32 * q : 32 * q + 4, :, :].bitcast(I32), stage[ROWS0 + 8 * q : ROWS0 + 8 * q + 8, :].bitcast(I32)
+                )
+
+        stage0 = sbuf([P, CHUNK + R], U8, "stage0")
+        picked_sc0 = sbuf([P, CHUNK], U8, "picked_sc0")
+        nc.vector.tensor_copy(picked_sc0[:], tab_sc[:].indirect(offsets[:, 0 : CHUNK // 16]))
+        nc.vector.tensor_copy(
+            stage0[:, CHUNK:].rearrange("p (t c i) -> p c t i", t=PACK, i=16),
+            wu_sc_raw[:].rearrange("p (c i t) -> p c t i", t=PACK, i=16),
+        )
+        nc.vector.tensor_copy(stage0[:, 0:CHUNK].bitcast(I32), picked_sc0[:].bitcast(I32))
+        spread(nc.scalar, planes0, stage0)
 
         wu = sbuf([P, PASSES, R], U32, "wu")
         nc.vector.tensor_copy(
             wu[:].rearrange("p a (t c i) -> p a c t i", t=PACK, i=4),
             wu_raw[:].rearrange("p a (c i t) -> p a c t i", t=PACK, i=4),
         )
-        wu_sc = sbuf([P, PASSES, R], U8, "wu_sc")
-        nc.vector.tensor_copy(
-            wu_sc[:].rearrange("p a (t c i) -> p a c t i", t=PACK, i=16),
-            wu_sc_raw[:].rearrange("p a (c i t) -> p a c t i", t=PACK, i=16),
-        )
+        wu_sc = planes0[:, :, CHUNK:]
 
-        vectors = sbuf([P, 16], F32, "vectors", tag="wu_sc_raw")
-        sm_t = vectors[:, 0:PACK]
-        b_t = vectors[:, 8 : 8 + BLOCKS]
-        nc.sync.dma_start(sm_t, sm.rearrange("(p t) -> p t", t=PACK))
-        wd = sbuf([P, 6 * N], U8, "wd", tag="wu_raw")
+        picked_sc1 = sbuf([P, J - CHUNK], U8, "picked_sc1")
+        nc.vector.tensor_copy(picked_sc1[:], tab_sc[:].indirect(offsets[:, CHUNK // 16 : J // 16]))
+        wd_sc = planes1[:, :, J - CHUNK :]
+
+        def v_sc(a, j0, width):
+            return planes0[:, a, j0 : j0 + width] if j0 < CHUNK else planes1[:, a, j0 - CHUNK : j0 - CHUNK + width]
+
+        wd = sbuf([P, 6 * N], U8, "wd", tag="tab_sc")
         wd8 = wd[:, 0 : 4 * N]
         wd4 = wd[:, 4 * N : 6 * N]
         nc.sync.dma_start(wd8.bitcast(I32), wd8_words[0].rearrange("p n i -> p (n i)").bitcast(I32))
         nc.sync.dma_start(wd4.bitcast(I32), wd4_words[0].bitcast(I32))
-        with nc.allow_non_contiguous_dma(reason="one bias value a partition and block"):
-            nc.sync.dma_start(b_t, b.rearrange("(c p) -> p c", p=P))
 
         h_first = sbuf([P, CHUNK], U32, "h_first")
         h_rest = sbuf([P, J - CHUNK], U32, "h_rest")
@@ -123,7 +128,7 @@ def tile_list_modp_gelu_res_noneb_kernel(
                         lhsT=wu[:, a, t * P : (t + 1) * P].bitcast(FP8X4),
                         lhsT_scale=wu_sc[:, a, t * P : (t + 1) * P],
                         rhs=v[:, a, 2 * half * HALF : 2 * (half + 1) * HALF].bitcast(FP4X4),
-                        rhs_scale=v_sc[:, a, j0 : j0 + HALF],
+                        rhs_scale=v_sc(a, j0, HALF),
                         start=(a == 0),
                         stop=(a == PASSES - 1),
                     )
@@ -195,12 +200,18 @@ def tile_list_modp_gelu_res_noneb_kernel(
             )
 
         picks = [part(0, gather(0, sbuf([P, CHUNK], U32, "picked0")))]
-        weight = sbuf([P, J], F32, "weight", tag="picked0")
-        nc.sync.dma_start(weight[:], wgo)
+        nc.vector.tensor_copy(stage1[:, 0 : J - CHUNK].bitcast(I32), picked_sc1[:].bitcast(I32))
+        spread(nc.sync, planes1, stage1)
+        late = sbuf([P, J + 16], F32, "late", tag="picked_sc1")
+        weight = late[:, 0:J]
+        b_t = late[:, J : J + BLOCKS]
+        with nc.allow_non_contiguous_dma(reason="one bias value a partition and block"):
+            nc.sync.dma_start(b_t, b.rearrange("(c p) -> p c", p=P))
+        nc.sync.dma_start(weight, wgo)
         picks.append(part(1, gather(1, placed.tile([P, CHUNK], U32, name="picked1", offset=4 * T - 4 * CHUNK, align_bytes=64))))
         picked2 = gather(2, placed.tile([P, CHUNK], U32, name="picked2", offset=4 * T - 6 * CHUNK, align_bytes=64))
         picked3 = gather(3, placed.tile([P, CHUNK], U32, name="picked3", offset=4 * T - 2 * CHUNK, align_bytes=64))
-        pages.append(sbuf([P, T], F32, "page1", tag="picked_sc"))
+        pages.append(sbuf([P, T], F32, "page1", tag="picked0"))
         nc.vector.memset(pages[1][:].bitcast(I32), 0)
         hidden_first(picks[0])
         picks.append(part(2, picked2, "g0_1"))

@@ -48,9 +48,9 @@ def tile_list_modp_gelu_res_noneb_kernel(
         wu_sc_raw = sbuf([P, R], U8, "wu_sc_raw")
         nc.vector.memset(wu_sc_raw[0:ROWS0, :].bitcast(I32), 0)
         nc.scalar.dma_start(wu_sc_raw[ROWS0:P, :].bitcast(I32), wu_scales.rearrange("a q r -> q a r").bitcast(I32))
-        stage1 = sbuf([P, J - CHUNK + N], U8, "stage1")
-        nc.scalar.dma_start(stage1[ROWS0:P:2, J - CHUNK :].bitcast(I32), wd4_scales[0].bitcast(I32))
-        nc.scalar.dma_start(stage1[ROWS0 + 1 : P : 2, J - CHUNK :].bitcast(I32), wd8_scales[0].bitcast(I32))
+        stage0 = sbuf([P, CHUNK + R + N], U8, "stage0")
+        nc.scalar.dma_start(stage0[ROWS0:P:2, CHUNK + R :].bitcast(I32), wd4_scales[0].bitcast(I32))
+        nc.scalar.dma_start(stage0[ROWS0 + 1 : P : 2, CHUNK + R :].bitcast(I32), wd8_scales[0].bitcast(I32))
         sm_t = sbuf([P, PACK], F32, "sm_t")
         nc.scalar.dma_start(sm_t[:], sm.rearrange("(p t) -> p t", t=PACK))
         sm_t = sm_t[:]
@@ -59,9 +59,9 @@ def tile_list_modp_gelu_res_noneb_kernel(
         tab = sbuf([P, T], U32, "tab")
         nc.sync.dma_start(tab[:].bitcast(I32), tab_words[0].rearrange("p t i -> p (t i)").bitcast(I32))
 
-        planes0 = sbuf([P, 2, CHUNK + R], U8, "sc_planes0")
+        planes0 = sbuf([P, 2, CHUNK + R + N], U8, "sc_planes0")
         nc.vector.memset(planes0[:].bitcast(I32), 0)
-        planes1 = sbuf([P, 2, J - CHUNK + N], U8, "sc_planes1")
+        planes1 = sbuf([P, 2, J - CHUNK], U8, "sc_planes1")
         nc.vector.memset(planes1[:].bitcast(I32), 0)
         pages = [sbuf([P, T], F32, "page0")]
         nc.vector.memset(pages[0][:].bitcast(I32), 0)
@@ -72,35 +72,26 @@ def tile_list_modp_gelu_res_noneb_kernel(
                     planes[32 * q : 32 * q + 4, :, :].bitcast(I32), stage[ROWS0 + 8 * q : ROWS0 + 8 * q + 8, :].bitcast(I32)
                 )
 
-        stage0 = sbuf([P, CHUNK + R], U8, "stage0")
         picked_sc0 = sbuf([P, CHUNK], U8, "picked_sc0")
         nc.vector.tensor_copy(picked_sc0[:], tab_sc[:].indirect(offsets[:, 0 : CHUNK // 16]))
         nc.vector.tensor_copy(
-            stage0[:, CHUNK:].rearrange("p (t c i) -> p c t i", t=PACK, i=16),
+            stage0[:, CHUNK : CHUNK + R].rearrange("p (t c i) -> p c t i", t=PACK, i=16),
             wu_sc_raw[:].rearrange("p (c i t) -> p c t i", t=PACK, i=16),
         )
         nc.vector.tensor_copy(stage0[:, 0:CHUNK].bitcast(I32), picked_sc0[:].bitcast(I32))
-        spread(nc.scalar, planes0, stage0)
+        spread(nc.sync, planes0, stage0)
 
         wu = sbuf([P, PASSES, R], U32, "wu")
         nc.vector.tensor_copy(
             wu[:].rearrange("p a (t c i) -> p a c t i", t=PACK, i=4),
             wu_raw[:].rearrange("p a (c i t) -> p a c t i", t=PACK, i=4),
         )
-        wu_sc = planes0[:, :, CHUNK:]
+        wu_sc = planes0[:, :, CHUNK : CHUNK + R]
+        wd_sc = planes0[:, :, CHUNK + R :]
 
-        picked_sc1 = sbuf([P, J - CHUNK], U8, "picked_sc1")
-        nc.vector.tensor_copy(picked_sc1[:], tab_sc[:].indirect(offsets[:, CHUNK // 16 : J // 16]))
-        wd_sc = planes1[:, :, J - CHUNK :]
 
         def v_sc(a, j0, width):
             return planes0[:, a, j0 : j0 + width] if j0 < CHUNK else planes1[:, a, j0 - CHUNK : j0 - CHUNK + width]
-
-        wd = sbuf([P, 6 * N], U8, "wd", tag="tab_sc")
-        wd8 = wd[:, 0 : 4 * N]
-        wd4 = wd[:, 4 * N : 6 * N]
-        nc.sync.dma_start(wd8.bitcast(I32), wd8_words[0].rearrange("p n i -> p (n i)").bitcast(I32))
-        nc.sync.dma_start(wd4.bitcast(I32), wd4_words[0].bitcast(I32))
 
         h_first = sbuf([P, CHUNK], U32, "h_first")
         h_rest = sbuf([P, J - CHUNK], U32, "h_rest")
@@ -110,13 +101,10 @@ def tile_list_modp_gelu_res_noneb_kernel(
             return (h_first[:, j0 : j0 + width] if j0 < CHUNK else h_rest[:, j0 - CHUNK : j0 - CHUNK + width]).bitcast(FP8X4)
 
         def gather(c, picked):
-            nc.vector.tensor_copy(picked[:], tab[:].indirect(offsets[:, c * CHUNK // 16 : (c + 1) * CHUNK // 16]))
-            return picked
+            nc.vector.tensor_copy(picked, tab[:].indirect(offsets[:, c * CHUNK // 16 : (c + 1) * CHUNK // 16]))
 
-        def part(c, picked, tag=None):
-            v = sbuf([P, PASSES, 2 * CHUNK], U8, "v%d" % c, tag)
-            nc.vector.tensor_copy(v[:].bitcast(U16), picked[:].bitcast(U16).rearrange("p (j a) -> p a j", a=PASSES))
-            return v
+        def part(v, picked):
+            nc.vector.tensor_copy(v[:].bitcast(U16), picked.bitcast(U16).rearrange("p (j a) -> p a j", a=PASSES))
 
         def up(c, half, v):
             bank = psum.tile([P, PACK, HALF], F32, name="a_bank", tag="a_bank", bufs=4)
@@ -138,19 +126,17 @@ def tile_list_modp_gelu_res_noneb_kernel(
             cols = slice(c * CHUNK, (c + 1) * CHUNK)
             nc.vector.quantize_mx(out=h_codes(c * CHUNK, CHUNK), scales=h_sc[:, cols], in_=woven[:])
 
-        def hidden_first(v):
-            woven = sbuf([P, CHUNK * PACK], BF16, "woven0")
-            for half in range(CHUNK // HALF):
-                bank = up(0, half, v)
-                g = sbuf([P, HALF, PACK], F32, "g0_%d" % half)
-                nc.scalar.activation(g[:], bank[:].rearrange("p t j -> p j t"), ACT.Gelu_apprx_tanh)
-                nc.vector.tensor_tensor(
-                    woven[:, half * HALF * PACK : (half + 1) * HALF * PACK].rearrange("p (j t) -> p j t", t=PACK),
-                    g[:],
-                    sm_t.unsqueeze(1).to_broadcast([P, HALF, PACK]),
-                    MULT,
-                )
-            quantise(0, woven)
+        def first_half(half, v, woven):
+            g = sbuf([P, HALF, PACK], F32, "g0_%d" % half)
+            nc.scalar.activation(g[:], up(0, half, v)[:].rearrange("p t j -> p j t"), ACT.Gelu_apprx_tanh)
+            nc.vector.tensor_tensor(
+                woven[:].rearrange("p (j t) -> p j t", t=PACK),
+                g[:],
+                sm_t.unsqueeze(1).to_broadcast([P, HALF, PACK]),
+                MULT,
+            )
+            cols = slice(half * HALF, (half + 1) * HALF)
+            nc.vector.quantize_mx(out=h_codes(half * HALF, HALF), scales=h_sc[:, cols], in_=woven[:])
 
         def hidden(c, v):
             g = sbuf([P, PACK, CHUNK], F32, "g%d" % c, "g")
@@ -199,31 +185,54 @@ def tile_list_modp_gelu_res_noneb_kernel(
                 page[:].indirect(offsets[:, j0 // 16 : (j0 + width) // 16]), y, weight[:, j0 : j0 + width], MULT
             )
 
-        picks = [part(0, gather(0, sbuf([P, CHUNK], U32, "picked0")))]
-        nc.vector.tensor_copy(stage1[:, 0 : J - CHUNK].bitcast(I32), picked_sc1[:].bitcast(I32))
-        spread(nc.sync, planes1, stage1)
-        late = sbuf([P, J + 16], F32, "late", tag="picked_sc1")
+        picked_sc1 = sbuf([P, J - CHUNK], U8, "picked_sc1")
+        nc.vector.tensor_copy(picked_sc1[:], tab_sc[:].indirect(offsets[:, CHUNK // 16 : J // 16]))
+        wd = sbuf([P, 6 * N], U8, "wd", tag="stage0")
+        wd8 = wd[:, 0 : 4 * N]
+        wd4 = wd[:, 4 * N : 6 * N]
+        nc.sync.dma_start(wd8.bitcast(I32), wd8_words[0].rearrange("p n i -> p (n i)").bitcast(I32))
+        nc.sync.dma_start(wd4.bitcast(I32), wd4_words[0].bitcast(I32))
+        spread(nc.sync, planes1, picked_sc1)
+        late = sbuf([P, J + 16], F32, "late", tag="tab_sc")
         weight = late[:, 0:J]
         b_t = late[:, J : J + BLOCKS]
         with nc.allow_non_contiguous_dma(reason="one bias value a partition and block"):
             nc.sync.dma_start(b_t, b.rearrange("(c p) -> p c", p=P))
         nc.sync.dma_start(weight, wgo)
-        picks.append(part(1, gather(1, placed.tile([P, CHUNK], U32, name="picked1", offset=4 * T - 4 * CHUNK, align_bytes=64))))
-        picked2 = gather(2, placed.tile([P, CHUNK], U32, name="picked2", offset=4 * T - 6 * CHUNK, align_bytes=64))
-        picked3 = gather(3, placed.tile([P, CHUNK], U32, name="picked3", offset=4 * T - 2 * CHUNK, align_bytes=64))
-        pages.append(sbuf([P, T], F32, "page1", tag="picked0"))
+
+        page_bytes = 4 * T
+        picks = [sbuf([P, PASSES, 2 * CHUNK], U8, "v%d" % c) for c in range(CHUNKS - 1)]
+        seam = page_bytes - 2 * CHUNK
+        picked0 = placed.tile([P, CHUNK], U32, name="picked0", offset=seam, align_bytes=64)
+        gather(0, picked0[:])
+        part(picks[0], picked0[:])
+        picked_rest = placed.tile([P, J - CHUNK], U32, name="picked_rest", offset=seam, align_bytes=64)
+        picked = [None] + [picked_rest[:, c * CHUNK : (c + 1) * CHUNK] for c in range(CHUNKS - 1)]
+        gather(1, picked[1])
+        gather(2, picked[2])
+        part(picks[1], picked[1])
+        gather(3, picked[3])
+        part(picks[2], picked[2])
+        first_half(0, picks[0], sbuf([P, HALF * PACK], BF16, "woven0_0"))
+        first_half(1, picks[0], placed.tile([P, HALF * PACK], BF16, name="woven0_1", offset=3 * page_bytes - HALF * PACK, align_bytes=64))
+        pages.append(placed.tile([P, T], F32, name="page1", offset=2 * page_bytes, align_bytes=64))
         nc.vector.memset(pages[1][:].bitcast(I32), 0)
-        hidden_first(picks[0])
-        picks.append(part(2, picked2, "g0_1"))
-        picks.append(part(3, picked3, "woven0"))
+        picks.append(placed.tile([P, PASSES, 2 * CHUNK], U8, name="v3", offset=3 * page_bytes, align_bytes=64))
+        part(picks[3], picked[3])
         for i in range(2):
-            pages.append(placed.tile([P, T], F32, name="page%d" % (2 + i), offset=4 * T * i, align_bytes=64))
+            pages.append(placed.tile([P, T], F32, name="page%d" % (2 + i), offset=page_bytes * i, align_bytes=64))
             nc.gpsimd.memset(pages[2 + i][:].bitcast(I32), 0)
 
         for c in range(CHUNKS):
             blocks = BLOCKS if c < CHUNKS // 2 else BLOCKS - 1
-            banks = [down(block, c * CHUNK, CHUNK, HALF) for block in range(blocks)]
-            for block in range(blocks):
+            if c == 0:
+                y = sbuf([P, CHUNK], F32, "y_first")
+                for half in range(CHUNK // HALF):
+                    add_bias(y[:, half * HALF : (half + 1) * HALF], down(0, half * HALF, HALF, HALF), 0)
+                scatter(pages[0], y[:], 0, CHUNK)
+            first = 1 if c == 0 else 0
+            banks = {block: down(block, c * CHUNK, CHUNK, HALF) for block in range(first, blocks)}
+            for block in range(first, blocks):
                 if block == blocks - 1 and c + 1 < CHUNKS:
                     y = hidden(c + 1, picks[c + 1])[:].bitcast(F32)[:, 0:CHUNK]
                 else:

@@ -54,7 +54,8 @@ def tile_list_modp_gelu_res_noneb_kernel(
         sm_t = sbuf([P, PACK], F32, "sm_t")
         nc.scalar.dma_start(sm_t[:], sm.rearrange("(p t) -> p t", t=PACK))
         sm_t = sm_t[:]
-        wu_raw = sbuf([P, PASSES, R], U32, "wu_raw")
+        page_bytes = 4 * T
+        wu_raw = placed.tile([P, PASSES, R], U32, name="wu_raw", offset=3 * page_bytes - 4 * R, align_bytes=64)
         nc.sync.dma_start(wu_raw[:].bitcast(I32), wu_words.rearrange("a p r i -> p a (r i)").bitcast(I32))
         tab = sbuf([P, T], U32, "tab")
         nc.sync.dma_start(tab[:].bitcast(I32), tab_words[0].rearrange("p t i -> p (t i)").bitcast(I32))
@@ -81,11 +82,22 @@ def tile_list_modp_gelu_res_noneb_kernel(
         nc.vector.tensor_copy(stage0[:, 0:CHUNK].bitcast(I32), picked_sc0[:].bitcast(I32))
         spread(nc.sync, planes0, stage0)
 
-        wu = sbuf([P, PASSES, R], U32, "wu")
+        wu = sbuf([P, PASSES, R], U32, "wu", "picked_sc0")
         nc.vector.tensor_copy(
             wu[:].rearrange("p a (t c i) -> p a c t i", t=PACK, i=4),
             wu_raw[:].rearrange("p a (c i t) -> p a c t i", t=PACK, i=4),
         )
+        idle = psum.tile([P, R], F32, name="y_bank", tag="y_bank", bufs=4)
+        for i in range(3):
+            nc.tensor.matmul_mx(
+                out=idle[:],
+                lhsT=wu[:, 0, 0:P].bitcast(FP8X4),
+                lhsT_scale=stage0[:, CHUNK : CHUNK + P],
+                rhs=wu[:, 0, :].bitcast(FP8X4),
+                rhs_scale=stage0[:, CHUNK : CHUNK + R],
+                start=True,
+                stop=True,
+            )
         wu_sc = planes0[:, :, CHUNK : CHUNK + R]
         wd_sc = planes0[:, :, CHUNK + R :]
 
@@ -138,20 +150,23 @@ def tile_list_modp_gelu_res_noneb_kernel(
             cols = slice(half * HALF, (half + 1) * HALF)
             nc.vector.quantize_mx(out=h_codes(half * HALF, HALF), scales=h_sc[:, cols], in_=woven[:])
 
-        def hidden(c, v):
+        def scaled(c):
             g = sbuf([P, PACK, CHUNK], F32, "g%d" % c, "g")
             for half in range(CHUNK // HALF):
-                nc.scalar.activation(g[:, :, half * HALF : (half + 1) * HALF], up(c, half, v)[:], ACT.Gelu_apprx_tanh)
+                nc.scalar.activation(g[:, :, half * HALF : (half + 1) * HALF], up(c, half, picks[c])[:], ACT.Gelu_apprx_tanh)
             planes = sbuf([P, PACK * CHUNK], BF16, "planes%d" % c, "h_first" if c == 1 else None)
             for t in range(PACK):
                 nc.scalar.activation(planes[:, t * CHUNK : (t + 1) * CHUNK], g[:, t, :], ACT.Copy, scale=sm_t[:, t : t + 1])
+            return g[:, PACK - 1, :], planes
+
+        def weave(c, planes):
             woven = sbuf([P, CHUNK * PACK], BF16, "woven%d" % c)
             nc.scalar.copy(
                 woven[:].rearrange("p (c i t) -> p c t i", t=PACK, i=4),
                 planes[:].rearrange("p (t c i) -> p c t i", t=PACK, i=4),
             )
             quantise(c, woven)
-            return planes
+            return planes[:].bitcast(F32)[:, 0:CHUNK]
 
         def down(block, j0, width, narrow):
             bank = psum.tile([P, width], F32, name="y_bank", tag="y_bank", bufs=4)
@@ -185,7 +200,9 @@ def tile_list_modp_gelu_res_noneb_kernel(
                 page[:].indirect(offsets[:, j0 // 16 : (j0 + width) // 16]), y, weight[:, j0 : j0 + width], MULT
             )
 
-        picked_sc1 = sbuf([P, J - CHUNK], U8, "picked_sc1")
+        pages.append(placed.tile([P, T], F32, name="page1", offset=2 * page_bytes, align_bytes=64))
+        nc.gpsimd.memset(pages[1][:].bitcast(I32), 0)
+        picked_sc1 = placed.tile([P, J - CHUNK], U8, name="picked_sc1", offset=3 * page_bytes, align_bytes=64)
         nc.vector.tensor_copy(picked_sc1[:], tab_sc[:].indirect(offsets[:, CHUNK // 16 : J // 16]))
         wd = sbuf([P, 6 * N], U8, "wd", tag="stage0")
         wd8 = wd[:, 0 : 4 * N]
@@ -200,50 +217,54 @@ def tile_list_modp_gelu_res_noneb_kernel(
             nc.sync.dma_start(b_t, b.rearrange("(c p) -> p c", p=P))
         nc.sync.dma_start(weight, wgo)
 
-        page_bytes = 4 * T
-        picks = [sbuf([P, PASSES, 2 * CHUNK], U8, "v%d" % c) for c in range(CHUNKS - 1)]
-        seam = page_bytes - 2 * CHUNK
-        picked0 = placed.tile([P, CHUNK], U32, name="picked0", offset=seam, align_bytes=64)
+        picks = [sbuf([P, PASSES, 2 * CHUNK], U8, "v%d" % c) for c in range(CHUNKS)]
+        picked0 = sbuf([P, CHUNK], U32, "picked0")
         gather(0, picked0[:])
         part(picks[0], picked0[:])
-        picked_rest = placed.tile([P, J - CHUNK], U32, name="picked_rest", offset=seam, align_bytes=64)
+        picked_rest = sbuf([P, J - CHUNK], U32, "picked_rest", "picked0")
         picked = [None] + [picked_rest[:, c * CHUNK : (c + 1) * CHUNK] for c in range(CHUNKS - 1)]
         gather(1, picked[1])
         gather(2, picked[2])
         part(picks[1], picked[1])
         gather(3, picked[3])
         part(picks[2], picked[2])
-        first_half(0, picks[0], sbuf([P, HALF * PACK], BF16, "woven0_0"))
-        first_half(1, picks[0], placed.tile([P, HALF * PACK], BF16, name="woven0_1", offset=3 * page_bytes - HALF * PACK, align_bytes=64))
-        pages.append(placed.tile([P, T], F32, name="page1", offset=2 * page_bytes, align_bytes=64))
-        nc.vector.memset(pages[1][:].bitcast(I32), 0)
-        picks.append(placed.tile([P, PASSES, 2 * CHUNK], U8, name="v3", offset=3 * page_bytes, align_bytes=64))
         part(picks[3], picked[3])
+        first_half(0, picks[0], sbuf([P, HALF * PACK], BF16, "woven0_0"))
+        first_half(1, picks[0], placed.tile([P, HALF * PACK], BF16, name="woven0_1", offset=page_bytes - HALF * PACK, align_bytes=64))
         for i in range(2):
             pages.append(placed.tile([P, T], F32, name="page%d" % (2 + i), offset=page_bytes * i, align_bytes=64))
             nc.gpsimd.memset(pages[2 + i][:].bitcast(I32), 0)
 
-        for c in range(CHUNKS):
-            blocks = BLOCKS if c < CHUNKS // 2 else BLOCKS - 1
-            if c == 0:
-                y = sbuf([P, CHUNK], F32, "y_first")
-                for half in range(CHUNK // HALF):
-                    add_bias(y[:, half * HALF : (half + 1) * HALF], down(0, half * HALF, HALF, HALF), 0)
-                scatter(pages[0], y[:], 0, CHUNK)
-            first = 1 if c == 0 else 0
-            banks = {block: down(block, c * CHUNK, CHUNK, HALF) for block in range(first, blocks)}
-            for block in range(first, blocks):
-                if block == blocks - 1 and c + 1 < CHUNKS:
-                    y = hidden(c + 1, picks[c + 1])[:].bitcast(F32)[:, 0:CHUNK]
-                else:
-                    y = sbuf([P, CHUNK], F32, "y%d_%d" % (c, block))[:]
-                add_bias(y, banks[block], block)
-                scatter(pages[block], y, c * CHUNK, CHUNK)
-                if c == CHUNKS - 1:
-                    nc.sync.dma_start(out[block * P : (block + 1) * P, :], pages[block][:])
+        def place(c, block, bank, y=None, chunks=1):
+            if y is None:
+                y = sbuf([P, chunks * CHUNK], F32, "y%d_%d" % (c, block))[:]
+            add_bias(y, bank, block)
+            scatter(pages[block], y, c * CHUNK, chunks * CHUNK)
+            if c + chunks == CHUNKS:
+                nc.sync.dma_start(out[block * P : (block + 1) * P, :], pages[block][:])
 
-        last = BLOCKS - 1
-        y = sbuf([P, J // 2], F32, "y_last")
-        add_bias(y[:], down(last, J // 2, J // 2, J // 2), last)
-        scatter(pages[last], y[:], J // 2, J // 2)
-        nc.sync.dma_start(out[last * P : N, :], pages[last][:])
+        def downs(c, blocks):
+            return {block: down(block, c * CHUNK, CHUNK, HALF) for block in blocks}
+
+        y = sbuf([P, CHUNK], F32, "y_first")
+        for half in range(CHUNK // HALF):
+            add_bias(y[:, half * HALF : (half + 1) * HALF], down(0, half * HALF, HALF, HALF), 0)
+        scatter(pages[0], y[:], 0, CHUNK)
+        banks = downs(0, range(1, BLOCKS))
+        place(0, 1, banks[1])
+        place(0, 2, banks[2])
+        place(0, 3, banks[3], weave(1, scaled(1)[1]))
+
+        banks = downs(1, range(BLOCKS))
+        for block in range(BLOCKS - 1):
+            place(1, block, banks[block])
+        place(1, 3, banks[3], weave(2, scaled(2)[1]))
+
+        banks = downs(2, range(BLOCKS - 1))
+        place(2, 0, banks[0])
+        place(2, 1, banks[1])
+        place(2, 2, banks[2], weave(3, scaled(3)[1]))
+        banks = downs(3, range(BLOCKS - 1))
+        for block in range(BLOCKS - 1):
+            place(3, block, banks[block])
+        place(2, 3, down(3, 2 * CHUNK, 2 * CHUNK, 2 * CHUNK), chunks=2)

@@ -51,14 +51,14 @@ def tile_list_modp_gelu_res_noneb_kernel(
         stage0 = sbuf([P, CHUNK + R + N], U8, "stage0")
         nc.scalar.dma_start(stage0[ROWS0:P:2, CHUNK + R :].bitcast(I32), wd4_scales[0].bitcast(I32))
         nc.scalar.dma_start(stage0[ROWS0 + 1 : P : 2, CHUNK + R :].bitcast(I32), wd8_scales[0].bitcast(I32))
-        sm_t = sbuf([P, PACK], F32, "sm_t")
-        nc.scalar.dma_start(sm_t[:], sm.rearrange("(p t) -> p t", t=PACK))
-        sm_t = sm_t[:]
         page_bytes = 4 * T
-        wu_raw = placed.tile([P, PASSES, R], U32, name="wu_raw", offset=3 * page_bytes - 4 * R, align_bytes=64)
-        nc.sync.dma_start(wu_raw[:].bitcast(I32), wu_words.rearrange("a p r i -> p a (r i)").bitcast(I32))
+        wu_raw0 = placed.tile([P, R], U32, name="wu_raw0", offset=3 * page_bytes - 2 * R, align_bytes=64)
+        nc.sync.dma_start(wu_raw0[:].bitcast(I32), wu_words[0].rearrange("p r i -> p (r i)").bitcast(I32))
         tab = sbuf([P, T], U32, "tab")
         nc.sync.dma_start(tab[:].bitcast(I32), tab_words[0].rearrange("p t i -> p (t i)").bitcast(I32))
+        beyond = 3 * page_bytes + 4 * R
+        wu_raw1 = placed.tile([P, R], U32, name="wu_raw1", offset=beyond, align_bytes=64)
+        nc.sync.dma_start(wu_raw1[:].bitcast(I32), wu_words[1].rearrange("p r i -> p (r i)").bitcast(I32))
 
         planes0 = sbuf([P, 2, CHUNK + R + N], U8, "sc_planes0")
         nc.vector.memset(planes0[:].bitcast(I32), 0)
@@ -80,24 +80,19 @@ def tile_list_modp_gelu_res_noneb_kernel(
             wu_sc_raw[:].rearrange("p (c i t) -> p c t i", t=PACK, i=16),
         )
         nc.vector.tensor_copy(stage0[:, 0:CHUNK].bitcast(I32), picked_sc0[:].bitcast(I32))
+        sm_t = sbuf([P, PACK], F32, "sm_t", "wu_sc_raw")
+        nc.sync.dma_start(sm_t[:], sm.rearrange("(p t) -> p t", t=PACK))
+        sm_t = sm_t[:]
         spread(nc.sync, planes0, stage0)
 
         wu = sbuf([P, PASSES, R], U32, "wu", "picked_sc0")
-        nc.vector.tensor_copy(
-            wu[:].rearrange("p a (t c i) -> p a c t i", t=PACK, i=4),
-            wu_raw[:].rearrange("p a (c i t) -> p a c t i", t=PACK, i=4),
-        )
-        idle = psum.tile([P, R], F32, name="y_bank", tag="y_bank", bufs=4)
-        for i in range(3):
-            nc.tensor.matmul_mx(
-                out=idle[:],
-                lhsT=wu[:, 0, 0:P].bitcast(FP8X4),
-                lhsT_scale=stage0[:, CHUNK : CHUNK + P],
-                rhs=wu[:, 0, :].bitcast(FP8X4),
-                rhs_scale=stage0[:, CHUNK : CHUNK + R],
-                start=True,
-                stop=True,
+
+        def reorder(a, raw):
+            nc.vector.tensor_copy(
+                wu[:, a, :].rearrange("p (t c i) -> p c t i", t=PACK, i=4), raw[:].rearrange("p (c i t) -> p c t i", t=PACK, i=4)
             )
+
+        reorder(0, wu_raw0)
         wu_sc = planes0[:, :, CHUNK : CHUNK + R]
         wd_sc = planes0[:, :, CHUNK + R :]
 
@@ -112,8 +107,8 @@ def tile_list_modp_gelu_res_noneb_kernel(
         def h_codes(j0, width):
             return (h_first[:, j0 : j0 + width] if j0 < CHUNK else h_rest[:, j0 - CHUNK : j0 - CHUNK + width]).bitcast(FP8X4)
 
-        def gather(c, picked):
-            nc.vector.tensor_copy(picked, tab[:].indirect(offsets[:, c * CHUNK // 16 : (c + 1) * CHUNK // 16]))
+        def gather(c, picked, chunks=1):
+            nc.vector.tensor_copy(picked, tab[:].indirect(offsets[:, c * CHUNK // 16 : (c + chunks) * CHUNK // 16]))
 
         def part(v, picked):
             nc.vector.tensor_copy(v[:].bitcast(U16), picked.bitcast(U16).rearrange("p (j a) -> p a j", a=PASSES))
@@ -217,20 +212,23 @@ def tile_list_modp_gelu_res_noneb_kernel(
             nc.sync.dma_start(b_t, b.rearrange("(c p) -> p c", p=P))
         nc.sync.dma_start(weight, wgo)
 
-        picks = [sbuf([P, PASSES, 2 * CHUNK], U8, "v%d" % c) for c in range(CHUNKS)]
-        picked0 = sbuf([P, CHUNK], U32, "picked0")
+        picks = [sbuf([P, PASSES, 2 * CHUNK], U8, "v%d" % c) for c in range(2)]
+        picked0 = placed.tile([P, CHUNK], U32, name="picked0", offset=beyond + 4 * R, align_bytes=64)
         gather(0, picked0[:])
+        reorder(1, wu_raw1)
         part(picks[0], picked0[:])
-        picked_rest = sbuf([P, J - CHUNK], U32, "picked_rest", "picked0")
-        picked = [None] + [picked_rest[:, c * CHUNK : (c + 1) * CHUNK] for c in range(CHUNKS - 1)]
-        gather(1, picked[1])
-        gather(2, picked[2])
-        part(picks[1], picked[1])
-        gather(3, picked[3])
-        part(picks[2], picked[2])
-        part(picks[3], picked[3])
+        picked12 = placed.tile([P, 2 * CHUNK], U32, name="picked12", offset=beyond + 4 * R - 4 * CHUNK, align_bytes=64)
+        gather(1, picked12[:], 2)
+        part(picks[1], picked12[:, 0:CHUNK])
+        seam = page_bytes - HALF * PACK
         first_half(0, picks[0], sbuf([P, HALF * PACK], BF16, "woven0_0"))
-        first_half(1, picks[0], placed.tile([P, HALF * PACK], BF16, name="woven0_1", offset=page_bytes - HALF * PACK, align_bytes=64))
+        first_half(1, picks[0], placed.tile([P, HALF * PACK], BF16, name="woven0_1", offset=seam, align_bytes=64))
+        picked3 = placed.tile([P, CHUNK], U32, name="picked3", offset=seam, align_bytes=64)
+        gather(3, picked3[:])
+        picks.append(sbuf([P, PASSES, 2 * CHUNK], U8, "v2", "g0_1"))
+        part(picks[2], picked12[:, CHUNK:])
+        picks.append(sbuf([P, PASSES, 2 * CHUNK], U8, "v3"))
+        part(picks[3], picked3[:])
         for i in range(2):
             pages.append(placed.tile([P, T], F32, name="page%d" % (2 + i), offset=page_bytes * i, align_bytes=64))
             nc.gpsimd.memset(pages[2 + i][:].bitcast(I32), 0)

@@ -93,6 +93,17 @@ def tile_list_modp_gelu_res_noneb_kernel(
             )
 
         reorder(0, wu_raw0)
+        idle = psum.tile([P, R], F32, name="y_bank", tag="y_bank", bufs=4)
+        for i in range(3):
+            nc.tensor.matmul_mx(
+                out=idle[:],
+                lhsT=wu[:, 0, 0:P].bitcast(FP8X4),
+                lhsT_scale=stage0[:, CHUNK : CHUNK + P],
+                rhs=wu[:, 0, :].bitcast(FP8X4),
+                rhs_scale=stage0[:, CHUNK : CHUNK + R],
+                start=True,
+                stop=True,
+            )
         wu_sc = planes0[:, :, CHUNK : CHUNK + R]
         wd_sc = planes0[:, :, CHUNK + R :]
 

@@ -93,17 +93,6 @@ def tile_list_modp_gelu_res_noneb_kernel(
             )
 
         reorder(0, wu_raw0)
-        idle = psum.tile([P, R], F32, name="y_bank", tag="y_bank", bufs=4)
-        for i in range(3):
-            nc.tensor.matmul_mx(
-                out=idle[:],
-                lhsT=wu[:, 0, 0:P].bitcast(FP8X4),
-                lhsT_scale=stage0[:, CHUNK : CHUNK + P],
-                rhs=wu[:, 0, :].bitcast(FP8X4),
-                rhs_scale=stage0[:, CHUNK : CHUNK + R],
-                start=True,
-                stop=True,
-            )
         wu_sc = planes0[:, :, CHUNK : CHUNK + R]
         wd_sc = planes0[:, :, CHUNK + R :]
 
@@ -122,7 +111,7 @@ def tile_list_modp_gelu_res_noneb_kernel(
             nc.vector.tensor_copy(picked, tab[:].indirect(offsets[:, c * CHUNK // 16 : (c + chunks) * CHUNK // 16]))
 
         def part(v, picked):
-            nc.vector.tensor_copy(v[:].bitcast(U16), picked.bitcast(U16).rearrange("p (j a) -> p a j", a=PASSES))
+            nc.vector.tensor_copy(v.bitcast(U16), picked.bitcast(U16).rearrange("p (j a) -> p a j", a=PASSES))
 
         def up(c, half, v):
             bank = psum.tile([P, PACK, HALF], F32, name="a_bank", tag="a_bank", bufs=4)
@@ -209,7 +198,19 @@ def tile_list_modp_gelu_res_noneb_kernel(
         pages.append(placed.tile([P, T], F32, name="page1", offset=2 * page_bytes, align_bytes=64))
         nc.gpsimd.memset(pages[1][:].bitcast(I32), 0)
         picked_sc1 = placed.tile([P, J - CHUNK], U8, name="picked_sc1", offset=3 * page_bytes, align_bytes=64)
-        nc.vector.tensor_copy(picked_sc1[:], tab_sc[:].indirect(offsets[:, CHUNK // 16 : J // 16]))
+        nc.vector.tensor_copy(picked_sc1[:, 0 : 2 * CHUNK], tab_sc[:].indirect(offsets[:, CHUNK // 16 : 3 * CHUNK // 16]))
+        nc.vector.tensor_copy(picked_sc1[:, 2 * CHUNK :], tab_sc[:].indirect(offsets[:, 3 * CHUNK // 16 : J // 16]))
+        idle = psum.tile([P, R], F32, name="y_bank", tag="y_bank", bufs=4)
+        for i in range(3):
+            nc.tensor.matmul_mx(
+                out=idle[:],
+                lhsT=wu[:, 0, 0:P].bitcast(FP8X4),
+                lhsT_scale=picked_sc1[:, 0:P],
+                rhs=wu[:, 0, :].bitcast(FP8X4),
+                rhs_scale=stage0[:, CHUNK : CHUNK + R],
+                start=True,
+                stop=True,
+            )
         wd = sbuf([P, 6 * N], U8, "wd", tag="stage0")
         wd8 = wd[:, 0 : 4 * N]
         wd4 = wd[:, 4 * N : 6 * N]
@@ -227,19 +228,20 @@ def tile_list_modp_gelu_res_noneb_kernel(
         picked0 = placed.tile([P, CHUNK], U32, name="picked0", offset=beyond + 4 * R, align_bytes=64)
         gather(0, picked0[:])
         reorder(1, wu_raw1)
-        part(picks[0], picked0[:])
+        for half in range(CHUNK // HALF):
+            part(picks[0][:, :, 2 * half * HALF : 2 * (half + 1) * HALF], picked0[:, half * HALF : (half + 1) * HALF])
         picked12 = placed.tile([P, 2 * CHUNK], U32, name="picked12", offset=beyond + 4 * R - 4 * CHUNK, align_bytes=64)
         gather(1, picked12[:], 2)
-        part(picks[1], picked12[:, 0:CHUNK])
+        part(picks[1][:], picked12[:, 0:CHUNK])
         seam = page_bytes - HALF * PACK
         first_half(0, picks[0], sbuf([P, HALF * PACK], BF16, "woven0_0"))
         first_half(1, picks[0], placed.tile([P, HALF * PACK], BF16, name="woven0_1", offset=seam, align_bytes=64))
         picked3 = placed.tile([P, CHUNK], U32, name="picked3", offset=seam, align_bytes=64)
         gather(3, picked3[:])
         picks.append(sbuf([P, PASSES, 2 * CHUNK], U8, "v2", "g0_1"))
-        part(picks[2], picked12[:, CHUNK:])
+        part(picks[2][:], picked12[:, CHUNK:])
         picks.append(sbuf([P, PASSES, 2 * CHUNK], U8, "v3"))
-        part(picks[3], picked3[:])
+        part(picks[3][:], picked3[:])
         for i in range(2):
             pages.append(placed.tile([P, T], F32, name="page%d" % (2 + i), offset=page_bytes * i, align_bytes=64))
             nc.gpsimd.memset(pages[2 + i][:].bitcast(I32), 0)

@@ -62,8 +62,10 @@ def tile_list_modp_gelu_res_noneb_kernel(
 
         planes0 = sbuf([P, 2, CHUNK + R + N], U8, "sc_planes0")
         nc.vector.memset(planes0[:].bitcast(I32), 0)
-        planes1 = sbuf([P, 2, J - CHUNK], U8, "sc_planes1")
+        planes1 = sbuf([P, 2, 2 * CHUNK], U8, "sc_planes1")
         nc.vector.memset(planes1[:].bitcast(I32), 0)
+        planes3 = sbuf([P, 2, CHUNK], U8, "sc_planes3")
+        nc.vector.memset(planes3[:].bitcast(I32), 0)
         pages = [sbuf([P, T], F32, "page0")]
         nc.vector.memset(pages[0][:].bitcast(I32), 0)
 
@@ -98,7 +100,8 @@ def tile_list_modp_gelu_res_noneb_kernel(
 
 
         def v_sc(a, j0, width):
-            return planes0[:, a, j0 : j0 + width] if j0 < CHUNK else planes1[:, a, j0 - CHUNK : j0 - CHUNK + width]
+            planes, first = [(planes0, 0), (planes1, CHUNK), (planes1, CHUNK), (planes3, 3 * CHUNK)][j0 // CHUNK]
+            return planes[:, a, j0 - first : j0 - first + width]
 
         h_first = sbuf([P, CHUNK], U32, "h_first")
         h_rest = sbuf([P, J - CHUNK], U32, "h_rest")
@@ -142,8 +145,6 @@ def tile_list_modp_gelu_res_noneb_kernel(
                 sm_t.unsqueeze(1).to_broadcast([P, HALF, PACK]),
                 MULT,
             )
-            cols = slice(half * HALF, (half + 1) * HALF)
-            nc.vector.quantize_mx(out=h_codes(half * HALF, HALF), scales=h_sc[:, cols], in_=woven[:])
 
         def scaled(c):
             g = sbuf([P, PACK, CHUNK], F32, "g%d" % c, "g")
@@ -197,9 +198,9 @@ def tile_list_modp_gelu_res_noneb_kernel(
 
         pages.append(placed.tile([P, T], F32, name="page1", offset=2 * page_bytes, align_bytes=64))
         nc.gpsimd.memset(pages[1][:].bitcast(I32), 0)
-        picked_sc1 = placed.tile([P, J - CHUNK], U8, name="picked_sc1", offset=3 * page_bytes, align_bytes=64)
-        nc.vector.tensor_copy(picked_sc1[:, 0 : 2 * CHUNK], tab_sc[:].indirect(offsets[:, CHUNK // 16 : 3 * CHUNK // 16]))
-        nc.vector.tensor_copy(picked_sc1[:, 2 * CHUNK :], tab_sc[:].indirect(offsets[:, 3 * CHUNK // 16 : J // 16]))
+        picked_sc1 = placed.tile([P, 2 * CHUNK], U8, name="picked_sc1", offset=3 * page_bytes, align_bytes=64)
+        nc.vector.tensor_copy(picked_sc1[:, 0:CHUNK], tab_sc[:].indirect(offsets[:, CHUNK // 16 : 2 * CHUNK // 16]))
+        nc.vector.tensor_copy(picked_sc1[:, CHUNK:], tab_sc[:].indirect(offsets[:, 2 * CHUNK // 16 : 3 * CHUNK // 16]))
         idle = psum.tile([P, R], F32, name="y_bank", tag="y_bank", bufs=4)
         for i in range(3):
             nc.tensor.matmul_mx(
@@ -217,12 +218,6 @@ def tile_list_modp_gelu_res_noneb_kernel(
         nc.sync.dma_start(wd8.bitcast(I32), wd8_words[0].rearrange("p n i -> p (n i)").bitcast(I32))
         nc.sync.dma_start(wd4.bitcast(I32), wd4_words[0].bitcast(I32))
         spread(nc.sync, planes1, picked_sc1)
-        late = sbuf([P, J + 16], F32, "late", tag="tab_sc")
-        weight = late[:, 0:J]
-        b_t = late[:, J : J + BLOCKS]
-        with nc.allow_non_contiguous_dma(reason="one bias value a partition and block"):
-            nc.sync.dma_start(b_t, b.rearrange("(c p) -> p c", p=P))
-        nc.sync.dma_start(weight, wgo)
 
         picks = [sbuf([P, PASSES, 2 * CHUNK], U8, "v%d" % c) for c in range(2)]
         picked0 = placed.tile([P, CHUNK], U32, name="picked0", offset=beyond + 4 * R, align_bytes=64)
@@ -230,12 +225,29 @@ def tile_list_modp_gelu_res_noneb_kernel(
         reorder(1, wu_raw1)
         for half in range(CHUNK // HALF):
             part(picks[0][:, :, 2 * half * HALF : 2 * (half + 1) * HALF], picked0[:, half * HALF : (half + 1) * HALF])
+        picked_sc3 = placed.tile([P, CHUNK], U8, name="picked_sc3", offset=beyond, align_bytes=64)
+        nc.vector.tensor_copy(picked_sc3[:], tab_sc[:].indirect(offsets[:, 3 * CHUNK // 16 : J // 16]))
+        spread(nc.sync, planes3, picked_sc3)
+        late = sbuf([P, J + 16], F32, "late", tag="tab_sc")
+        weight = late[:, 0:J]
+        b_t = late[:, J : J + BLOCKS]
+        with nc.allow_non_contiguous_dma(reason="one bias value a partition and block"):
+            nc.sync.dma_start(b_t, b.rearrange("(c p) -> p c", p=P))
+        nc.sync.dma_start(weight, wgo)
         picked12 = placed.tile([P, 2 * CHUNK], U32, name="picked12", offset=beyond + 4 * R - 4 * CHUNK, align_bytes=64)
-        gather(1, picked12[:], 2)
+        gather(1, picked12[:, 0:CHUNK])
+        gather(2, picked12[:, CHUNK:])
         part(picks[1][:], picked12[:, 0:CHUNK])
         seam = page_bytes - HALF * PACK
-        first_half(0, picks[0], sbuf([P, HALF * PACK], BF16, "woven0_0"))
-        first_half(1, picks[0], placed.tile([P, HALF * PACK], BF16, name="woven0_1", offset=seam, align_bytes=64))
+        wovens = [
+            placed.tile([P, HALF * PACK], BF16, name="woven0_0", offset=seam, align_bytes=64),
+            sbuf([P, HALF * PACK], BF16, "woven0_1"),
+        ]
+        for half in range(CHUNK // HALF):
+            first_half(half, picks[0], wovens[half])
+        for half in range(CHUNK // HALF):
+            cols = slice(half * HALF, (half + 1) * HALF)
+            nc.vector.quantize_mx(out=h_codes(half * HALF, HALF), scales=h_sc[:, cols], in_=wovens[half][:])
         picked3 = placed.tile([P, CHUNK], U32, name="picked3", offset=seam, align_bytes=64)
         gather(3, picked3[:])
         picks.append(sbuf([P, PASSES, 2 * CHUNK], U8, "v2", "g0_1"))

@@ -43,7 +43,7 @@ def tile_list_modp_gelu_res_noneb_kernel(
         nc.sync.dma_start(offsets[:], offs)
 
         tab_sc = sbuf([P, T], U8, "tab_sc")
-        nc.gpsimd.memset(tab_sc[0:ROWS0, :].bitcast(I32), 0)
+        nc.vector.memset(tab_sc[0:ROWS0, :].bitcast(I32), 0)
         nc.sync.dma_start(tab_sc[ROWS0:P, :].bitcast(I32), tab_scales.rearrange("a q t -> q a t").bitcast(I32))
         wu_sc_raw = sbuf([P, R], U8, "wu_sc_raw")
         nc.vector.memset(wu_sc_raw[0:ROWS0, :].bitcast(I32), 0)
@@ -52,20 +52,23 @@ def tile_list_modp_gelu_res_noneb_kernel(
         nc.scalar.dma_start(stage0[ROWS0:P:2, CHUNK + R :].bitcast(I32), wd4_scales[0].bitcast(I32))
         nc.scalar.dma_start(stage0[ROWS0 + 1 : P : 2, CHUNK + R :].bitcast(I32), wd8_scales[0].bitcast(I32))
         page_bytes = 4 * T
-        wu_raw0 = placed.tile([P, R], U32, name="wu_raw0", offset=3 * page_bytes - 2 * R, align_bytes=64)
+        wu_raw0 = sbuf([P, R], U32, "wu_raw0")
         nc.sync.dma_start(wu_raw0[:].bitcast(I32), wu_words[0].rearrange("p r i -> p (r i)").bitcast(I32))
         tab = sbuf([P, T], U32, "tab")
         nc.sync.dma_start(tab[:].bitcast(I32), tab_words[0].rearrange("p t i -> p (t i)").bitcast(I32))
-        beyond = 3 * page_bytes + 4 * R
+        at_weight = 3 * page_bytes
+        at_wd = at_weight + 4 * J
+        at_sm = at_wd + 6 * N
+        at_b = at_sm + 64
+        at_sc = at_b + 64
+        beyond = at_sc + J - CHUNK
         wu_raw1 = placed.tile([P, R], U32, name="wu_raw1", offset=beyond, align_bytes=64)
         nc.sync.dma_start(wu_raw1[:].bitcast(I32), wu_words[1].rearrange("p r i -> p (r i)").bitcast(I32))
 
         planes0 = sbuf([P, 2, CHUNK + R + N], U8, "sc_planes0")
         nc.vector.memset(planes0[:].bitcast(I32), 0)
-        planes1 = sbuf([P, 2, 2 * CHUNK], U8, "sc_planes1")
+        planes1 = sbuf([P, 2, J - CHUNK], U8, "sc_planes1")
         nc.vector.memset(planes1[:].bitcast(I32), 0)
-        planes3 = sbuf([P, 2, CHUNK], U8, "sc_planes3")
-        nc.vector.memset(planes3[:].bitcast(I32), 0)
         pages = [sbuf([P, T], F32, "page0")]
         nc.vector.memset(pages[0][:].bitcast(I32), 0)
 
@@ -75,32 +78,40 @@ def tile_list_modp_gelu_res_noneb_kernel(
                     planes[32 * q : 32 * q + 4, :, :].bitcast(I32), stage[ROWS0 + 8 * q : ROWS0 + 8 * q + 8, :].bitcast(I32)
                 )
 
-        picked_sc0 = sbuf([P, CHUNK], U8, "picked_sc0")
-        nc.vector.tensor_copy(picked_sc0[:], tab_sc[:].indirect(offsets[:, 0 : CHUNK // 16]))
+        picked_sc0 = placed.tile([P, beyond - 2 * page_bytes], U8, name="picked_sc0", offset=2 * page_bytes, align_bytes=64)
+        nc.vector.tensor_copy(picked_sc0[:, 0:CHUNK], tab_sc[:].indirect(offsets[:, 0 : CHUNK // 16]))
         nc.vector.tensor_copy(
             stage0[:, CHUNK : CHUNK + R].rearrange("p (t c i) -> p c t i", t=PACK, i=16),
             wu_sc_raw[:].rearrange("p (c i t) -> p c t i", t=PACK, i=16),
         )
-        nc.vector.tensor_copy(stage0[:, 0:CHUNK].bitcast(I32), picked_sc0[:].bitcast(I32))
-        sm_t = sbuf([P, PACK], F32, "sm_t", "wu_sc_raw")
+        nc.vector.tensor_copy(stage0[:, 0:CHUNK].bitcast(I32), picked_sc0[:, 0:CHUNK].bitcast(I32))
+        spread(nc.sync, planes0, stage0)
+        sm_t = placed.tile([P, PACK], F32, name="sm_t", offset=at_sm, align_bytes=64)
         nc.sync.dma_start(sm_t[:], sm.rearrange("(p t) -> p t", t=PACK))
         sm_t = sm_t[:]
-        spread(nc.sync, planes0, stage0)
+        wd = placed.tile([P, 6 * N], U8, name="wd", offset=at_wd, align_bytes=64)
+        wd8 = wd[:, 0 : 4 * N]
+        wd4 = wd[:, 4 * N : 6 * N]
+        nc.sync.dma_start(wd8.bitcast(I32), wd8_words[0].rearrange("p n i -> p (n i)").bitcast(I32))
+        nc.sync.dma_start(wd4.bitcast(I32), wd4_words[0].bitcast(I32))
+        weight = placed.tile([P, J], F32, name="weight", offset=at_weight, align_bytes=64)
+        nc.sync.dma_start(weight[:], wgo)
+        b_t = placed.tile([P, BLOCKS], F32, name="b_t", offset=at_b, align_bytes=64)
+        with nc.allow_non_contiguous_dma(reason="one bias value a partition and block"):
+            nc.sync.dma_start(b_t[:], b.rearrange("(c p) -> p c", p=P))
 
-        wu = sbuf([P, PASSES, R], U32, "wu", "picked_sc0")
+        wu = [sbuf([P, R], U32, "wu%d" % a) for a in range(PASSES)]
 
-        def reorder(a, raw):
-            nc.vector.tensor_copy(
-                wu[:, a, :].rearrange("p (t c i) -> p c t i", t=PACK, i=4), raw[:].rearrange("p (c i t) -> p c t i", t=PACK, i=4)
-            )
+        def reorder(copy, a, raw):
+            copy(wu[a][:].rearrange("p (t c i) -> p c t i", t=PACK, i=4), raw[:].rearrange("p (c i t) -> p c t i", t=PACK, i=4))
 
-        reorder(0, wu_raw0)
+        reorder(nc.scalar.copy, 0, wu_raw0)
         wu_sc = planes0[:, :, CHUNK : CHUNK + R]
         wd_sc = planes0[:, :, CHUNK + R :]
 
 
         def v_sc(a, j0, width):
-            planes, first = [(planes0, 0), (planes1, CHUNK), (planes1, CHUNK), (planes3, 3 * CHUNK)][j0 // CHUNK]
+            planes, first = (planes0, 0) if j0 < CHUNK else (planes1, CHUNK)
             return planes[:, a, j0 - first : j0 - first + width]
 
         h_first = sbuf([P, CHUNK], U32, "h_first")
@@ -119,16 +130,16 @@ def tile_list_modp_gelu_res_noneb_kernel(
         def up(c, half, v):
             bank = psum.tile([P, PACK, HALF], F32, name="a_bank", tag="a_bank", bufs=4)
             j0 = c * CHUNK + half * HALF
-            for t in range(PACK):
-                for a in range(PASSES):
+            for a in range(PASSES):
+                for t in range(PACK):
                     nc.tensor.matmul_mx(
                         out=bank[:, t, :],
-                        lhsT=wu[:, a, t * P : (t + 1) * P].bitcast(FP8X4),
+                        lhsT=wu[a][:, t * P : (t + 1) * P].bitcast(FP8X4),
                         lhsT_scale=wu_sc[:, a, t * P : (t + 1) * P],
                         rhs=v[:, a, 2 * half * HALF : 2 * (half + 1) * HALF].bitcast(FP4X4),
                         rhs_scale=v_sc(a, j0, HALF),
-                        start=(a == 0),
-                        stop=(a == PASSES - 1),
+                        start=(a == 0 and t == 0),
+                        stop=(a == PASSES - 1 and t == PACK - 1),
                     )
             return bank
 
@@ -198,42 +209,16 @@ def tile_list_modp_gelu_res_noneb_kernel(
 
         pages.append(placed.tile([P, T], F32, name="page1", offset=2 * page_bytes, align_bytes=64))
         nc.gpsimd.memset(pages[1][:].bitcast(I32), 0)
-        picked_sc1 = placed.tile([P, 2 * CHUNK], U8, name="picked_sc1", offset=3 * page_bytes, align_bytes=64)
-        nc.vector.tensor_copy(picked_sc1[:, 0:CHUNK], tab_sc[:].indirect(offsets[:, CHUNK // 16 : 2 * CHUNK // 16]))
-        nc.vector.tensor_copy(picked_sc1[:, CHUNK:], tab_sc[:].indirect(offsets[:, 2 * CHUNK // 16 : 3 * CHUNK // 16]))
-        idle = psum.tile([P, R], F32, name="y_bank", tag="y_bank", bufs=4)
-        for i in range(3):
-            nc.tensor.matmul_mx(
-                out=idle[:],
-                lhsT=wu[:, 0, 0:P].bitcast(FP8X4),
-                lhsT_scale=picked_sc1[:, 0:P],
-                rhs=wu[:, 0, :].bitcast(FP8X4),
-                rhs_scale=stage0[:, CHUNK : CHUNK + R],
-                start=True,
-                stop=True,
-            )
-        wd = sbuf([P, 6 * N], U8, "wd", tag="stage0")
-        wd8 = wd[:, 0 : 4 * N]
-        wd4 = wd[:, 4 * N : 6 * N]
-        nc.sync.dma_start(wd8.bitcast(I32), wd8_words[0].rearrange("p n i -> p (n i)").bitcast(I32))
-        nc.sync.dma_start(wd4.bitcast(I32), wd4_words[0].bitcast(I32))
+        picked_sc1 = placed.tile([P, J - CHUNK], U8, name="picked_sc1", offset=at_sc, align_bytes=64)
+        nc.vector.tensor_copy(picked_sc1[:], tab_sc[:].indirect(offsets[:, CHUNK // 16 : J // 16]))
         spread(nc.sync, planes1, picked_sc1)
 
         picks = [sbuf([P, PASSES, 2 * CHUNK], U8, "v%d" % c) for c in range(2)]
         picked0 = placed.tile([P, CHUNK], U32, name="picked0", offset=beyond + 4 * R, align_bytes=64)
         gather(0, picked0[:])
-        reorder(1, wu_raw1)
+        reorder(nc.vector.tensor_copy, 1, wu_raw1)
         for half in range(CHUNK // HALF):
             part(picks[0][:, :, 2 * half * HALF : 2 * (half + 1) * HALF], picked0[:, half * HALF : (half + 1) * HALF])
-        picked_sc3 = placed.tile([P, CHUNK], U8, name="picked_sc3", offset=beyond, align_bytes=64)
-        nc.vector.tensor_copy(picked_sc3[:], tab_sc[:].indirect(offsets[:, 3 * CHUNK // 16 : J // 16]))
-        spread(nc.sync, planes3, picked_sc3)
-        late = sbuf([P, J + 16], F32, "late", tag="tab_sc")
-        weight = late[:, 0:J]
-        b_t = late[:, J : J + BLOCKS]
-        with nc.allow_non_contiguous_dma(reason="one bias value a partition and block"):
-            nc.sync.dma_start(b_t, b.rearrange("(c p) -> p c", p=P))
-        nc.sync.dma_start(weight, wgo)
         picked12 = placed.tile([P, 2 * CHUNK], U32, name="picked12", offset=beyond + 4 * R - 4 * CHUNK, align_bytes=64)
         gather(1, picked12[:, 0:CHUNK])
         gather(2, picked12[:, CHUNK:])

@@ -24,6 +24,7 @@ CHUNKS = J // CHUNK
 HALF = 128
 BLOCKS = N // P
 ROWS0 = 96
+EARLY = 2 * CHUNK
 
 
 def tile_list_modp_gelu_res_noneb_kernel(
@@ -34,6 +35,7 @@ def tile_list_modp_gelu_res_noneb_kernel(
         lists = ctx.enter_context(tc.tile_pool(name="lists", bufs=1))
         pool = ctx.enter_context(tc.tile_pool(name="pool", bufs=1))
         placed = ctx.enter_context(tc.tile_pool(name="placed", bufs=1))
+        hidden = ctx.enter_context(tc.tile_pool(name="hidden", bufs=1))
         psum = ctx.enter_context(tc.psum_pool(name="psum", bufs=1))
 
         def sbuf(shape, dtype, name, tag=None):
@@ -48,9 +50,9 @@ def tile_list_modp_gelu_res_noneb_kernel(
         wu_sc_raw = sbuf([P, R], U8, "wu_sc_raw")
         nc.vector.memset(wu_sc_raw[0:ROWS0, :].bitcast(I32), 0)
         nc.scalar.dma_start(wu_sc_raw[ROWS0:P, :].bitcast(I32), wu_scales.rearrange("a q r -> q a r").bitcast(I32))
-        stage0 = sbuf([P, CHUNK + R + N], U8, "stage0")
-        nc.scalar.dma_start(stage0[ROWS0:P:2, CHUNK + R :].bitcast(I32), wd4_scales[0].bitcast(I32))
-        nc.scalar.dma_start(stage0[ROWS0 + 1 : P : 2, CHUNK + R :].bitcast(I32), wd8_scales[0].bitcast(I32))
+        stage0 = sbuf([P, EARLY + R + N], U8, "stage0")
+        nc.scalar.dma_start(stage0[ROWS0:P:2, EARLY + R :].bitcast(I32), wd4_scales[0].bitcast(I32))
+        nc.scalar.dma_start(stage0[ROWS0 + 1 : P : 2, EARLY + R :].bitcast(I32), wd8_scales[0].bitcast(I32))
         page_bytes = 4 * T
         wu_raw0 = sbuf([P, R], U32, "wu_raw0")
         nc.sync.dma_start(wu_raw0[:].bitcast(I32), wu_words[0].rearrange("p r i -> p (r i)").bitcast(I32))
@@ -61,13 +63,13 @@ def tile_list_modp_gelu_res_noneb_kernel(
         at_sm = at_wd + 6 * N
         at_b = at_sm + 64
         at_sc = at_b + 64
-        beyond = at_sc + J - CHUNK
+        beyond = at_sc + J - EARLY
         wu_raw1 = placed.tile([P, R], U32, name="wu_raw1", offset=beyond, align_bytes=64)
         nc.sync.dma_start(wu_raw1[:].bitcast(I32), wu_words[1].rearrange("p r i -> p (r i)").bitcast(I32))
 
-        planes0 = sbuf([P, 2, CHUNK + R + N], U8, "sc_planes0")
+        planes0 = sbuf([P, 2, EARLY + R + N], U8, "sc_planes0")
         nc.vector.memset(planes0[:].bitcast(I32), 0)
-        planes1 = sbuf([P, 2, J - CHUNK], U8, "sc_planes1")
+        planes1 = sbuf([P, 2, J - EARLY], U8, "sc_planes1")
         nc.vector.memset(planes1[:].bitcast(I32), 0)
         pages = [sbuf([P, T], F32, "page0")]
         nc.vector.memset(pages[0][:].bitcast(I32), 0)
@@ -79,12 +81,12 @@ def tile_list_modp_gelu_res_noneb_kernel(
                 )
 
         picked_sc0 = placed.tile([P, beyond - 2 * page_bytes], U8, name="picked_sc0", offset=2 * page_bytes, align_bytes=64)
-        nc.vector.tensor_copy(picked_sc0[:, 0:CHUNK], tab_sc[:].indirect(offsets[:, 0 : CHUNK // 16]))
+        nc.vector.tensor_copy(picked_sc0[:, 0:EARLY], tab_sc[:].indirect(offsets[:, 0 : EARLY // 16]))
         nc.vector.tensor_copy(
-            stage0[:, CHUNK : CHUNK + R].rearrange("p (t c i) -> p c t i", t=PACK, i=16),
+            stage0[:, EARLY : EARLY + R].rearrange("p (t c i) -> p c t i", t=PACK, i=16),
             wu_sc_raw[:].rearrange("p (c i t) -> p c t i", t=PACK, i=16),
         )
-        nc.vector.tensor_copy(stage0[:, 0:CHUNK].bitcast(I32), picked_sc0[:, 0:CHUNK].bitcast(I32))
+        nc.vector.tensor_copy(stage0[:, 0:EARLY].bitcast(I32), picked_sc0[:, 0:EARLY].bitcast(I32))
         spread(nc.sync, planes0, stage0)
         sm_t = placed.tile([P, PACK], F32, name="sm_t", offset=at_sm, align_bytes=64)
         nc.sync.dma_start(sm_t[:], sm.rearrange("(p t) -> p t", t=PACK))
@@ -94,11 +96,6 @@ def tile_list_modp_gelu_res_noneb_kernel(
         wd4 = wd[:, 4 * N : 6 * N]
         nc.sync.dma_start(wd8.bitcast(I32), wd8_words[0].rearrange("p n i -> p (n i)").bitcast(I32))
         nc.sync.dma_start(wd4.bitcast(I32), wd4_words[0].bitcast(I32))
-        weight = placed.tile([P, J], F32, name="weight", offset=at_weight, align_bytes=64)
-        nc.sync.dma_start(weight[:], wgo)
-        b_t = placed.tile([P, BLOCKS], F32, name="b_t", offset=at_b, align_bytes=64)
-        with nc.allow_non_contiguous_dma(reason="one bias value a partition and block"):
-            nc.sync.dma_start(b_t[:], b.rearrange("(c p) -> p c", p=P))
 
         wu = [sbuf([P, R], U32, "wu%d" % a) for a in range(PASSES)]
 
@@ -106,15 +103,26 @@ def tile_list_modp_gelu_res_noneb_kernel(
             copy(wu[a][:].rearrange("p (t c i) -> p c t i", t=PACK, i=4), raw[:].rearrange("p (c i t) -> p c t i", t=PACK, i=4))
 
         reorder(nc.scalar.copy, 0, wu_raw0)
-        wu_sc = planes0[:, :, CHUNK : CHUNK + R]
-        wd_sc = planes0[:, :, CHUNK + R :]
+        idle = psum.tile([P, R], F32, name="y_bank", tag="y_bank", bufs=4)
+        for i in range(3):
+            nc.tensor.matmul_mx(
+                out=idle[:],
+                lhsT=wu[0][:, 0:P].bitcast(FP8X4),
+                lhsT_scale=wu_sc_raw[:, 0:P],
+                rhs=wu[0][:].bitcast(FP8X4),
+                rhs_scale=wu_sc_raw[:],
+                start=True,
+                stop=True,
+            )
+        wu_sc = planes0[:, :, EARLY : EARLY + R]
+        wd_sc = planes0[:, :, EARLY + R :]
 
 
         def v_sc(a, j0, width):
-            planes, first = (planes0, 0) if j0 < CHUNK else (planes1, CHUNK)
+            planes, first = (planes0, 0) if j0 < EARLY else (planes1, EARLY)
             return planes[:, a, j0 - first : j0 - first + width]
 
-        h_first = sbuf([P, CHUNK], U32, "h_first")
+        h_first = hidden.tile([P, CHUNK], U32, name="h_first", offset=12 * CHUNK, align_bytes=64)
         h_rest = sbuf([P, J - CHUNK], U32, "h_rest")
         h_sc = sbuf([P, J], U8, "h_sc")
 
@@ -157,14 +165,17 @@ def tile_list_modp_gelu_res_noneb_kernel(
                 MULT,
             )
 
-        def scaled(c):
-            g = sbuf([P, PACK, CHUNK], F32, "g%d" % c, "g")
-            for half in range(CHUNK // HALF):
-                nc.scalar.activation(g[:, :, half * HALF : (half + 1) * HALF], up(c, half, picks[c])[:], ACT.Gelu_apprx_tanh)
-            planes = sbuf([P, PACK * CHUNK], BF16, "planes%d" % c, "h_first" if c == 1 else None)
+        def at_planes(c):
+            return (20 * c - 8) * CHUNK
+
+        def gelu(c, half, g):
+            nc.scalar.activation(g[:, :, half * HALF : (half + 1) * HALF], up(c, half, picks[c])[:], ACT.Gelu_apprx_tanh)
+
+        def scale(c, g):
+            planes = hidden.tile([P, PACK * CHUNK], BF16, name="planes%d" % c, offset=at_planes(c), align_bytes=64)
             for t in range(PACK):
                 nc.scalar.activation(planes[:, t * CHUNK : (t + 1) * CHUNK], g[:, t, :], ACT.Copy, scale=sm_t[:, t : t + 1])
-            return g[:, PACK - 1, :], planes
+            return planes
 
         def weave(c, planes):
             woven = sbuf([P, CHUNK * PACK], BF16, "woven%d" % c)
@@ -173,9 +184,12 @@ def tile_list_modp_gelu_res_noneb_kernel(
                 planes[:].rearrange("p (t c i) -> p c t i", t=PACK, i=4),
             )
             quantise(c, woven)
-            return planes[:].bitcast(F32)[:, 0:CHUNK]
 
-        def down(block, j0, width, narrow):
+        def behind_weave(c, half, shape, name):
+            size = 4 * CHUNK * (PACK if len(shape) == 3 else 1)
+            return hidden.tile(shape, F32, name=name, offset=at_planes(c) + 4 * CHUNK - (0 if half else size), align_bytes=64)
+
+        def down(block, j0, width):
             bank = psum.tile([P, width], F32, name="y_bank", tag="y_bank", bufs=4)
             cols = slice(block * P, (block + 1) * P)
             nc.tensor.matmul_mx(
@@ -187,16 +201,15 @@ def tile_list_modp_gelu_res_noneb_kernel(
                 start=True,
                 stop=False,
             )
-            for s in range(0, width, narrow):
-                nc.tensor.matmul_mx(
-                    out=bank[:, s : s + narrow],
-                    lhsT=wd4[:, 2 * block * P : 2 * (block + 1) * P].bitcast(FP4X4),
-                    lhsT_scale=wd_sc[:, 0, cols],
-                    rhs=h_codes(j0 + s, narrow),
-                    rhs_scale=h_sc[:, j0 + s : j0 + s + narrow],
-                    start=False,
-                    stop=(s + narrow == width),
-                )
+            nc.tensor.matmul_mx(
+                out=bank[:],
+                lhsT=wd4[:, 2 * block * P : 2 * (block + 1) * P].bitcast(FP4X4),
+                lhsT_scale=wd_sc[:, 0, cols],
+                rhs=h_codes(j0, width),
+                rhs_scale=h_sc[:, j0 : j0 + width],
+                start=False,
+                stop=True,
+            )
             return bank
 
         def add_bias(y, bank, block):
@@ -209,8 +222,14 @@ def tile_list_modp_gelu_res_noneb_kernel(
 
         pages.append(placed.tile([P, T], F32, name="page1", offset=2 * page_bytes, align_bytes=64))
         nc.gpsimd.memset(pages[1][:].bitcast(I32), 0)
-        picked_sc1 = placed.tile([P, J - CHUNK], U8, name="picked_sc1", offset=at_sc, align_bytes=64)
-        nc.vector.tensor_copy(picked_sc1[:], tab_sc[:].indirect(offsets[:, CHUNK // 16 : J // 16]))
+        picked_sc1 = placed.tile([P, J - EARLY], U8, name="picked_sc1", offset=at_sc, align_bytes=64)
+        nc.vector.tensor_copy(picked_sc1[:], tab_sc[:].indirect(offsets[:, EARLY // 16 : J // 16]))
+        late = sbuf([P, J + 16], F32, "late", tag="tab_sc")
+        weight = late[:, 0:J]
+        b_t = late[:, J : J + BLOCKS]
+        with nc.allow_non_contiguous_dma(reason="one bias value a partition and block"):
+            nc.sync.dma_start(b_t, b.rearrange("(c p) -> p c", p=P))
+        nc.sync.dma_start(weight, wgo)
         spread(nc.sync, planes1, picked_sc1)
 
         picks = [sbuf([P, PASSES, 2 * CHUNK], U8, "v%d" % c) for c in range(2)]
@@ -243,36 +262,51 @@ def tile_list_modp_gelu_res_noneb_kernel(
             pages.append(placed.tile([P, T], F32, name="page%d" % (2 + i), offset=page_bytes * i, align_bytes=64))
             nc.gpsimd.memset(pages[2 + i][:].bitcast(I32), 0)
 
-        def place(c, block, bank, y=None, chunks=1):
+        def biased(c, block, y=None, bank=None):
             if y is None:
-                y = sbuf([P, chunks * CHUNK], F32, "y%d_%d" % (c, block))[:]
-            add_bias(y, bank, block)
+                y = sbuf([P, CHUNK], F32, "y%d_%d" % (c, block))[:]
+            add_bias(y, down(block, c * CHUNK, CHUNK) if bank is None else bank, block)
+            return y
+
+        def place(c, block, y, chunks=1):
             scatter(pages[block], y, c * CHUNK, chunks * CHUNK)
             if c + chunks == CHUNKS:
                 nc.sync.dma_start(out[block * P : (block + 1) * P, :], pages[block][:])
 
-        def downs(c, blocks):
-            return {block: down(block, c * CHUNK, CHUNK, HALF) for block in blocks}
-
+        g = sbuf([P, PACK, CHUNK], F32, "g1", "g")
+        gelu(1, 0, g)
+        gelu(1, 1, g)
         y = sbuf([P, CHUNK], F32, "y_first")
         for half in range(CHUNK // HALF):
-            add_bias(y[:, half * HALF : (half + 1) * HALF], down(0, half * HALF, HALF, HALF), 0)
-        scatter(pages[0], y[:], 0, CHUNK)
-        banks = downs(0, range(1, BLOCKS))
-        place(0, 1, banks[1])
-        place(0, 2, banks[2])
-        place(0, 3, banks[3], weave(1, scaled(1)[1]))
+            add_bias(y[:, half * HALF : (half + 1) * HALF], down(0, half * HALF, HALF), 0)
+        place(0, 0, y[:])
+        banks = [down(block, 0, CHUNK) for block in range(1, BLOCKS)]
+        place(0, 1, biased(0, 1, bank=banks[0]))
+        planes = scale(1, g)
+        place(0, 2, biased(0, 2, bank=banks[1]))
+        weave(1, planes)
+        place(0, 3, biased(0, 3, behind_weave(1, 1, [P, CHUNK], "y0_3")[:], banks[2]))
 
-        banks = downs(1, range(BLOCKS))
-        for block in range(BLOCKS - 1):
-            place(1, block, banks[block])
-        place(1, 3, banks[3], weave(2, scaled(2)[1]))
+        g = behind_weave(1, 0, [P, PACK, CHUNK], "g2")
+        gelu(2, 0, g)
+        gelu(2, 1, g)
+        planes = scale(2, g)
+        spent = g
+        place(1, 0, biased(1, 0, spent[:, 0, :]))
+        weave(2, planes)
+        place(1, 1, biased(1, 1, spent[:, 1, :]))
+        place(1, 2, biased(1, 2, spent[:, 2, :]))
 
-        banks = downs(2, range(BLOCKS - 1))
-        place(2, 0, banks[0])
-        place(2, 1, banks[1])
-        place(2, 2, banks[2], weave(3, scaled(3)[1]))
-        banks = downs(3, range(BLOCKS - 1))
-        for block in range(BLOCKS - 1):
-            place(3, block, banks[block])
-        place(2, 3, down(3, 2 * CHUNK, 2 * CHUNK, 2 * CHUNK), chunks=2)
+        g = behind_weave(2, 0, [P, PACK, CHUNK], "g3")
+        gelu(3, 0, g)
+        gelu(3, 1, g)
+        place(1, 3, biased(1, 3, spent[:, 3, :]))
+        weave(3, scale(3, g))
+        for block in range(2):
+            place(2, block, biased(2, block, behind_weave(3, block, [P, CHUNK], "y2_%d" % block)[:]))
+        for block in range(2):
+            place(3, block, biased(3, block))
+        for block in range(2, BLOCKS):
+            y = sbuf([P, 2 * CHUNK], F32, "y_last%d" % block)
+            add_bias(y[:], down(block, 2 * CHUNK, 2 * CHUNK), block)
+            place(2, block, y[:], chunks=2)

@@ -45,7 +45,7 @@ def tile_list_modp_gelu_res_noneb_kernel(
         nc.sync.dma_start(offsets[:], offs)
 
         tab_sc = sbuf([P, T], U8, "tab_sc")
-        nc.vector.memset(tab_sc[0:ROWS0, :].bitcast(I32), 0)
+        nc.gpsimd.memset(tab_sc[0:ROWS0, :].bitcast(I32), 0)
         nc.sync.dma_start(tab_sc[ROWS0:P, :].bitcast(I32), tab_scales.rearrange("a q t -> q a t").bitcast(I32))
         wu_sc_raw = sbuf([P, R], U8, "wu_sc_raw")
         nc.vector.memset(wu_sc_raw[0:ROWS0, :].bitcast(I32), 0)
@@ -74,9 +74,9 @@ def tile_list_modp_gelu_res_noneb_kernel(
         pages = [sbuf([P, T], F32, "page0")]
         nc.vector.memset(pages[0][:].bitcast(I32), 0)
 
-        def spread(queue, planes, stage):
-            for q in range(4):
-                queue.dma_start(
+        def spread(queues, planes, stage):
+            for q in (0, 2, 1, 3):
+                queues[q // 2].dma_start(
                     planes[32 * q : 32 * q + 4, :, :].bitcast(I32), stage[ROWS0 + 8 * q : ROWS0 + 8 * q + 8, :].bitcast(I32)
                 )
 
@@ -87,7 +87,7 @@ def tile_list_modp_gelu_res_noneb_kernel(
             wu_sc_raw[:].rearrange("p (c i t) -> p c t i", t=PACK, i=16),
         )
         nc.vector.tensor_copy(stage0[:, 0:EARLY].bitcast(I32), picked_sc0[:, 0:EARLY].bitcast(I32))
-        spread(nc.sync, planes0, stage0)
+        spread((nc.sync, nc.scalar), planes0, stage0)
         sm_t = placed.tile([P, PACK], F32, name="sm_t", offset=at_sm, align_bytes=64)
         nc.sync.dma_start(sm_t[:], sm.rearrange("(p t) -> p t", t=PACK))
         sm_t = sm_t[:]
@@ -108,9 +108,9 @@ def tile_list_modp_gelu_res_noneb_kernel(
             nc.tensor.matmul_mx(
                 out=idle[:],
                 lhsT=wu[0][:, 0:P].bitcast(FP8X4),
-                lhsT_scale=wu_sc_raw[:, 0:P],
+                lhsT_scale=stage0[:, EARLY : EARLY + P],
                 rhs=wu[0][:].bitcast(FP8X4),
-                rhs_scale=wu_sc_raw[:],
+                rhs_scale=stage0[:, EARLY : EARLY + R],
                 start=True,
                 stop=True,
             )
@@ -230,7 +230,7 @@ def tile_list_modp_gelu_res_noneb_kernel(
         with nc.allow_non_contiguous_dma(reason="one bias value a partition and block"):
             nc.sync.dma_start(b_t, b.rearrange("(c p) -> p c", p=P))
         nc.sync.dma_start(weight, wgo)
-        spread(nc.sync, planes1, picked_sc1)
+        spread((nc.sync, nc.sync), planes1, picked_sc1)
 
         picks = [sbuf([P, PASSES, 2 * CHUNK], U8, "v%d" % c) for c in range(2)]
         picked0 = placed.tile([P, CHUNK], U32, name="picked0", offset=beyond + 4 * R, align_bytes=64)

@@ -44,7 +44,8 @@ def tile_list_modp_gelu_res_noneb_kernel(
         offsets = lists.tile([P, J // 16], U16, name="offsets")
         nc.sync.dma_start(offsets[:], offs)
 
-        tab_sc = sbuf([P, T], U8, "tab_sc")
+        late = ctx.enter_context(tc.tile_pool(name="late", bufs=1))
+        tab_sc = late.tile([P, T], U8, name="tab_sc", offset=4 * J - 64, align_bytes=64)
         nc.gpsimd.memset(tab_sc[0:ROWS0, :].bitcast(I32), 0)
         nc.sync.dma_start(tab_sc[ROWS0:P, :].bitcast(I32), tab_scales.rearrange("a q t -> q a t").bitcast(I32))
         wu_sc_raw = sbuf([P, R], U8, "wu_sc_raw")
@@ -80,22 +81,17 @@ def tile_list_modp_gelu_res_noneb_kernel(
                     planes[32 * q : 32 * q + 4, :, :].bitcast(I32), stage[ROWS0 + 8 * q : ROWS0 + 8 * q + 8, :].bitcast(I32)
                 )
 
-        picked_sc0 = placed.tile([P, beyond - 2 * page_bytes], U8, name="picked_sc0", offset=2 * page_bytes, align_bytes=64)
-        nc.vector.tensor_copy(picked_sc0[:, 0:EARLY], tab_sc[:].indirect(offsets[:, 0 : EARLY // 16]))
         nc.vector.tensor_copy(
             stage0[:, EARLY : EARLY + R].rearrange("p (t c i) -> p c t i", t=PACK, i=16),
             wu_sc_raw[:].rearrange("p (c i t) -> p c t i", t=PACK, i=16),
         )
+        picked_sc0 = placed.tile([P, beyond - 2 * page_bytes], U8, name="picked_sc0", offset=2 * page_bytes, align_bytes=64)
+        nc.vector.tensor_copy(picked_sc0[:, 0:EARLY], tab_sc[:].indirect(offsets[:, 0 : EARLY // 16]))
         nc.vector.tensor_copy(stage0[:, 0:EARLY].bitcast(I32), picked_sc0[:, 0:EARLY].bitcast(I32))
         spread((nc.sync, nc.scalar), planes0, stage0)
         sm_t = placed.tile([P, PACK], F32, name="sm_t", offset=at_sm, align_bytes=64)
         nc.sync.dma_start(sm_t[:], sm.rearrange("(p t) -> p t", t=PACK))
         sm_t = sm_t[:]
-        wd = placed.tile([P, 6 * N], U8, name="wd", offset=at_wd, align_bytes=64)
-        wd8 = wd[:, 0 : 4 * N]
-        wd4 = wd[:, 4 * N : 6 * N]
-        nc.sync.dma_start(wd8.bitcast(I32), wd8_words[0].rearrange("p n i -> p (n i)").bitcast(I32))
-        nc.sync.dma_start(wd4.bitcast(I32), wd4_words[0].bitcast(I32))
 
         wu = [sbuf([P, R], U32, "wu%d" % a) for a in range(PASSES)]
 
@@ -224,12 +220,16 @@ def tile_list_modp_gelu_res_noneb_kernel(
         nc.gpsimd.memset(pages[1][:].bitcast(I32), 0)
         picked_sc1 = placed.tile([P, J - EARLY], U8, name="picked_sc1", offset=at_sc, align_bytes=64)
         nc.vector.tensor_copy(picked_sc1[:], tab_sc[:].indirect(offsets[:, EARLY // 16 : J // 16]))
-        late = sbuf([P, J + 16], F32, "late", tag="tab_sc")
-        weight = late[:, 0:J]
-        b_t = late[:, J : J + BLOCKS]
+        wd = late.tile([P, 6 * N], U8, name="wd", offset=4 * J + 64, align_bytes=64)
+        wd8 = wd[:, 0 : 4 * N]
+        wd4 = wd[:, 4 * N : 6 * N]
+        nc.sync.dma_start(wd8.bitcast(I32), wd8_words[0].rearrange("p n i -> p (n i)").bitcast(I32))
+        nc.sync.dma_start(wd4.bitcast(I32), wd4_words[0].bitcast(I32))
+        b_t = late.tile([P, BLOCKS], F32, name="b_t", offset=4 * J, align_bytes=64)
         with nc.allow_non_contiguous_dma(reason="one bias value a partition and block"):
-            nc.sync.dma_start(b_t, b.rearrange("(c p) -> p c", p=P))
-        nc.sync.dma_start(weight, wgo)
+            nc.sync.dma_start(b_t[:], b.rearrange("(c p) -> p c", p=P))
+        weight = late.tile([P, J], F32, name="weight", offset=0, align_bytes=64)
+        nc.sync.dma_start(weight[:], wgo)
         spread((nc.sync, nc.sync), planes1, picked_sc1)
 
         picks = [sbuf([P, PASSES, 2 * CHUNK], U8, "v%d" % c) for c in range(2)]

@@ -24,7 +24,9 @@ CHUNKS = J // CHUNK
 HALF = 128
 BLOCKS = N // P
 ROWS0 = 96
-EARLY = 2 * CHUNK
+EARLY = CHUNK
+WARM_PASSES = 5
+WARM_COLUMNS = 32
 
 
 def tile_list_modp_gelu_res_noneb_kernel(
@@ -46,73 +48,82 @@ def tile_list_modp_gelu_res_noneb_kernel(
 
         late = ctx.enter_context(tc.tile_pool(name="late", bufs=1))
         tab_sc = late.tile([P, T], U8, name="tab_sc", offset=4 * J - 64, align_bytes=64)
-        nc.gpsimd.memset(tab_sc[0:ROWS0, :].bitcast(I32), 0)
         nc.sync.dma_start(tab_sc[ROWS0:P, :].bitcast(I32), tab_scales.rearrange("a q t -> q a t").bitcast(I32))
-        wu_sc_raw = sbuf([P, R], U8, "wu_sc_raw")
-        nc.vector.memset(wu_sc_raw[0:ROWS0, :].bitcast(I32), 0)
-        nc.scalar.dma_start(wu_sc_raw[ROWS0:P, :].bitcast(I32), wu_scales.rearrange("a q r -> q a r").bitcast(I32))
+        early = ctx.enter_context(tc.tile_pool(name="early", bufs=1))
+        wu_sc_raw = early.tile([P, R], U8, name="wu_sc_raw", offset=0, align_bytes=64)
+        nc.sync.dma_start(wu_sc_raw[ROWS0:P, :].bitcast(I32), wu_scales.rearrange("a q r -> q a r").bitcast(I32))
         stage0 = sbuf([P, EARLY + R + N], U8, "stage0")
         nc.scalar.dma_start(stage0[ROWS0:P:2, EARLY + R :].bitcast(I32), wd4_scales[0].bitcast(I32))
         nc.scalar.dma_start(stage0[ROWS0 + 1 : P : 2, EARLY + R :].bitcast(I32), wd8_scales[0].bitcast(I32))
+        sm_t = sbuf([P, PACK], F32, "sm_t")
+        nc.scalar.dma_start(sm_t[:], sm.rearrange("(p t) -> p t", t=PACK))
+        sm_t = sm_t[:]
         page_bytes = 4 * T
-        wu_raw0 = sbuf([P, R], U32, "wu_raw0")
-        nc.sync.dma_start(wu_raw0[:].bitcast(I32), wu_words[0].rearrange("p r i -> p (r i)").bitcast(I32))
+        wu_raw = [sbuf([P, R], U32, "wu_raw%d" % a) for a in range(PASSES)]
+        nc.sync.dma_start(wu_raw[0][:].bitcast(I32), wu_words[0].rearrange("p r i -> p (r i)").bitcast(I32))
         tab = sbuf([P, T], U32, "tab")
         nc.sync.dma_start(tab[:].bitcast(I32), tab_words[0].rearrange("p t i -> p (t i)").bitcast(I32))
-        at_weight = 3 * page_bytes
-        at_wd = at_weight + 4 * J
-        at_sm = at_wd + 6 * N
-        at_b = at_sm + 64
-        at_sc = at_b + 64
-        beyond = at_sc + J - EARLY
-        wu_raw1 = placed.tile([P, R], U32, name="wu_raw1", offset=beyond, align_bytes=64)
-        nc.sync.dma_start(wu_raw1[:].bitcast(I32), wu_words[1].rearrange("p r i -> p (r i)").bitcast(I32))
+        nc.sync.dma_start(wu_raw[1][:].bitcast(I32), wu_words[1].rearrange("p r i -> p (r i)").bitcast(I32))
 
+        seed = sbuf([P, 2], F32, "seed")
+        nc.vector.memset(seed[:, 0:1], 0.0)
+        nc.scalar.activation(seed[:, 1:2], seed[:, 0:1], ACT.Gelu_apprx_tanh)
+
+        def clear_beside_gpsimd(words):
+            cut = words.shape[1] // 2 - 1
+            nc.vector.memset(words[:, 0:cut], 0)
+            nc.vector.memset(words[:, cut:], 0)
+
+        clear_beside_gpsimd(tab_sc[0:ROWS0, :].bitcast(I32))
+        clear_beside_gpsimd(wu_sc_raw[0:ROWS0, :].bitcast(I32))
         planes0 = sbuf([P, 2, EARLY + R + N], U8, "sc_planes0")
-        nc.vector.memset(planes0[:].bitcast(I32), 0)
-        planes1 = sbuf([P, 2, J - EARLY], U8, "sc_planes1")
-        nc.vector.memset(planes1[:].bitcast(I32), 0)
+        clear_beside_gpsimd(planes0[:].rearrange("p a n -> p (a n)").bitcast(I32))
         pages = [sbuf([P, T], F32, "page0")]
-        nc.vector.memset(pages[0][:].bitcast(I32), 0)
+        nc.gpsimd.memset(pages[0][:].bitcast(I32), 0)
+        planes1 = sbuf([P, 2, J - EARLY], U8, "sc_planes1")
+        nc.gpsimd.memset(planes1[:].bitcast(I32), 0)
 
-        def spread(queues, planes, stage):
+        def spread(queue, planes, stage):
             for q in (0, 2, 1, 3):
-                queues[q // 2].dma_start(
+                queue.dma_start(
                     planes[32 * q : 32 * q + 4, :, :].bitcast(I32), stage[ROWS0 + 8 * q : ROWS0 + 8 * q + 8, :].bitcast(I32)
                 )
 
+        def gather_scales(picked, j0, width):
+            nc.vector.tensor_copy(picked, tab_sc[:].indirect(offsets[:, j0 // 16 : (j0 + width) // 16]))
+
+        picked_sc0 = placed.tile([P, EARLY], U8, name="picked_sc0", offset=2 * page_bytes, align_bytes=64)
+        picked_sc1 = early.tile([P, J - EARLY], U8, name="picked_sc1", offset=0, align_bytes=64)
+        gather_scales(picked_sc0[:], 0, EARLY)
         nc.vector.tensor_copy(
             stage0[:, EARLY : EARLY + R].rearrange("p (t c i) -> p c t i", t=PACK, i=16),
             wu_sc_raw[:].rearrange("p (c i t) -> p c t i", t=PACK, i=16),
         )
-        picked_sc0 = placed.tile([P, beyond - 2 * page_bytes], U8, name="picked_sc0", offset=2 * page_bytes, align_bytes=64)
-        nc.vector.tensor_copy(picked_sc0[:, 0:EARLY], tab_sc[:].indirect(offsets[:, 0 : EARLY // 16]))
-        nc.vector.tensor_copy(stage0[:, 0:EARLY].bitcast(I32), picked_sc0[:, 0:EARLY].bitcast(I32))
-        spread((nc.sync, nc.scalar), planes0, stage0)
-        sm_t = placed.tile([P, PACK], F32, name="sm_t", offset=at_sm, align_bytes=64)
-        nc.sync.dma_start(sm_t[:], sm.rearrange("(p t) -> p t", t=PACK))
-        sm_t = sm_t[:]
+        nc.vector.tensor_copy(stage0[:, 0:EARLY].bitcast(I32), picked_sc0[:].bitcast(I32))
+        spread(nc.scalar, planes0, stage0)
+        gather_scales(picked_sc1[:], EARLY, J - EARLY)
 
-        wu = [sbuf([P, R], U32, "wu%d" % a) for a in range(PASSES)]
+        wu = [[sbuf([P, 2 * P], U32, "wu%d_%d" % (a, u)) for u in range(2)] for a in range(PASSES)]
+        for a in range(PASSES):
+            for u in range(2):
+                nc.scalar.copy(
+                    wu[a][u][:].rearrange("p (t c i) -> p c t i", t=2, i=4),
+                    wu_raw[a][:].rearrange("p (c i t) -> p c t i", t=PACK, i=4)[:, :, 2 * u : 2 * u + 2, :],
+                )
 
-        def reorder(copy, a, raw):
-            copy(wu[a][:].rearrange("p (t c i) -> p c t i", t=PACK, i=4), raw[:].rearrange("p (c i t) -> p c t i", t=PACK, i=4))
-
-        reorder(nc.scalar.copy, 0, wu_raw0)
         idle = psum.tile([P, R], F32, name="y_bank", tag="y_bank", bufs=4)
-        for i in range(3):
+        for i in range(WARM_PASSES):
             nc.tensor.matmul_mx(
-                out=idle[:],
-                lhsT=wu[0][:, 0:P].bitcast(FP8X4),
-                lhsT_scale=stage0[:, EARLY : EARLY + P],
-                rhs=wu[0][:].bitcast(FP8X4),
+                out=idle[0:WARM_COLUMNS, :],
+                lhsT=wu_raw[0][:, 0:WARM_COLUMNS].bitcast(FP8X4),
+                lhsT_scale=stage0[:, EARLY : EARLY + WARM_COLUMNS],
+                rhs=wu_raw[0][:].bitcast(FP8X4),
                 rhs_scale=stage0[:, EARLY : EARLY + R],
                 start=True,
                 stop=True,
             )
         wu_sc = planes0[:, :, EARLY : EARLY + R]
         wd_sc = planes0[:, :, EARLY + R :]
-
 
         def v_sc(a, j0, width):
             planes, first = (planes0, 0) if j0 < EARLY else (planes1, EARLY)
@@ -125,8 +136,8 @@ def tile_list_modp_gelu_res_noneb_kernel(
         def h_codes(j0, width):
             return (h_first[:, j0 : j0 + width] if j0 < CHUNK else h_rest[:, j0 - CHUNK : j0 - CHUNK + width]).bitcast(FP8X4)
 
-        def gather(c, picked, chunks=1):
-            nc.vector.tensor_copy(picked, tab[:].indirect(offsets[:, c * CHUNK // 16 : (c + chunks) * CHUNK // 16]))
+        def gather(picked, j0, width):
+            nc.vector.tensor_copy(picked, tab[:].indirect(offsets[:, j0 // 16 : (j0 + width) // 16]))
 
         def part(v, picked):
             nc.vector.tensor_copy(v.bitcast(U16), picked.bitcast(U16).rearrange("p (j a) -> p a j", a=PASSES))
@@ -138,9 +149,9 @@ def tile_list_modp_gelu_res_noneb_kernel(
                 for t in range(PACK):
                     nc.tensor.matmul_mx(
                         out=bank[:, t, :],
-                        lhsT=wu[a][:, t * P : (t + 1) * P].bitcast(FP8X4),
+                        lhsT=wu[a][t // 2][:, t % 2 * P : (t % 2 + 1) * P].bitcast(FP8X4),
                         lhsT_scale=wu_sc[:, a, t * P : (t + 1) * P],
-                        rhs=v[:, a, 2 * half * HALF : 2 * (half + 1) * HALF].bitcast(FP4X4),
+                        rhs=v[:, a, :].bitcast(FP4X4),
                         rhs_scale=v_sc(a, j0, HALF),
                         start=(a == 0 and t == 0),
                         stop=(a == PASSES - 1 and t == PACK - 1),
@@ -165,7 +176,7 @@ def tile_list_modp_gelu_res_noneb_kernel(
             return (20 * c - 8) * CHUNK
 
         def gelu(c, half, g):
-            nc.scalar.activation(g[:, :, half * HALF : (half + 1) * HALF], up(c, half, picks[c])[:], ACT.Gelu_apprx_tanh)
+            nc.scalar.activation(g[:, :, half * HALF : (half + 1) * HALF], up(c, half, picks[c][:, :, 2 * half * HALF : 2 * (half + 1) * HALF])[:], ACT.Gelu_apprx_tanh)
 
         def scale(c, g):
             planes = hidden.tile([P, PACK * CHUNK], BF16, name="planes%d" % c, offset=at_planes(c), align_bytes=64)
@@ -218,8 +229,7 @@ def tile_list_modp_gelu_res_noneb_kernel(
 
         pages.append(placed.tile([P, T], F32, name="page1", offset=2 * page_bytes, align_bytes=64))
         nc.gpsimd.memset(pages[1][:].bitcast(I32), 0)
-        picked_sc1 = placed.tile([P, J - EARLY], U8, name="picked_sc1", offset=at_sc, align_bytes=64)
-        nc.vector.tensor_copy(picked_sc1[:], tab_sc[:].indirect(offsets[:, EARLY // 16 : J // 16]))
+        spread(nc.sync, planes1, picked_sc1)
         wd = late.tile([P, 6 * N], U8, name="wd", offset=4 * J + 64, align_bytes=64)
         wd8 = wd[:, 0 : 4 * N]
         wd4 = wd[:, 4 * N : 6 * N]
@@ -230,17 +240,21 @@ def tile_list_modp_gelu_res_noneb_kernel(
             nc.sync.dma_start(b_t[:], b.rearrange("(c p) -> p c", p=P))
         weight = late.tile([P, J], F32, name="weight", offset=0, align_bytes=64)
         nc.sync.dma_start(weight[:], wgo)
-        spread((nc.sync, nc.sync), planes1, picked_sc1)
 
-        picks = [sbuf([P, PASSES, 2 * CHUNK], U8, "v%d" % c) for c in range(2)]
-        picked0 = placed.tile([P, CHUNK], U32, name="picked0", offset=beyond + 4 * R, align_bytes=64)
-        gather(0, picked0[:])
-        reorder(nc.vector.tensor_copy, 1, wu_raw1)
-        for half in range(CHUNK // HALF):
-            part(picks[0][:, :, 2 * half * HALF : 2 * (half + 1) * HALF], picked0[:, half * HALF : (half + 1) * HALF])
-        picked12 = placed.tile([P, 2 * CHUNK], U32, name="picked12", offset=beyond + 4 * R - 4 * CHUNK, align_bytes=64)
-        gather(1, picked12[:, 0:CHUNK])
-        gather(2, picked12[:, CHUNK:])
+        at_words = 3 * page_bytes
+        halves = [sbuf([P, PASSES, 2 * HALF], U8, "v0_%d" % half) for half in range(2)]
+        picked0 = [
+            placed.tile([P, HALF], U32, name="picked0_%d" % half, offset=at_words + 4 * HALF * (half + 4), align_bytes=64)
+            for half in range(2)
+        ]
+        for half in range(2):
+            gather(picked0[half][:], half * HALF, HALF)
+        for half in range(2):
+            part(halves[half][:], picked0[half][:])
+        picked12 = placed.tile([P, 2 * CHUNK], U32, name="picked12", offset=at_words + 4 * HALF, align_bytes=64)
+        picks = [None, sbuf([P, PASSES, 2 * CHUNK], U8, "v1")]
+        gather(picked12[:, 0:CHUNK], CHUNK, CHUNK)
+        gather(picked12[:, CHUNK:], 2 * CHUNK, CHUNK)
         part(picks[1][:], picked12[:, 0:CHUNK])
         seam = page_bytes - HALF * PACK
         wovens = [
@@ -248,12 +262,12 @@ def tile_list_modp_gelu_res_noneb_kernel(
             sbuf([P, HALF * PACK], BF16, "woven0_1"),
         ]
         for half in range(CHUNK // HALF):
-            first_half(half, picks[0], wovens[half])
+            first_half(half, halves[half][:], wovens[half])
         for half in range(CHUNK // HALF):
             cols = slice(half * HALF, (half + 1) * HALF)
             nc.vector.quantize_mx(out=h_codes(half * HALF, HALF), scales=h_sc[:, cols], in_=wovens[half][:])
         picked3 = placed.tile([P, CHUNK], U32, name="picked3", offset=seam, align_bytes=64)
-        gather(3, picked3[:])
+        gather(picked3[:], 3 * CHUNK, CHUNK)
         picks.append(sbuf([P, PASSES, 2 * CHUNK], U8, "v2", "g0_1"))
         part(picks[2][:], picked12[:, CHUNK:])
         picks.append(sbuf([P, PASSES, 2 * CHUNK], U8, "v3"))

@@ -20,13 +20,13 @@ P = 128
 PACK = 4
 PASSES = K // (P * PACK)
 CHUNK = 256
-CHUNKS = J // CHUNK
 HALF = 128
 BLOCKS = N // P
 ROWS0 = 96
-EARLY = CHUNK
 WARM_PASSES = 5
 WARM_COLUMNS = 32
+PAGE_BYTES = 4 * T
+LAP = 64
 
 
 def tile_list_modp_gelu_res_noneb_kernel(
@@ -35,30 +35,30 @@ def tile_list_modp_gelu_res_noneb_kernel(
     nc = tc.nc
     with ExitStack() as ctx:
         lists = ctx.enter_context(tc.tile_pool(name="lists", bufs=1))
-        pool = ctx.enter_context(tc.tile_pool(name="pool", bufs=1))
-        placed = ctx.enter_context(tc.tile_pool(name="placed", bufs=1))
-        hidden = ctx.enter_context(tc.tile_pool(name="hidden", bufs=1))
+        free = ctx.enter_context(tc.tile_pool(name="free", bufs=1))
         psum = ctx.enter_context(tc.psum_pool(name="psum", bufs=1))
+        arenas = {name: ctx.enter_context(tc.tile_pool(name=name, bufs=1)) for name in ("late", "early", "paged", "words", "hidden")}
 
         def sbuf(shape, dtype, name, tag=None):
-            return pool.tile(shape, dtype, name=name, tag=tag or name, align_bytes=64)
+            return free.tile(shape, dtype, name=name, tag=tag or name, align_bytes=64)
+
+        def placed(arena, at, shape, dtype, name):
+            return arenas[arena].tile(shape, dtype, name=name, offset=at, align_bytes=64)
+
+        def entries(j0, width):
+            return offsets[:, j0 // 16 : (j0 + width) // 16]
 
         offsets = lists.tile([P, J // 16], U16, name="offsets")
         nc.sync.dma_start(offsets[:], offs)
-
-        late = ctx.enter_context(tc.tile_pool(name="late", bufs=1))
-        tab_sc = late.tile([P, T], U8, name="tab_sc", offset=4 * J - 64, align_bytes=64)
+        tab_sc = placed("late", 4 * J - LAP, [P, T], U8, "tab_sc")
         nc.sync.dma_start(tab_sc[ROWS0:P, :].bitcast(I32), tab_scales.rearrange("a q t -> q a t").bitcast(I32))
-        early = ctx.enter_context(tc.tile_pool(name="early", bufs=1))
-        wu_sc_raw = early.tile([P, R], U8, name="wu_sc_raw", offset=0, align_bytes=64)
+        wu_sc_raw = placed("early", 0, [P, R], U8, "wu_sc_raw")
         nc.sync.dma_start(wu_sc_raw[ROWS0:P, :].bitcast(I32), wu_scales.rearrange("a q r -> q a r").bitcast(I32))
-        stage0 = sbuf([P, EARLY + R + N], U8, "stage0")
-        nc.scalar.dma_start(stage0[ROWS0:P:2, EARLY + R :].bitcast(I32), wd4_scales[0].bitcast(I32))
-        nc.scalar.dma_start(stage0[ROWS0 + 1 : P : 2, EARLY + R :].bitcast(I32), wd8_scales[0].bitcast(I32))
+        stage = sbuf([P, CHUNK + R + N], U8, "stage")
+        nc.scalar.dma_start(stage[ROWS0:P:2, CHUNK + R :].bitcast(I32), wd4_scales[0].bitcast(I32))
+        nc.scalar.dma_start(stage[ROWS0 + 1 : P : 2, CHUNK + R :].bitcast(I32), wd8_scales[0].bitcast(I32))
         sm_t = sbuf([P, PACK], F32, "sm_t")
         nc.scalar.dma_start(sm_t[:], sm.rearrange("(p t) -> p t", t=PACK))
-        sm_t = sm_t[:]
-        page_bytes = 4 * T
         wu_raw = [sbuf([P, R], U32, "wu_raw%d" % a) for a in range(PASSES)]
         nc.sync.dma_start(wu_raw[0][:].bitcast(I32), wu_words[0].rearrange("p r i -> p (r i)").bitcast(I32))
         tab = sbuf([P, T], U32, "tab")
@@ -76,32 +76,38 @@ def tile_list_modp_gelu_res_noneb_kernel(
 
         clear_beside_gpsimd(tab_sc[0:ROWS0, :].bitcast(I32))
         clear_beside_gpsimd(wu_sc_raw[0:ROWS0, :].bitcast(I32))
-        planes0 = sbuf([P, 2, EARLY + R + N], U8, "sc_planes0")
-        clear_beside_gpsimd(planes0[:].rearrange("p a n -> p (a n)").bitcast(I32))
+        planes_first = sbuf([P, 2, CHUNK + R + N], U8, "planes_first")
+        clear_beside_gpsimd(planes_first[:].rearrange("p a n -> p (a n)").bitcast(I32))
         pages = [sbuf([P, T], F32, "page0")]
         nc.gpsimd.memset(pages[0][:].bitcast(I32), 0)
-        planes1 = sbuf([P, 2, J - EARLY], U8, "sc_planes1")
-        nc.gpsimd.memset(planes1[:].bitcast(I32), 0)
-
-        def spread(queue, planes, stage):
-            for q in (0, 2, 1, 3):
-                queue.dma_start(
-                    planes[32 * q : 32 * q + 4, :, :].bitcast(I32), stage[ROWS0 + 8 * q : ROWS0 + 8 * q + 8, :].bitcast(I32)
-                )
+        planes_rest = sbuf([P, 2, J - CHUNK], U8, "planes_rest")
+        nc.gpsimd.memset(planes_rest[:].bitcast(I32), 0)
 
         def gather_scales(picked, j0, width):
-            nc.vector.tensor_copy(picked, tab_sc[:].indirect(offsets[:, j0 // 16 : (j0 + width) // 16]))
+            nc.vector.tensor_copy(picked, tab_sc[:].indirect(entries(j0, width)))
 
-        picked_sc0 = placed.tile([P, EARLY], U8, name="picked_sc0", offset=2 * page_bytes, align_bytes=64)
-        picked_sc1 = early.tile([P, J - EARLY], U8, name="picked_sc1", offset=0, align_bytes=64)
-        gather_scales(picked_sc0[:], 0, EARLY)
+        def spread(queue, planes, rows):
+            for q in (0, 2, 1, 3):
+                queue.dma_start(
+                    planes[32 * q : 32 * q + 4, :, :].bitcast(I32), rows[ROWS0 + 8 * q : ROWS0 + 8 * q + 8, :].bitcast(I32)
+                )
+
+        picked_sc_first = placed("paged", PAGE_BYTES, [P, CHUNK], U8, "picked_sc_first")
+        gather_scales(picked_sc_first[:], 0, CHUNK)
         nc.vector.tensor_copy(
-            stage0[:, EARLY : EARLY + R].rearrange("p (t c i) -> p c t i", t=PACK, i=16),
+            stage[:, CHUNK : CHUNK + R].rearrange("p (t c i) -> p c t i", t=PACK, i=16),
             wu_sc_raw[:].rearrange("p (c i t) -> p c t i", t=PACK, i=16),
         )
-        nc.vector.tensor_copy(stage0[:, 0:EARLY].bitcast(I32), picked_sc0[:].bitcast(I32))
-        spread(nc.scalar, planes0, stage0)
-        gather_scales(picked_sc1[:], EARLY, J - EARLY)
+        nc.vector.tensor_copy(stage[:, 0:CHUNK].bitcast(I32), picked_sc_first[:].bitcast(I32))
+        spread(nc.scalar, planes_first, stage)
+        picked_sc_rest = placed("early", 0, [P, J - CHUNK], U8, "picked_sc_rest")
+        gather_scales(picked_sc_rest[:], CHUNK, J - CHUNK)
+        wu_sc = planes_first[:, :, CHUNK : CHUNK + R]
+        wd_sc = planes_first[:, :, CHUNK + R :]
+
+        def v_sc(a, j0, width):
+            planes, first = (planes_first, 0) if j0 < CHUNK else (planes_rest, CHUNK)
+            return planes[:, a, j0 - first : j0 - first + width]
 
         wu = [[sbuf([P, 2 * P], U32, "wu%d_%d" % (a, u)) for u in range(2)] for a in range(PASSES)]
         for a in range(PASSES):
@@ -116,35 +122,36 @@ def tile_list_modp_gelu_res_noneb_kernel(
             nc.tensor.matmul_mx(
                 out=idle[0:WARM_COLUMNS, :],
                 lhsT=wu_raw[0][:, 0:WARM_COLUMNS].bitcast(FP8X4),
-                lhsT_scale=stage0[:, EARLY : EARLY + WARM_COLUMNS],
+                lhsT_scale=stage[:, CHUNK : CHUNK + WARM_COLUMNS],
                 rhs=wu_raw[0][:].bitcast(FP8X4),
-                rhs_scale=stage0[:, EARLY : EARLY + R],
+                rhs_scale=stage[:, CHUNK : CHUNK + R],
                 start=True,
                 stop=True,
             )
-        wu_sc = planes0[:, :, EARLY : EARLY + R]
-        wd_sc = planes0[:, :, EARLY + R :]
 
-        def v_sc(a, j0, width):
-            planes, first = (planes0, 0) if j0 < EARLY else (planes1, EARLY)
-            return planes[:, a, j0 - first : j0 - first + width]
+        pages.append(placed("paged", PAGE_BYTES, [P, T], F32, "page1"))
+        nc.gpsimd.memset(pages[1][:].bitcast(I32), 0)
 
-        h_first = hidden.tile([P, CHUNK], U32, name="h_first", offset=12 * CHUNK, align_bytes=64)
-        h_rest = sbuf([P, J - CHUNK], U32, "h_rest")
-        h_sc = sbuf([P, J], U8, "h_sc")
-
-        def h_codes(j0, width):
-            return (h_first[:, j0 : j0 + width] if j0 < CHUNK else h_rest[:, j0 - CHUNK : j0 - CHUNK + width]).bitcast(FP8X4)
+        spread(nc.sync, planes_rest, picked_sc_rest)
+        wd = placed("late", 4 * J + LAP, [P, 6 * N], U8, "wd")
+        wd8 = wd[:, 0 : 4 * N]
+        wd4 = wd[:, 4 * N : 6 * N]
+        nc.sync.dma_start(wd8.bitcast(I32), wd8_words[0].rearrange("p n i -> p (n i)").bitcast(I32))
+        nc.sync.dma_start(wd4.bitcast(I32), wd4_words[0].bitcast(I32))
+        b_t = placed("late", 4 * J, [P, BLOCKS], F32, "b_t")
+        with nc.allow_non_contiguous_dma(reason="one bias value a partition and block"):
+            nc.sync.dma_start(b_t[:], b.rearrange("(c p) -> p c", p=P))
+        weight = placed("late", 0, [P, J], F32, "weight")
+        nc.sync.dma_start(weight[:], wgo)
 
         def gather(picked, j0, width):
-            nc.vector.tensor_copy(picked, tab[:].indirect(offsets[:, j0 // 16 : (j0 + width) // 16]))
+            nc.vector.tensor_copy(picked, tab[:].indirect(entries(j0, width)))
 
         def part(v, picked):
             nc.vector.tensor_copy(v.bitcast(U16), picked.bitcast(U16).rearrange("p (j a) -> p a j", a=PASSES))
 
-        def up(c, half, v):
-            bank = psum.tile([P, PACK, HALF], F32, name="a_bank", tag="a_bank", bufs=4)
-            j0 = c * CHUNK + half * HALF
+        def up(v, j0):
+            bank = psum.tile([P, PACK, HALF], F32, name="a_bank", tag="a_bank", bufs=3)
             for a in range(PASSES):
                 for t in range(PACK):
                     nc.tensor.matmul_mx(
@@ -158,46 +165,51 @@ def tile_list_modp_gelu_res_noneb_kernel(
                     )
             return bank
 
-        def quantise(c, woven):
-            cols = slice(c * CHUNK, (c + 1) * CHUNK)
-            nc.vector.quantize_mx(out=h_codes(c * CHUNK, CHUNK), scales=h_sc[:, cols], in_=woven[:])
+        slices_bytes = 2 * PACK * CHUNK
+        g_bytes = 4 * PACK * CHUNK
 
-        def first_half(half, v, woven):
-            g = sbuf([P, HALF, PACK], F32, "g0_%d" % half)
-            nc.scalar.activation(g[:], up(0, half, v)[:].rearrange("p t j -> p j t"), ACT.Gelu_apprx_tanh)
-            nc.vector.tensor_tensor(
-                woven[:].rearrange("p (j t) -> p j t", t=PACK),
-                g[:],
-                sm_t.unsqueeze(1).to_broadcast([P, HALF, PACK]),
-                MULT,
-            )
+        def at_slices(c):
+            return g_bytes + (c - 1) * (slices_bytes + 2 * g_bytes)
 
-        def at_planes(c):
-            return (20 * c - 8) * CHUNK
+        h_first = placed("hidden", at_slices(1), [P, CHUNK], U32, "h_first")
+        h_rest = sbuf([P, J - CHUNK], U32, "h_rest")
+        h_sc = sbuf([P, J], U8, "h_sc")
 
-        def gelu(c, half, g):
-            nc.scalar.activation(g[:, :, half * HALF : (half + 1) * HALF], up(c, half, picks[c][:, :, 2 * half * HALF : 2 * (half + 1) * HALF])[:], ACT.Gelu_apprx_tanh)
+        def h_codes(j0, width):
+            return (h_first[:, j0 : j0 + width] if j0 < CHUNK else h_rest[:, j0 - CHUNK : j0 - CHUNK + width]).bitcast(FP8X4)
 
-        def scale(c, g):
-            planes = hidden.tile([P, PACK * CHUNK], BF16, name="planes%d" % c, offset=at_planes(c), align_bytes=64)
-            for t in range(PACK):
-                nc.scalar.activation(planes[:, t * CHUNK : (t + 1) * CHUNK], g[:, t, :], ACT.Copy, scale=sm_t[:, t : t + 1])
-            return planes
+        def quantise(woven, j0, width):
+            nc.vector.quantize_mx(out=h_codes(j0, width), scales=h_sc[:, j0 : j0 + width], in_=woven)
 
-        def weave(c, planes):
+        def gelu(c, g, v):
+            for half in range(2):
+                bank = up(v[:, :, 2 * half * HALF : 2 * (half + 1) * HALF], c * CHUNK + half * HALF)
+                nc.scalar.activation(g[:, :, half * HALF : (half + 1) * HALF], bank[:], ACT.Gelu_apprx_tanh)
+
+        def smooth(slices, g, steps=range(PACK)):
+            for t in steps:
+                nc.scalar.activation(slices[:, t * CHUNK : (t + 1) * CHUNK], g[:, t, :], ACT.Copy, scale=sm_t[:, t : t + 1])
+            return slices
+
+        def slices_of(c):
+            return placed("hidden", at_slices(c), [P, PACK * CHUNK], BF16, "slices%d" % c)
+
+        def weave(c, slices):
             woven = sbuf([P, CHUNK * PACK], BF16, "woven%d" % c)
             nc.scalar.copy(
                 woven[:].rearrange("p (c i t) -> p c t i", t=PACK, i=4),
-                planes[:].rearrange("p (t c i) -> p c t i", t=PACK, i=4),
+                slices[:].rearrange("p (t c i) -> p c t i", t=PACK, i=4),
             )
-            quantise(c, woven)
+            quantise(woven[:], c * CHUNK, CHUNK)
 
-        def behind_weave(c, half, shape, name):
-            size = 4 * CHUNK * (PACK if len(shape) == 3 else 1)
-            return hidden.tile(shape, F32, name=name, offset=at_planes(c) + 4 * CHUNK - (0 if half else size), align_bytes=64)
+        def next_g(c):
+            return placed("hidden", at_slices(c) + LAP - g_bytes, [P, PACK, CHUNK], F32, "g%d" % (c + 1))
 
-        def down(block, j0, width):
-            bank = psum.tile([P, width], F32, name="y_bank", tag="y_bank", bufs=4)
+        def cover_y(c):
+            return placed("hidden", at_slices(c) + LAP, [P, CHUNK], F32, "y_cover%d" % c)
+
+        def down(block, j0, width, tag="y_bank", bufs=4):
+            bank = psum.tile([P, width], F32, name=tag, tag=tag, bufs=bufs)
             cols = slice(block * P, (block + 1) * P)
             nc.tensor.matmul_mx(
                 out=bank[:],
@@ -222,105 +234,81 @@ def tile_list_modp_gelu_res_noneb_kernel(
         def add_bias(y, bank, block):
             nc.scalar.activation(y, bank[:], ACT.Identity, bias=b_t[:, block : block + 1])
 
-        def scatter(page, y, j0, width):
-            nc.vector.tensor_tensor(
-                page[:].indirect(offsets[:, j0 // 16 : (j0 + width) // 16]), y, weight[:, j0 : j0 + width], MULT
-            )
+        def scatter(block, y, j0, width):
+            page = pages[block % len(pages)]
+            nc.vector.tensor_tensor(page[:].indirect(entries(j0, width)), y, weight[:, j0 : j0 + width], MULT)
+            if j0 + width == J:
+                nc.sync.dma_start(out[block * P : (block + 1) * P, :], page[:])
 
-        pages.append(placed.tile([P, T], F32, name="page1", offset=2 * page_bytes, align_bytes=64))
-        nc.gpsimd.memset(pages[1][:].bitcast(I32), 0)
-        spread(nc.sync, planes1, picked_sc1)
-        wd = late.tile([P, 6 * N], U8, name="wd", offset=4 * J + 64, align_bytes=64)
-        wd8 = wd[:, 0 : 4 * N]
-        wd4 = wd[:, 4 * N : 6 * N]
-        nc.sync.dma_start(wd8.bitcast(I32), wd8_words[0].rearrange("p n i -> p (n i)").bitcast(I32))
-        nc.sync.dma_start(wd4.bitcast(I32), wd4_words[0].bitcast(I32))
-        b_t = late.tile([P, BLOCKS], F32, name="b_t", offset=4 * J, align_bytes=64)
-        with nc.allow_non_contiguous_dma(reason="one bias value a partition and block"):
-            nc.sync.dma_start(b_t[:], b.rearrange("(c p) -> p c", p=P))
-        weight = late.tile([P, J], F32, name="weight", offset=0, align_bytes=64)
-        nc.sync.dma_start(weight[:], wgo)
+        def place(block, y, j0, width=CHUNK, bank=None):
+            add_bias(y, down(block, j0, width) if bank is None else bank, block)
+            scatter(block, y, j0, width)
 
-        at_words = 3 * page_bytes
         halves = [sbuf([P, PASSES, 2 * HALF], U8, "v0_%d" % half) for half in range(2)]
-        picked0 = [
-            placed.tile([P, HALF], U32, name="picked0_%d" % half, offset=at_words + 4 * HALF * (half + 4), align_bytes=64)
-            for half in range(2)
-        ]
+        picked0 = [placed("words", 4 * HALF * (half + 3), [P, HALF], U32, "picked0_%d" % half) for half in range(2)]
         for half in range(2):
             gather(picked0[half][:], half * HALF, HALF)
         for half in range(2):
             part(halves[half][:], picked0[half][:])
-        picked12 = placed.tile([P, 2 * CHUNK], U32, name="picked12", offset=at_words + 4 * HALF, align_bytes=64)
-        picks = [None, sbuf([P, PASSES, 2 * CHUNK], U8, "v1")]
+        picked12 = placed("words", 0, [P, 2 * CHUNK], U32, "picked12")
+        v1 = sbuf([P, PASSES, 2 * CHUNK], U8, "v1")
         gather(picked12[:, 0:CHUNK], CHUNK, CHUNK)
         gather(picked12[:, CHUNK:], 2 * CHUNK, CHUNK)
-        part(picks[1][:], picked12[:, 0:CHUNK])
-        seam = page_bytes - HALF * PACK
-        wovens = [
-            placed.tile([P, HALF * PACK], BF16, name="woven0_0", offset=seam, align_bytes=64),
-            sbuf([P, HALF * PACK], BF16, "woven0_1"),
-        ]
-        for half in range(CHUNK // HALF):
-            first_half(half, halves[half][:], wovens[half])
-        for half in range(CHUNK // HALF):
-            cols = slice(half * HALF, (half + 1) * HALF)
-            nc.vector.quantize_mx(out=h_codes(half * HALF, HALF), scales=h_sc[:, cols], in_=wovens[half][:])
-        picked3 = placed.tile([P, CHUNK], U32, name="picked3", offset=seam, align_bytes=64)
+        part(v1[:], picked12[:, 0:CHUNK])
+
+        wovens = [placed("paged", 0, [P, HALF * PACK], BF16, "woven0_0"), sbuf([P, HALF * PACK], BF16, "woven0_1")]
+        for half in range(2):
+            g = sbuf([P, HALF, PACK], F32, "g0_%d" % half)
+            nc.scalar.activation(g[:], up(halves[half][:], half * HALF)[:].rearrange("p t j -> p j t"), ACT.Gelu_apprx_tanh)
+            nc.vector.tensor_tensor(
+                wovens[half][:].rearrange("p (j t) -> p j t", t=PACK),
+                g[:],
+                sm_t[:].unsqueeze(1).to_broadcast([P, HALF, PACK]),
+                MULT,
+            )
+        for half in range(2):
+            quantise(wovens[half][:], half * HALF, HALF)
+        picked3 = placed("paged", 0, [P, CHUNK], U32, "picked3")
         gather(picked3[:], 3 * CHUNK, CHUNK)
-        picks.append(sbuf([P, PASSES, 2 * CHUNK], U8, "v2", "g0_1"))
-        part(picks[2][:], picked12[:, CHUNK:])
-        picks.append(sbuf([P, PASSES, 2 * CHUNK], U8, "v3"))
-        part(picks[3][:], picked3[:])
-        for i in range(2):
-            pages.append(placed.tile([P, T], F32, name="page%d" % (2 + i), offset=page_bytes * i, align_bytes=64))
-            nc.gpsimd.memset(pages[2 + i][:].bitcast(I32), 0)
+        v2 = sbuf([P, PASSES, 2 * CHUNK], U8, "v2", "g0_1")
+        part(v2[:], picked12[:, CHUNK:])
+        v3 = sbuf([P, PASSES, 2 * CHUNK], U8, "v3")
+        part(v3[:], picked3[:])
+        pages.append(placed("paged", 0, [P, T], F32, "page2"))
+        nc.gpsimd.memset(pages[2][:].bitcast(I32), 0)
 
-        def biased(c, block, y=None, bank=None):
-            if y is None:
-                y = sbuf([P, CHUNK], F32, "y%d_%d" % (c, block))[:]
-            add_bias(y, down(block, c * CHUNK, CHUNK) if bank is None else bank, block)
-            return y
-
-        def place(c, block, y, chunks=1):
-            scatter(pages[block], y, c * CHUNK, chunks * CHUNK)
-            if c + chunks == CHUNKS:
-                nc.sync.dma_start(out[block * P : (block + 1) * P, :], pages[block][:])
-
-        g = sbuf([P, PACK, CHUNK], F32, "g1", "g")
-        gelu(1, 0, g)
-        gelu(1, 1, g)
+        g = sbuf([P, PACK, CHUNK], F32, "g1")
+        gelu(1, g, v1)
         y = sbuf([P, CHUNK], F32, "y_first")
-        for half in range(CHUNK // HALF):
+        for half in range(2):
             add_bias(y[:, half * HALF : (half + 1) * HALF], down(0, half * HALF, HALF), 0)
-        place(0, 0, y[:])
-        banks = [down(block, 0, CHUNK) for block in range(1, BLOCKS)]
-        place(0, 1, biased(0, 1, bank=banks[0]))
-        planes = scale(1, g)
-        place(0, 2, biased(0, 2, bank=banks[1]))
-        weave(1, planes)
-        place(0, 3, biased(0, 3, behind_weave(1, 1, [P, CHUNK], "y0_3")[:], banks[2]))
+        scatter(0, y[:], 0, CHUNK)
+        banks = [down(1, 0, CHUNK), down(2, 0, CHUNK)]
+        kept = down(3, 0, CHUNK, "kept_bank", 1)
+        place(1, sbuf([P, CHUNK], F32, "y0_1")[:], 0, bank=banks[0])
+        weave(1, smooth(slices_of(1), g))
+        place(2, cover_y(1)[:], 0, bank=banks[1])
 
-        g = behind_weave(1, 0, [P, PACK, CHUNK], "g2")
-        gelu(2, 0, g)
-        gelu(2, 1, g)
-        planes = scale(2, g)
-        spent = g
-        place(1, 0, biased(1, 0, spent[:, 0, :]))
-        weave(2, planes)
-        place(1, 1, biased(1, 1, spent[:, 1, :]))
-        place(1, 2, biased(1, 2, spent[:, 2, :]))
+        g = next_g(1)
+        gelu(2, g, v2)
+        place(0, sbuf([P, CHUNK], F32, "y1_0")[:], CHUNK)
+        slices = smooth(slices_of(2), g)
+        place(1, g[:, 1, :], CHUNK)
+        weave(2, slices)
+        place(2, cover_y(2)[:], CHUNK)
 
-        g = behind_weave(2, 0, [P, PACK, CHUNK], "g3")
-        gelu(3, 0, g)
-        gelu(3, 1, g)
-        place(1, 3, biased(1, 3, spent[:, 3, :]))
-        weave(3, scale(3, g))
+        g = next_g(2)
+        gelu(3, g, v3)
+        slices = smooth(slices_of(3), g, range(2))
+        place(0, g[:, 0, :], 2 * CHUNK)
+        weave(3, smooth(slices, g, range(2, PACK)))
+        place(1, cover_y(3)[:], 2 * CHUNK)
         for block in range(2):
-            place(2, block, biased(2, block, behind_weave(3, block, [P, CHUNK], "y2_%d" % block)[:]))
-        for block in range(2):
-            place(3, block, biased(3, block))
-        for block in range(2, BLOCKS):
-            y = sbuf([P, 2 * CHUNK], F32, "y_last%d" % block)
-            add_bias(y[:], down(block, 2 * CHUNK, 2 * CHUNK), block)
-            place(2, block, y[:], chunks=2)
+            place(block, g[:, 1 + block, :], 3 * CHUNK)
+        place(2, sbuf([P, 2 * CHUNK], F32, "y_wide")[:], 2 * CHUNK, 2 * CHUNK)
+
+        y = placed("hidden", at_slices(2) + slices_bytes - LAP, [P, J], F32, "y_last")
+        add_bias(y[:, 0:CHUNK], kept, 3)
+        add_bias(y[:, CHUNK : 2 * CHUNK], down(3, CHUNK, CHUNK), 3)
+        add_bias(y[:, 2 * CHUNK :], down(3, 2 * CHUNK, 2 * CHUNK), 3)
+        scatter(3, y[:], 0, J)

@@ -92,7 +92,7 @@ def tile_list_modp_gelu_res_noneb_kernel(
                     planes[32 * q : 32 * q + 4, :, :].bitcast(I32), rows[ROWS0 + 8 * q : ROWS0 + 8 * q + 8, :].bitcast(I32)
                 )
 
-        picked_sc_first = placed("paged", PAGE_BYTES, [P, CHUNK], U8, "picked_sc_first")
+        picked_sc_first = placed("paged", 2 * PAGE_BYTES, [P, CHUNK], U8, "picked_sc_first")
         gather_scales(picked_sc_first[:], 0, CHUNK)
         nc.vector.tensor_copy(
             stage[:, CHUNK : CHUNK + R].rearrange("p (t c i) -> p c t i", t=PACK, i=16),
@@ -129,7 +129,7 @@ def tile_list_modp_gelu_res_noneb_kernel(
                 stop=True,
             )
 
-        pages.append(placed("paged", PAGE_BYTES, [P, T], F32, "page1"))
+        pages.append(placed("paged", 2 * PAGE_BYTES, [P, T], F32, "page1"))
         nc.gpsimd.memset(pages[1][:].bitcast(I32), 0)
 
         spread(nc.sync, planes_rest, picked_sc_rest)
@@ -151,7 +151,7 @@ def tile_list_modp_gelu_res_noneb_kernel(
             nc.vector.tensor_copy(v.bitcast(U16), picked.bitcast(U16).rearrange("p (j a) -> p a j", a=PASSES))
 
         def up(v, j0):
-            bank = psum.tile([P, PACK, HALF], F32, name="a_bank", tag="a_bank", bufs=3)
+            bank = psum.tile([P, PACK, HALF], F32, name="a_bank", tag="a_bank", bufs=4)
             for a in range(PASSES):
                 for t in range(PACK):
                     nc.tensor.matmul_mx(
@@ -205,11 +205,11 @@ def tile_list_modp_gelu_res_noneb_kernel(
         def next_g(c):
             return placed("hidden", at_slices(c) + LAP - g_bytes, [P, PACK, CHUNK], F32, "g%d" % (c + 1))
 
-        def cover_y(c):
-            return placed("hidden", at_slices(c) + LAP, [P, CHUNK], F32, "y_cover%d" % c)
+        def cover_y(c, i):
+            return placed("hidden", at_slices(c) + LAP + 4 * CHUNK * i, [P, CHUNK], F32, "y_cover%d_%d" % (c, i))
 
-        def down(block, j0, width, tag="y_bank", bufs=4):
-            bank = psum.tile([P, width], F32, name=tag, tag=tag, bufs=bufs)
+        def down(block, j0, width):
+            bank = psum.tile([P, width], F32, name="y_bank", tag="y_bank", bufs=4)
             cols = slice(block * P, (block + 1) * P)
             nc.tensor.matmul_mx(
                 out=bank[:],
@@ -235,7 +235,7 @@ def tile_list_modp_gelu_res_noneb_kernel(
             nc.scalar.activation(y, bank[:], ACT.Identity, bias=b_t[:, block : block + 1])
 
         def scatter(block, y, j0, width):
-            page = pages[block % len(pages)]
+            page = pages[block]
             nc.vector.tensor_tensor(page[:].indirect(entries(j0, width)), y, weight[:, j0 : j0 + width], MULT)
             if j0 + width == J:
                 nc.sync.dma_start(out[block * P : (block + 1) * P, :], page[:])
@@ -256,7 +256,8 @@ def tile_list_modp_gelu_res_noneb_kernel(
         gather(picked12[:, CHUNK:], 2 * CHUNK, CHUNK)
         part(v1[:], picked12[:, 0:CHUNK])
 
-        wovens = [placed("paged", 0, [P, HALF * PACK], BF16, "woven0_0"), sbuf([P, HALF * PACK], BF16, "woven0_1")]
+        seam = PAGE_BYTES - LAP
+        wovens = [placed("paged", seam, [P, HALF * PACK], BF16, "woven0_0"), sbuf([P, HALF * PACK], BF16, "woven0_1")]
         for half in range(2):
             g = sbuf([P, HALF, PACK], F32, "g0_%d" % half)
             nc.scalar.activation(g[:], up(halves[half][:], half * HALF)[:].rearrange("p t j -> p j t"), ACT.Gelu_apprx_tanh)
@@ -268,14 +269,15 @@ def tile_list_modp_gelu_res_noneb_kernel(
             )
         for half in range(2):
             quantise(wovens[half][:], half * HALF, HALF)
-        picked3 = placed("paged", 0, [P, CHUNK], U32, "picked3")
+        picked3 = placed("paged", seam, [P, CHUNK], U32, "picked3")
         gather(picked3[:], 3 * CHUNK, CHUNK)
         v2 = sbuf([P, PASSES, 2 * CHUNK], U8, "v2", "g0_1")
         part(v2[:], picked12[:, CHUNK:])
         v3 = sbuf([P, PASSES, 2 * CHUNK], U8, "v3")
         part(v3[:], picked3[:])
-        pages.append(placed("paged", 0, [P, T], F32, "page2"))
-        nc.gpsimd.memset(pages[2][:].bitcast(I32), 0)
+        for i in range(2):
+            pages.append(placed("paged", PAGE_BYTES * i, [P, T], F32, "page%d" % (2 + i)))
+            nc.gpsimd.memset(pages[2 + i][:].bitcast(I32), 0)
 
         g = sbuf([P, PACK, CHUNK], F32, "g1")
         gelu(1, g, v1)
@@ -283,32 +285,30 @@ def tile_list_modp_gelu_res_noneb_kernel(
         for half in range(2):
             add_bias(y[:, half * HALF : (half + 1) * HALF], down(0, half * HALF, HALF), 0)
         scatter(0, y[:], 0, CHUNK)
-        banks = [down(1, 0, CHUNK), down(2, 0, CHUNK)]
-        kept = down(3, 0, CHUNK, "kept_bank", 1)
-        place(1, sbuf([P, CHUNK], F32, "y0_1")[:], 0, bank=banks[0])
-        weave(1, smooth(slices_of(1), g))
-        place(2, cover_y(1)[:], 0, bank=banks[1])
+        sums = [down(block, 0, CHUNK) for block in range(1, BLOCKS)]
+        place(1, sbuf([P, CHUNK], F32, "y0_1")[:], 0, bank=sums[0])
+        slices = smooth(slices_of(1), g)
+        place(2, sbuf([P, CHUNK], F32, "y0_2")[:], 0, bank=sums[1])
+        weave(1, slices)
+        place(3, cover_y(1, 0)[:], 0, bank=sums[2])
 
         g = next_g(1)
         gelu(2, g, v2)
-        place(0, sbuf([P, CHUNK], F32, "y1_0")[:], CHUNK)
-        slices = smooth(slices_of(2), g)
-        place(1, g[:, 1, :], CHUNK)
+        slices = smooth(slices_of(2), g, range(2))
+        place(0, g[:, 0, :], CHUNK)
+        smooth(slices, g, range(2, PACK))
+        place(1, g[:, 3, :], CHUNK)
         weave(2, slices)
-        place(2, cover_y(2)[:], CHUNK)
+        place(2, cover_y(2, 0)[:], CHUNK)
 
         g = next_g(2)
         gelu(3, g, v3)
-        slices = smooth(slices_of(3), g, range(2))
-        place(0, g[:, 0, :], 2 * CHUNK)
-        weave(3, smooth(slices, g, range(2, PACK)))
-        place(1, cover_y(3)[:], 2 * CHUNK)
-        for block in range(2):
-            place(block, g[:, 1 + block, :], 3 * CHUNK)
-        place(2, sbuf([P, 2 * CHUNK], F32, "y_wide")[:], 2 * CHUNK, 2 * CHUNK)
-
-        y = placed("hidden", at_slices(2) + slices_bytes - LAP, [P, J], F32, "y_last")
-        add_bias(y[:, 0:CHUNK], kept, 3)
-        add_bias(y[:, CHUNK : 2 * CHUNK], down(3, CHUNK, CHUNK), 3)
-        add_bias(y[:, 2 * CHUNK :], down(3, 2 * CHUNK, 2 * CHUNK), 3)
-        scatter(3, y[:], 0, J)
+        place(3, cover_y(2, 1)[:], CHUNK)
+        slices = smooth(slices_of(3), g)
+        place(0, g[:, 3, :], 2 * CHUNK)
+        weave(3, slices)
+        for block in (1, 2):
+            place(block, cover_y(3, block - 1)[:], 2 * CHUNK)
+        for block in range(3):
+            place(block, g[:, block, :], 3 * CHUNK)
+        place(3, sbuf([P, 2 * CHUNK], F32, "y_wide")[:], 2 * CHUNK, 2 * CHUNK)

@@ -23,8 +23,8 @@ CHUNK = 256
 HALF = 128
 BLOCKS = N // P
 ROWS0 = 96
-WARM_PASSES = 5
-WARM_COLUMNS = 32
+WARM_PASSES = 3
+WARM_COLUMNS = 128
 PAGE_BYTES = 4 * T
 LAP = 64
 
@@ -186,8 +186,8 @@ def tile_list_modp_gelu_res_noneb_kernel(
                 bank = up(v[:, :, 2 * half * HALF : 2 * (half + 1) * HALF], c * CHUNK + half * HALF)
                 nc.scalar.activation(g[:, :, half * HALF : (half + 1) * HALF], bank[:], ACT.Gelu_apprx_tanh)
 
-        def smooth(slices, g, steps=range(PACK)):
-            for t in steps:
+        def smooth(slices, g):
+            for t in range(PACK):
                 nc.scalar.activation(slices[:, t * CHUNK : (t + 1) * CHUNK], g[:, t, :], ACT.Copy, scale=sm_t[:, t : t + 1])
             return slices
 
@@ -294,21 +294,20 @@ def tile_list_modp_gelu_res_noneb_kernel(
 
         g = next_g(1)
         gelu(2, g, v2)
-        slices = smooth(slices_of(2), g, range(2))
-        place(0, g[:, 0, :], CHUNK)
-        smooth(slices, g, range(2, PACK))
-        place(1, g[:, 3, :], CHUNK)
+        slices = smooth(slices_of(2), g)
+        spent = g
+        place(0, spent[:, 0, :], CHUNK)
         weave(2, slices)
-        place(2, cover_y(2, 0)[:], CHUNK)
+        place(1, spent[:, 1, :], CHUNK)
+        place(2, spent[:, 2, :], CHUNK)
 
         g = next_g(2)
         gelu(3, g, v3)
-        place(3, cover_y(2, 1)[:], CHUNK)
-        slices = smooth(slices_of(3), g)
-        place(0, g[:, 3, :], 2 * CHUNK)
-        weave(3, slices)
-        for block in (1, 2):
-            place(block, cover_y(3, block - 1)[:], 2 * CHUNK)
-        for block in range(3):
+        place(3, spent[:, 3, :], CHUNK)
+        weave(3, smooth(slices_of(3), g))
+        for block in range(2):
+            place(block, cover_y(3, block)[:], 2 * CHUNK)
+        for block in range(2):
             place(block, g[:, block, :], 3 * CHUNK)
-        place(3, sbuf([P, 2 * CHUNK], F32, "y_wide")[:], 2 * CHUNK, 2 * CHUNK)
+        for block in range(2, BLOCKS):
+            place(block, sbuf([P, 2 * CHUNK], F32, "y_wide%d" % block)[:], 2 * CHUNK, 2 * CHUNK)

@@ -21,10 +21,11 @@ PACK = 4
 PASSES = K // (P * PACK)
 CHUNK = 256
 HALF = 128
+REST = J - 2 * CHUNK
 BLOCKS = N // P
 ROWS0 = 96
-WARM_PASSES = 3
-WARM_COLUMNS = 128
+WARM_PASSES = 6
+WARM_COLUMNS = 32
 PAGE_BYTES = 4 * T
 LAP = 64
 
@@ -50,13 +51,14 @@ def tile_list_modp_gelu_res_noneb_kernel(
 
         offsets = lists.tile([P, J // 16], U16, name="offsets")
         nc.sync.dma_start(offsets[:], offs)
-        tab_sc = placed("late", 4 * J - LAP, [P, T], U8, "tab_sc")
+        tab_sc = placed("late", 0, [P, T], U8, "tab_sc")
         nc.sync.dma_start(tab_sc[ROWS0:P, :].bitcast(I32), tab_scales.rearrange("a q t -> q a t").bitcast(I32))
-        wu_sc_raw = placed("early", 0, [P, R], U8, "wu_sc_raw")
+        wu_sc_raw = placed("early", 4 * J - LAP, [P, R], U8, "wu_sc_raw")
         nc.sync.dma_start(wu_sc_raw[ROWS0:P, :].bitcast(I32), wu_scales.rearrange("a q r -> q a r").bitcast(I32))
-        stage = sbuf([P, CHUNK + R + N], U8, "stage")
-        nc.scalar.dma_start(stage[ROWS0:P:2, CHUNK + R :].bitcast(I32), wd4_scales[0].bitcast(I32))
-        nc.scalar.dma_start(stage[ROWS0 + 1 : P : 2, CHUNK + R :].bitcast(I32), wd8_scales[0].bitcast(I32))
+        stage = sbuf([P, CHUNK + R], U8, "stage")
+        stage_next = sbuf([P, CHUNK + N], U8, "stage_next")
+        nc.scalar.dma_start(stage_next[ROWS0:P:2, CHUNK:].bitcast(I32), wd4_scales[0].bitcast(I32))
+        nc.scalar.dma_start(stage_next[ROWS0 + 1 : P : 2, CHUNK:].bitcast(I32), wd8_scales[0].bitcast(I32))
         sm_t = sbuf([P, PACK], F32, "sm_t")
         nc.scalar.dma_start(sm_t[:], sm.rearrange("(p t) -> p t", t=PACK))
         wu_raw = [sbuf([P, R], U32, "wu_raw%d" % a) for a in range(PASSES)]
@@ -76,12 +78,14 @@ def tile_list_modp_gelu_res_noneb_kernel(
 
         clear_beside_gpsimd(tab_sc[0:ROWS0, :].bitcast(I32))
         clear_beside_gpsimd(wu_sc_raw[0:ROWS0, :].bitcast(I32))
-        planes_first = sbuf([P, 2, CHUNK + R + N], U8, "planes_first")
+        planes_first = sbuf([P, 2, CHUNK + R], U8, "planes_first")
         clear_beside_gpsimd(planes_first[:].rearrange("p a n -> p (a n)").bitcast(I32))
         pages = [sbuf([P, T], F32, "page0")]
         nc.gpsimd.memset(pages[0][:].bitcast(I32), 0)
-        planes_rest = sbuf([P, 2, J - CHUNK], U8, "planes_rest")
-        nc.gpsimd.memset(planes_rest[:].bitcast(I32), 0)
+        planes_rest = sbuf([P, 2, REST], U8, "planes_rest")
+        clear_beside_gpsimd(planes_rest[:].rearrange("p a n -> p (a n)").bitcast(I32))
+        planes_next = sbuf([P, 2, CHUNK + N], U8, "planes_next")
+        nc.gpsimd.memset(planes_next[:].bitcast(I32), 0)
 
         def gather_scales(picked, j0, width):
             nc.vector.tensor_copy(picked, tab_sc[:].indirect(entries(j0, width)))
@@ -100,14 +104,17 @@ def tile_list_modp_gelu_res_noneb_kernel(
         )
         nc.vector.tensor_copy(stage[:, 0:CHUNK].bitcast(I32), picked_sc_first[:].bitcast(I32))
         spread(nc.scalar, planes_first, stage)
-        picked_sc_rest = placed("early", 0, [P, J - CHUNK], U8, "picked_sc_rest")
-        gather_scales(picked_sc_rest[:], CHUNK, J - CHUNK)
+        picked_sc_next = placed("early", 4 * J - LAP, [P, CHUNK], U8, "picked_sc_next")
+        gather_scales(picked_sc_next[:], CHUNK, CHUNK)
+        picked_sc_rest = placed("early", 4 * J - LAP + CHUNK, [P, REST], U8, "picked_sc_rest")
+        gather_scales(picked_sc_rest[:], 2 * CHUNK, REST)
+        nc.vector.tensor_copy(stage_next[:, 0:CHUNK].bitcast(I32), picked_sc_next[:].bitcast(I32))
         wu_sc = planes_first[:, :, CHUNK : CHUNK + R]
-        wd_sc = planes_first[:, :, CHUNK + R :]
+        wd_sc = planes_next[:, :, CHUNK:]
 
         def v_sc(a, j0, width):
-            planes, first = (planes_first, 0) if j0 < CHUNK else (planes_rest, CHUNK)
-            return planes[:, a, j0 - first : j0 - first + width]
+            c = min(j0 // CHUNK, 2)
+            return (planes_first, planes_next, planes_rest)[c][:, a, j0 - c * CHUNK : j0 - c * CHUNK + width]
 
         wu = [[sbuf([P, 2 * P], U32, "wu%d_%d" % (a, u)) for u in range(2)] for a in range(PASSES)]
         for a in range(PASSES):
@@ -132,17 +139,18 @@ def tile_list_modp_gelu_res_noneb_kernel(
         pages.append(placed("paged", 2 * PAGE_BYTES, [P, T], F32, "page1"))
         nc.gpsimd.memset(pages[1][:].bitcast(I32), 0)
 
-        spread(nc.sync, planes_rest, picked_sc_rest)
-        wd = placed("late", 4 * J + LAP, [P, 6 * N], U8, "wd")
+        wd = placed("late", 0, [P, 6 * N], U8, "wd")
         wd8 = wd[:, 0 : 4 * N]
         wd4 = wd[:, 4 * N : 6 * N]
         nc.sync.dma_start(wd8.bitcast(I32), wd8_words[0].rearrange("p n i -> p (n i)").bitcast(I32))
         nc.sync.dma_start(wd4.bitcast(I32), wd4_words[0].bitcast(I32))
-        b_t = placed("late", 4 * J, [P, BLOCKS], F32, "b_t")
+        spread(nc.sync, planes_next, stage_next)
+        b_t = placed("early", 4 * J, [P, BLOCKS], F32, "b_t")
         with nc.allow_non_contiguous_dma(reason="one bias value a partition and block"):
             nc.sync.dma_start(b_t[:], b.rearrange("(c p) -> p c", p=P))
-        weight = placed("late", 0, [P, J], F32, "weight")
+        weight = placed("early", 0, [P, J], F32, "weight")
         nc.sync.dma_start(weight[:], wgo)
+        spread(nc.sync, planes_rest, picked_sc_rest)
 
         def gather(picked, j0, width):
             nc.vector.tensor_copy(picked, tab[:].indirect(entries(j0, width)))

@@ -82,8 +82,6 @@ def tile_list_modp_gelu_res_noneb_kernel(
         clear_beside_gpsimd(planes_first[:].rearrange("p a n -> p (a n)").bitcast(I32))
         pages = [sbuf([P, T], F32, "page0")]
         nc.gpsimd.memset(pages[0][:].bitcast(I32), 0)
-        planes_rest = sbuf([P, 2, REST], U8, "planes_rest")
-        clear_beside_gpsimd(planes_rest[:].rearrange("p a n -> p (a n)").bitcast(I32))
         planes_next = sbuf([P, 2, CHUNK + N], U8, "planes_next")
         nc.gpsimd.memset(planes_next[:].bitcast(I32), 0)
 
@@ -96,7 +94,7 @@ def tile_list_modp_gelu_res_noneb_kernel(
                     planes[32 * q : 32 * q + 4, :, :].bitcast(I32), rows[ROWS0 + 8 * q : ROWS0 + 8 * q + 8, :].bitcast(I32)
                 )
 
-        picked_sc_first = placed("paged", 2 * PAGE_BYTES, [P, CHUNK], U8, "picked_sc_first")
+        picked_sc_first = placed("paged", 3 * PAGE_BYTES - LAP, [P, CHUNK], U8, "picked_sc_first")
         gather_scales(picked_sc_first[:], 0, CHUNK)
         nc.vector.tensor_copy(
             stage[:, CHUNK : CHUNK + R].rearrange("p (t c i) -> p c t i", t=PACK, i=16),
@@ -106,6 +104,8 @@ def tile_list_modp_gelu_res_noneb_kernel(
         spread(nc.scalar, planes_first, stage)
         picked_sc_next = placed("early", 4 * J - LAP, [P, CHUNK], U8, "picked_sc_next")
         gather_scales(picked_sc_next[:], CHUNK, CHUNK)
+        planes_rest = placed("paged", 3 * PAGE_BYTES, [P, 2, REST], U8, "planes_rest")
+        clear_beside_gpsimd(planes_rest[:].rearrange("p a n -> p (a n)").bitcast(I32))
         picked_sc_rest = placed("early", 4 * J - LAP + CHUNK, [P, REST], U8, "picked_sc_rest")
         gather_scales(picked_sc_rest[:], 2 * CHUNK, REST)
         nc.vector.tensor_copy(stage_next[:, 0:CHUNK].bitcast(I32), picked_sc_next[:].bitcast(I32))
@@ -145,12 +145,16 @@ def tile_list_modp_gelu_res_noneb_kernel(
         nc.sync.dma_start(wd8.bitcast(I32), wd8_words[0].rearrange("p n i -> p (n i)").bitcast(I32))
         nc.sync.dma_start(wd4.bitcast(I32), wd4_words[0].bitcast(I32))
         spread(nc.sync, planes_next, stage_next)
-        b_t = placed("early", 4 * J, [P, BLOCKS], F32, "b_t")
-        with nc.allow_non_contiguous_dma(reason="one bias value a partition and block"):
-            nc.sync.dma_start(b_t[:], b.rearrange("(c p) -> p c", p=P))
+        b_first = placed("early", 4 * J, [P, 1], F32, "b_first")
+        b_rest = placed("early", 4 * J + LAP, [P, BLOCKS - 1], F32, "b_rest")
         weight = placed("early", 0, [P, J], F32, "weight")
-        nc.sync.dma_start(weight[:], wgo)
+        by_block = b.rearrange("(c p) -> p c", p=P)
+        with nc.allow_non_contiguous_dma(reason="one bias value a partition and block"):
+            nc.sync.dma_start(b_first[:], by_block[:, 0:1])
+            nc.sync.dma_start(weight[:, 0:CHUNK], wgo[:, 0:CHUNK])
+            nc.sync.dma_start(b_rest[:], by_block[:, 1:])
         spread(nc.sync, planes_rest, picked_sc_rest)
+        nc.sync.dma_start(weight[:, CHUNK:], wgo[:, CHUNK:])
 
         def gather(picked, j0, width):
             nc.vector.tensor_copy(picked, tab[:].indirect(entries(j0, width)))
@@ -240,7 +244,7 @@ def tile_list_modp_gelu_res_noneb_kernel(
             return bank
 
         def add_bias(y, bank, block):
-            nc.scalar.activation(y, bank[:], ACT.Identity, bias=b_t[:, block : block + 1])
+            nc.scalar.activation(y, bank[:], ACT.Identity, bias=b_first[:] if block == 0 else b_rest[:, block - 1 : block])
 
         def scatter(block, y, j0, width):
             page = pages[block]

@@ -21,6 +21,7 @@ PACK = 4
 PASSES = K // (P * PACK)
 CHUNK = 256
 HALF = 128
+QUARTER = 64
 REST = J - 2 * CHUNK
 BLOCKS = N // P
 ROWS0 = 96
@@ -28,6 +29,7 @@ WARM_PASSES = 6
 WARM_COLUMNS = 32
 PAGE_BYTES = 4 * T
 LAP = 64
+AT_FIRST_CODES = 4 * PACK * CHUNK
 
 
 def tile_list_modp_gelu_res_noneb_kernel(
@@ -38,7 +40,7 @@ def tile_list_modp_gelu_res_noneb_kernel(
         lists = ctx.enter_context(tc.tile_pool(name="lists", bufs=1))
         free = ctx.enter_context(tc.tile_pool(name="free", bufs=1))
         psum = ctx.enter_context(tc.psum_pool(name="psum", bufs=1))
-        arenas = {name: ctx.enter_context(tc.tile_pool(name=name, bufs=1)) for name in ("late", "early", "paged", "words", "hidden")}
+        arenas = {name: ctx.enter_context(tc.tile_pool(name=name, bufs=1)) for name in ("late", "early", "paged", "words", "hidden", "last")}
 
         def sbuf(shape, dtype, name, tag=None):
             return free.tile(shape, dtype, name=name, tag=tag or name, align_bytes=64)
@@ -67,9 +69,10 @@ def tile_list_modp_gelu_res_noneb_kernel(
         nc.sync.dma_start(tab[:].bitcast(I32), tab_words[0].rearrange("p t i -> p (t i)").bitcast(I32))
         nc.sync.dma_start(wu_raw[1][:].bitcast(I32), wu_words[1].rearrange("p r i -> p (r i)").bitcast(I32))
 
-        seed = sbuf([P, 2], F32, "seed")
-        nc.vector.memset(seed[:, 0:1], 0.0)
-        nc.scalar.activation(seed[:, 1:2], seed[:, 0:1], ACT.Gelu_apprx_tanh)
+        zero = placed("hidden", AT_FIRST_CODES, [P, 1], F32, "zero")
+        nc.vector.memset(zero[:], 0.0)
+        unread = sbuf([P, 1], F32, "unread")
+        nc.scalar.activation(unread[:], zero[:], ACT.Gelu_apprx_tanh)
 
         def clear_beside_gpsimd(words):
             cut = words.shape[1] // 2 - 1
@@ -271,19 +274,23 @@ def tile_list_modp_gelu_res_noneb_kernel(
         seam = PAGE_BYTES - LAP
         wovens = [placed("paged", seam, [P, HALF * PACK], BF16, "woven0_0"), sbuf([P, HALF * PACK], BF16, "woven0_1")]
         for half in range(2):
-            g = sbuf([P, HALF, PACK], F32, "g0_%d" % half)
-            nc.scalar.activation(g[:], up(halves[half][:], half * HALF)[:].rearrange("p t j -> p j t"), ACT.Gelu_apprx_tanh)
-            nc.vector.tensor_tensor(
-                wovens[half][:].rearrange("p (j t) -> p j t", t=PACK),
-                g[:],
-                sm_t[:].unsqueeze(1).to_broadcast([P, HALF, PACK]),
-                MULT,
-            )
+            bank = up(halves[half][:], half * HALF)
+            for i in range(2):
+                last = half == 1 and i == 1
+                g = placed("last", 0, [P, QUARTER, PACK], F32, "g0_last") if last else sbuf([P, QUARTER, PACK], F32, "g0_%d%d" % (half, i))
+                sums = bank[:, :, i * QUARTER : (i + 1) * QUARTER].rearrange("p t j -> p j t")
+                nc.scalar.activation(g[:], sums, ACT.Gelu_apprx_tanh, bias=zero[:])
+                nc.vector.tensor_tensor(
+                    wovens[half][:, i * QUARTER * PACK : (i + 1) * QUARTER * PACK].rearrange("p (j t) -> p j t", t=PACK),
+                    g[:],
+                    sm_t[:].unsqueeze(1).to_broadcast([P, QUARTER, PACK]),
+                    MULT,
+                )
         for half in range(2):
             quantise(wovens[half][:], half * HALF, HALF)
         picked3 = placed("paged", seam, [P, CHUNK], U32, "picked3")
         gather(picked3[:], 3 * CHUNK, CHUNK)
-        v2 = sbuf([P, PASSES, 2 * CHUNK], U8, "v2", "g0_1")
+        v2 = placed("last", 0, [P, PASSES, 2 * CHUNK], U8, "v2")
         part(v2[:], picked12[:, CHUNK:])
         v3 = sbuf([P, PASSES, 2 * CHUNK], U8, "v3")
         part(v3[:], picked3[:])

@@ -25,7 +25,7 @@ QUARTER = 64
 REST = J - 2 * CHUNK
 BLOCKS = N // P
 ROWS0 = 96
-WARM_PASSES = 6
+WARM_PASSES = 7
 WARM_COLUMNS = 32
 PAGE_BYTES = 4 * T
 LAP = 64
@@ -132,9 +132,9 @@ def tile_list_modp_gelu_res_noneb_kernel(
             nc.tensor.matmul_mx(
                 out=idle[0:WARM_COLUMNS, :],
                 lhsT=wu_raw[0][:, 0:WARM_COLUMNS].bitcast(FP8X4),
-                lhsT_scale=stage[:, CHUNK : CHUNK + WARM_COLUMNS],
+                lhsT_scale=planes_next[:, 0, 0:WARM_COLUMNS],
                 rhs=wu_raw[0][:].bitcast(FP8X4),
-                rhs_scale=stage[:, CHUNK : CHUNK + R],
+                rhs_scale=planes_next[:, 0, 0:R],
                 start=True,
                 stop=True,
             )

@@ -25,7 +25,7 @@ QUARTER = 64
 REST = J - 2 * CHUNK
 BLOCKS = N // P
 ROWS0 = 96
-WARM_PASSES = 7
+WARM_PASSES = 6
 WARM_COLUMNS = 32
 PAGE_BYTES = 4 * T
 LAP = 64
@@ -40,7 +40,7 @@ def tile_list_modp_gelu_res_noneb_kernel(
         lists = ctx.enter_context(tc.tile_pool(name="lists", bufs=1))
         free = ctx.enter_context(tc.tile_pool(name="free", bufs=1))
         psum = ctx.enter_context(tc.psum_pool(name="psum", bufs=1))
-        arenas = {name: ctx.enter_context(tc.tile_pool(name=name, bufs=1)) for name in ("late", "early", "paged", "words", "hidden", "last")}
+        arenas = {name: ctx.enter_context(tc.tile_pool(name=name, bufs=1)) for name in ("a", "b", "d", "e", "f", "hidden")}
 
         def sbuf(shape, dtype, name, tag=None):
             return free.tile(shape, dtype, name=name, tag=tag or name, align_bytes=64)
@@ -53,21 +53,18 @@ def tile_list_modp_gelu_res_noneb_kernel(
 
         offsets = lists.tile([P, J // 16], U16, name="offsets")
         nc.sync.dma_start(offsets[:], offs)
-        tab_sc = placed("late", 0, [P, T], U8, "tab_sc")
-        nc.sync.dma_start(tab_sc[ROWS0:P, :].bitcast(I32), tab_scales.rearrange("a q t -> q a t").bitcast(I32))
-        wu_sc_raw = placed("early", 4 * J - LAP, [P, R], U8, "wu_sc_raw")
-        nc.sync.dma_start(wu_sc_raw[ROWS0:P, :].bitcast(I32), wu_scales.rearrange("a q r -> q a r").bitcast(I32))
-        stage = sbuf([P, CHUNK + R], U8, "stage")
+        tab_sc = sbuf([P, T], U8, "tab_sc")
+        nc.scalar.dma_start(tab_sc[ROWS0:P, :].bitcast(I32), tab_scales.rearrange("a q t -> q a t").bitcast(I32))
         stage_next = sbuf([P, CHUNK + N], U8, "stage_next")
-        nc.scalar.dma_start(stage_next[ROWS0:P:2, CHUNK:].bitcast(I32), wd4_scales[0].bitcast(I32))
-        nc.scalar.dma_start(stage_next[ROWS0 + 1 : P : 2, CHUNK:].bitcast(I32), wd8_scales[0].bitcast(I32))
-        sm_t = sbuf([P, PACK], F32, "sm_t")
-        nc.scalar.dma_start(sm_t[:], sm.rearrange("(p t) -> p t", t=PACK))
-        wu_raw = [sbuf([P, R], U32, "wu_raw%d" % a) for a in range(PASSES)]
-        nc.sync.dma_start(wu_raw[0][:].bitcast(I32), wu_words[0].rearrange("p r i -> p (r i)").bitcast(I32))
+        nc.sync.dma_start(stage_next[ROWS0:P:2, CHUNK:].bitcast(I32), wd4_scales[0].bitcast(I32))
+        wu_sc_raw = placed("d", 0, [P, R], U8, "wu_sc_raw")
+        nc.scalar.dma_start(wu_sc_raw[ROWS0:P, :].bitcast(I32), wu_scales.rearrange("a q r -> q a r").bitcast(I32))
         tab = sbuf([P, T], U32, "tab")
         nc.sync.dma_start(tab[:].bitcast(I32), tab_words[0].rearrange("p t i -> p (t i)").bitcast(I32))
-        nc.sync.dma_start(wu_raw[1][:].bitcast(I32), wu_words[1].rearrange("p r i -> p (r i)").bitcast(I32))
+        nc.scalar.dma_start(stage_next[ROWS0 + 1 : P : 2, CHUNK:].bitcast(I32), wd8_scales[0].bitcast(I32))
+        wu_raw = [sbuf([P, R], U32, "wu_raw%d" % a) for a in range(PASSES)]
+        for a in range(PASSES):
+            nc.sync.dma_start(wu_raw[a][:].bitcast(I32), wu_words[a].rearrange("p r i -> p (r i)").bitcast(I32))
 
         zero = placed("hidden", AT_FIRST_CODES, [P, 1], F32, "zero")
         nc.vector.memset(zero[:], 0.0)
@@ -81,12 +78,27 @@ def tile_list_modp_gelu_res_noneb_kernel(
 
         clear_beside_gpsimd(tab_sc[0:ROWS0, :].bitcast(I32))
         clear_beside_gpsimd(wu_sc_raw[0:ROWS0, :].bitcast(I32))
-        planes_first = sbuf([P, 2, CHUNK + R], U8, "planes_first")
-        clear_beside_gpsimd(planes_first[:].rearrange("p a n -> p (a n)").bitcast(I32))
+        planes_first = sbuf([P, 2 * (CHUNK + R)], U8, "planes_first")
+        clear_beside_gpsimd(planes_first[:].bitcast(I32))
+        at_rest = 2 * (CHUNK + N)
+        planes_late = sbuf([P, at_rest + 2 * REST], U8, "planes_late")
+        nc.gpsimd.memset(planes_late[:].bitcast(I32), 0)
         pages = [sbuf([P, T], F32, "page0")]
         nc.gpsimd.memset(pages[0][:].bitcast(I32), 0)
-        planes_next = sbuf([P, 2, CHUNK + N], U8, "planes_next")
-        nc.gpsimd.memset(planes_next[:].bitcast(I32), 0)
+        sm_t = sbuf([P, PACK], F32, "sm_t")
+        nc.gpsimd.dma_start(sm_t[:], sm.rearrange("(p t) -> p t", t=PACK))
+
+        idle = psum.tile([P, R], F32, name="y_bank", tag="y_bank", bufs=4)
+        for i in range(WARM_PASSES):
+            nc.tensor.matmul_mx(
+                out=idle[0:WARM_COLUMNS, :],
+                lhsT=planes_late[:, 0 : 4 * WARM_COLUMNS].bitcast(FP8X4),
+                lhsT_scale=tab_sc[:, 0:WARM_COLUMNS],
+                rhs=planes_late[:, 0 : 4 * R].bitcast(FP8X4),
+                rhs_scale=planes_late[:, 4 * R : 5 * R],
+                start=True,
+                stop=True,
+            )
 
         def gather_scales(picked, j0, width):
             nc.vector.tensor_copy(picked, tab_sc[:].indirect(entries(j0, width)))
@@ -94,30 +106,41 @@ def tile_list_modp_gelu_res_noneb_kernel(
         def spread(queue, planes, rows):
             for q in (0, 2, 1, 3):
                 queue.dma_start(
-                    planes[32 * q : 32 * q + 4, :, :].bitcast(I32), rows[ROWS0 + 8 * q : ROWS0 + 8 * q + 8, :].bitcast(I32)
+                    planes[32 * q : 32 * q + 4, :].bitcast(I32).rearrange("p (a n) -> p a n", a=2),
+                    rows[ROWS0 + 8 * q : ROWS0 + 8 * q + 8, :].bitcast(I32),
                 )
 
-        picked_sc_first = placed("paged", 3 * PAGE_BYTES - LAP, [P, CHUNK], U8, "picked_sc_first")
-        gather_scales(picked_sc_first[:], 0, CHUNK)
+        stage = sbuf([P, CHUNK + R], U8, "stage")
+        picked_sc0 = sbuf([P, CHUNK], U8, "picked_sc0")
+        gather_scales(picked_sc0[:], 0, CHUNK)
         nc.vector.tensor_copy(
             stage[:, CHUNK : CHUNK + R].rearrange("p (t c i) -> p c t i", t=PACK, i=16),
             wu_sc_raw[:].rearrange("p (c i t) -> p c t i", t=PACK, i=16),
         )
-        nc.vector.tensor_copy(stage[:, 0:CHUNK].bitcast(I32), picked_sc_first[:].bitcast(I32))
-        spread(nc.scalar, planes_first, stage)
-        picked_sc_next = placed("early", 4 * J - LAP, [P, CHUNK], U8, "picked_sc_next")
-        gather_scales(picked_sc_next[:], CHUNK, CHUNK)
-        planes_rest = placed("paged", 3 * PAGE_BYTES, [P, 2, REST], U8, "planes_rest")
-        clear_beside_gpsimd(planes_rest[:].rearrange("p a n -> p (a n)").bitcast(I32))
-        picked_sc_rest = placed("early", 4 * J - LAP + CHUNK, [P, REST], U8, "picked_sc_rest")
+        nc.vector.tensor_copy(stage[:, 0:CHUNK].bitcast(I32), picked_sc0[:].bitcast(I32))
+        spread(nc.scalar, planes_first[:], stage)
+        picked_sc1 = placed("d", 0, [P, CHUNK], U8, "picked_sc1")
+        gather_scales(picked_sc1[:], CHUNK, CHUNK)
+        picked_sc_rest = placed("d", CHUNK, [P, REST], U8, "picked_sc_rest")
         gather_scales(picked_sc_rest[:], 2 * CHUNK, REST)
-        nc.vector.tensor_copy(stage_next[:, 0:CHUNK].bitcast(I32), picked_sc_next[:].bitcast(I32))
-        wu_sc = planes_first[:, :, CHUNK : CHUNK + R]
-        wd_sc = planes_next[:, :, CHUNK:]
+        nc.vector.tensor_copy(stage_next[:, 0:CHUNK].bitcast(I32), picked_sc1[:].bitcast(I32))
+
+        def wu_sc(a, t):
+            at = a * (CHUNK + R) + CHUNK + t * P
+            return planes_first[:, at : at + P]
+
+        def wd_sc(tier, block):
+            at = tier * (CHUNK + N) + CHUNK + block * P
+            return planes_late[:, at : at + P]
 
         def v_sc(a, j0, width):
-            c = min(j0 // CHUNK, 2)
-            return (planes_first, planes_next, planes_rest)[c][:, a, j0 - c * CHUNK : j0 - c * CHUNK + width]
+            if j0 < CHUNK:
+                planes, at = planes_first, a * (CHUNK + R) + j0
+            elif j0 < 2 * CHUNK:
+                planes, at = planes_late, a * (CHUNK + N) + j0 - CHUNK
+            else:
+                planes, at = planes_late, at_rest + a * REST + j0 - 2 * CHUNK
+            return planes[:, at : at + width]
 
         wu = [[sbuf([P, 2 * P], U32, "wu%d_%d" % (a, u)) for u in range(2)] for a in range(PASSES)]
         for a in range(PASSES):
@@ -127,37 +150,7 @@ def tile_list_modp_gelu_res_noneb_kernel(
                     wu_raw[a][:].rearrange("p (c i t) -> p c t i", t=PACK, i=4)[:, :, 2 * u : 2 * u + 2, :],
                 )
 
-        idle = psum.tile([P, R], F32, name="y_bank", tag="y_bank", bufs=4)
-        for i in range(WARM_PASSES):
-            nc.tensor.matmul_mx(
-                out=idle[0:WARM_COLUMNS, :],
-                lhsT=wu_raw[0][:, 0:WARM_COLUMNS].bitcast(FP8X4),
-                lhsT_scale=planes_next[:, 0, 0:WARM_COLUMNS],
-                rhs=wu_raw[0][:].bitcast(FP8X4),
-                rhs_scale=planes_next[:, 0, 0:R],
-                start=True,
-                stop=True,
-            )
-
-        pages.append(placed("paged", 2 * PAGE_BYTES, [P, T], F32, "page1"))
-        nc.gpsimd.memset(pages[1][:].bitcast(I32), 0)
-
-        wd = placed("late", 0, [P, 6 * N], U8, "wd")
-        wd8 = wd[:, 0 : 4 * N]
-        wd4 = wd[:, 4 * N : 6 * N]
-        nc.sync.dma_start(wd8.bitcast(I32), wd8_words[0].rearrange("p n i -> p (n i)").bitcast(I32))
-        nc.sync.dma_start(wd4.bitcast(I32), wd4_words[0].bitcast(I32))
-        spread(nc.sync, planes_next, stage_next)
-        b_first = placed("early", 4 * J, [P, 1], F32, "b_first")
-        b_rest = placed("early", 4 * J + LAP, [P, BLOCKS - 1], F32, "b_rest")
-        weight = placed("early", 0, [P, J], F32, "weight")
-        by_block = b.rearrange("(c p) -> p c", p=P)
-        with nc.allow_non_contiguous_dma(reason="one bias value a partition and block"):
-            nc.sync.dma_start(b_first[:], by_block[:, 0:1])
-            nc.sync.dma_start(weight[:, 0:CHUNK], wgo[:, 0:CHUNK])
-            nc.sync.dma_start(b_rest[:], by_block[:, 1:])
-        spread(nc.sync, planes_rest, picked_sc_rest)
-        nc.sync.dma_start(weight[:, CHUNK:], wgo[:, CHUNK:])
+        spread(nc.sync, planes_late[:, 0:at_rest], stage_next)
 
         def gather(picked, j0, width):
             nc.vector.tensor_copy(picked, tab[:].indirect(entries(j0, width)))
@@ -172,7 +165,7 @@ def tile_list_modp_gelu_res_noneb_kernel(
                     nc.tensor.matmul_mx(
                         out=bank[:, t, :],
                         lhsT=wu[a][t // 2][:, t % 2 * P : (t % 2 + 1) * P].bitcast(FP8X4),
-                        lhsT_scale=wu_sc[:, a, t * P : (t + 1) * P],
+                        lhsT_scale=wu_sc(a, t),
                         rhs=v[:, a, :].bitcast(FP4X4),
                         rhs_scale=v_sc(a, j0, HALF),
                         start=(a == 0 and t == 0),
@@ -198,7 +191,7 @@ def tile_list_modp_gelu_res_noneb_kernel(
 
         def gelu(c, g, v):
             for half in range(2):
-                bank = up(v[:, :, 2 * half * HALF : 2 * (half + 1) * HALF], c * CHUNK + half * HALF)
+                bank = up(v[half], c * CHUNK + half * HALF)
                 nc.scalar.activation(g[:, :, half * HALF : (half + 1) * HALF], bank[:], ACT.Gelu_apprx_tanh)
 
         def smooth(slices, g):
@@ -225,11 +218,10 @@ def tile_list_modp_gelu_res_noneb_kernel(
 
         def down(block, j0, width):
             bank = psum.tile([P, width], F32, name="y_bank", tag="y_bank", bufs=4)
-            cols = slice(block * P, (block + 1) * P)
             nc.tensor.matmul_mx(
                 out=bank[:],
                 lhsT=wd8[:, 4 * block * P : 4 * (block + 1) * P].bitcast(FP8X4),
-                lhsT_scale=wd_sc[:, 1, cols],
+                lhsT_scale=wd_sc(1, block),
                 rhs=h_codes(j0, width),
                 rhs_scale=h_sc[:, j0 : j0 + width],
                 start=True,
@@ -238,7 +230,7 @@ def tile_list_modp_gelu_res_noneb_kernel(
             nc.tensor.matmul_mx(
                 out=bank[:],
                 lhsT=wd4[:, 2 * block * P : 2 * (block + 1) * P].bitcast(FP4X4),
-                lhsT_scale=wd_sc[:, 0, cols],
+                lhsT_scale=wd_sc(0, block),
                 rhs=h_codes(j0, width),
                 rhs_scale=h_sc[:, j0 : j0 + width],
                 start=False,
@@ -259,25 +251,47 @@ def tile_list_modp_gelu_res_noneb_kernel(
             add_bias(y, down(block, j0, width) if bank is None else bank, block)
             scatter(block, y, j0, width)
 
-        halves = [sbuf([P, PASSES, 2 * HALF], U8, "v0_%d" % half) for half in range(2)]
-        picked0 = [placed("words", 4 * HALF * (half + 3), [P, HALF], U32, "picked0_%d" % half) for half in range(2)]
+        def halves_of(v):
+            return [v[:, :, 2 * half * HALF : 2 * (half + 1) * HALF] for half in range(2)]
+
+        picked0 = [placed("a", 7872, [P, HALF], U32, "picked0_0"), placed("b", 3008, [P, HALF], U32, "picked0_1")]
+        v0 = [sbuf([P, PASSES, 2 * HALF], U8, "v0_%d" % half) for half in range(2)]
         for half in range(2):
             gather(picked0[half][:], half * HALF, HALF)
         for half in range(2):
-            part(halves[half][:], picked0[half][:])
-        picked12 = placed("words", 0, [P, 2 * CHUNK], U32, "picked12")
-        v1 = sbuf([P, PASSES, 2 * CHUNK], U8, "v1")
-        gather(picked12[:, 0:CHUNK], CHUNK, CHUNK)
-        gather(picked12[:, CHUNK:], 2 * CHUNK, CHUNK)
-        part(v1[:], picked12[:, 0:CHUNK])
-
-        seam = PAGE_BYTES - LAP
-        wovens = [placed("paged", seam, [P, HALF * PACK], BF16, "woven0_0"), sbuf([P, HALF * PACK], BF16, "woven0_1")]
+            part(v0[half][:], picked0[half][:])
+        picked1 = [placed("a", 8128, [P, HALF], U32, "picked1_0"), placed("b", 3456, [P, HALF], U32, "picked1_1")]
+        v1 = [sbuf([P, PASSES, 2 * HALF], U8, "v1_%d" % half)[:] for half in range(2)]
         for half in range(2):
-            bank = up(halves[half][:], half * HALF)
+            gather(picked1[half][:], CHUNK + half * HALF, HALF)
+        for half in range(2):
+            part(v1[half], picked1[half][:])
+        pages.append(placed("a", 0, [P, T], F32, "page1"))
+        nc.gpsimd.memset(pages[1][:].bitcast(I32), 0)
+        picked2 = placed("a", 8576, [P, CHUNK], U32, "picked2")
+        gather(picked2[:], 2 * CHUNK, CHUNK)
+
+        wd = placed("b", 0, [P, 6 * N], U8, "wd")
+        wd8 = wd[:, 0 : 4 * N]
+        wd4 = wd[:, 4 * N : 6 * N]
+        nc.sync.dma_start(wd8.bitcast(I32), wd8_words[0].rearrange("p n i -> p (n i)").bitcast(I32))
+        nc.sync.dma_start(wd4.bitcast(I32), wd4_words[0].bitcast(I32))
+        b_first = placed("b", 3584, [P, 1], F32, "b_first")
+        b_rest = placed("b", 3648, [P, BLOCKS - 1], F32, "b_rest")
+        weight = placed("b", 3904, [P, J], F32, "weight")
+        by_block = b.rearrange("(c p) -> p c", p=P)
+        with nc.allow_non_contiguous_dma(reason="one bias value a partition and block"):
+            nc.sync.dma_start(b_first[:], by_block[:, 0:1])
+            nc.sync.dma_start(weight[:, 0:CHUNK], wgo[:, 0:CHUNK])
+            nc.sync.dma_start(b_rest[:], by_block[:, 1:])
+        spread(nc.sync, planes_late[:, at_rest:], picked_sc_rest)
+        nc.sync.dma_start(weight[:, CHUNK:], wgo[:, CHUNK:])
+
+        wovens = [placed("e", 0, [P, HALF * PACK], BF16, "woven0_0"), placed("f", 0, [P, HALF * PACK], BF16, "woven0_1")]
+        for half in range(2):
+            bank = up(v0[half][:], half * HALF)
             for i in range(2):
-                last = half == 1 and i == 1
-                g = placed("last", 0, [P, QUARTER, PACK], F32, "g0_last") if last else sbuf([P, QUARTER, PACK], F32, "g0_%d%d" % (half, i))
+                g = sbuf([P, QUARTER, PACK], F32, "g0_%d%d" % (half, i))
                 sums = bank[:, :, i * QUARTER : (i + 1) * QUARTER].rearrange("p t j -> p j t")
                 nc.scalar.activation(g[:], sums, ACT.Gelu_apprx_tanh, bias=zero[:])
                 nc.vector.tensor_tensor(
@@ -288,15 +302,17 @@ def tile_list_modp_gelu_res_noneb_kernel(
                 )
         for half in range(2):
             quantise(wovens[half][:], half * HALF, HALF)
-        picked3 = placed("paged", seam, [P, CHUNK], U32, "picked3")
+        picked3 = placed("e", 0, [P, CHUNK], U32, "picked3")
         gather(picked3[:], 3 * CHUNK, CHUNK)
-        v2 = placed("last", 0, [P, PASSES, 2 * CHUNK], U8, "v2")
-        part(v2[:], picked12[:, CHUNK:])
-        v3 = sbuf([P, PASSES, 2 * CHUNK], U8, "v3")
-        part(v3[:], picked3[:])
-        for i in range(2):
-            pages.append(placed("paged", PAGE_BYTES * i, [P, T], F32, "page%d" % (2 + i)))
-            nc.gpsimd.memset(pages[2 + i][:].bitcast(I32), 0)
+        whole2 = placed("f", 960, [P, PASSES, 2 * CHUNK], U8, "v2")
+        part(whole2[:], picked2[:])
+        whole3 = sbuf([P, PASSES, 2 * CHUNK], U8, "v3")
+        part(whole3[:], picked3[:])
+        v2, v3 = halves_of(whole2), halves_of(whole3)
+        pages.append(placed("a", 9536, [P, T], F32, "page2"))
+        pages.append(placed("e", 960, [P, T], F32, "page3"))
+        for block in range(2, BLOCKS):
+            nc.gpsimd.memset(pages[block][:].bitcast(I32), 0)
 
         g = sbuf([P, PACK, CHUNK], F32, "g1")
         gelu(1, g, v1)

@@ -25,7 +25,7 @@ QUARTER = 64
 REST = J - 2 * CHUNK
 BLOCKS = N // P
 ROWS0 = 96
-WARM_PASSES = 6
+WARM_PASSES = 7
 WARM_COLUMNS = 32
 PAGE_BYTES = 4 * T
 LAP = 64
@@ -80,25 +80,14 @@ def tile_list_modp_gelu_res_noneb_kernel(
         clear_beside_gpsimd(wu_sc_raw[0:ROWS0, :].bitcast(I32))
         planes_first = sbuf([P, 2 * (CHUNK + R)], U8, "planes_first")
         clear_beside_gpsimd(planes_first[:].bitcast(I32))
-        at_rest = 2 * (CHUNK + N)
-        planes_late = sbuf([P, at_rest + 2 * REST], U8, "planes_late")
-        nc.gpsimd.memset(planes_late[:].bitcast(I32), 0)
+        rest = sbuf([P, 2 * REST + 4 * REST], U8, "rest")
+        nc.gpsimd.memset(rest[:, 0 : 4 * R].bitcast(I32), 0)
+        planes_next = sbuf([P, 2 * (CHUNK + N)], U8, "planes_next")
+        nc.gpsimd.memset(planes_next[:].bitcast(I32), 0)
         pages = [sbuf([P, T], F32, "page0")]
         nc.gpsimd.memset(pages[0][:].bitcast(I32), 0)
         sm_t = sbuf([P, PACK], F32, "sm_t")
         nc.gpsimd.dma_start(sm_t[:], sm.rearrange("(p t) -> p t", t=PACK))
-
-        idle = psum.tile([P, R], F32, name="y_bank", tag="y_bank", bufs=4)
-        for i in range(WARM_PASSES):
-            nc.tensor.matmul_mx(
-                out=idle[0:WARM_COLUMNS, :],
-                lhsT=planes_late[:, 0 : 4 * WARM_COLUMNS].bitcast(FP8X4),
-                lhsT_scale=tab_sc[:, 0:WARM_COLUMNS],
-                rhs=planes_late[:, 0 : 4 * R].bitcast(FP8X4),
-                rhs_scale=planes_late[:, 4 * R : 5 * R],
-                start=True,
-                stop=True,
-            )
 
         def gather_scales(picked, j0, width):
             nc.vector.tensor_copy(picked, tab_sc[:].indirect(entries(j0, width)))
@@ -119,6 +108,19 @@ def tile_list_modp_gelu_res_noneb_kernel(
         )
         nc.vector.tensor_copy(stage[:, 0:CHUNK].bitcast(I32), picked_sc0[:].bitcast(I32))
         spread(nc.scalar, planes_first[:], stage)
+
+        idle = psum.tile([P, R], F32, name="y_bank", tag="y_bank", bufs=4)
+        for i in range(WARM_PASSES):
+            nc.tensor.matmul_mx(
+                out=idle[0:WARM_COLUMNS, :],
+                lhsT=rest[:, 0 : 4 * WARM_COLUMNS].bitcast(FP8X4),
+                lhsT_scale=picked_sc0[:, 0:WARM_COLUMNS],
+                rhs=rest[:, 0 : 4 * R].bitcast(FP8X4),
+                rhs_scale=tab_sc[:, 0:R],
+                start=True,
+                stop=True,
+            )
+
         picked_sc1 = placed("d", 0, [P, CHUNK], U8, "picked_sc1")
         gather_scales(picked_sc1[:], CHUNK, CHUNK)
         picked_sc_rest = placed("d", CHUNK, [P, REST], U8, "picked_sc_rest")
@@ -131,15 +133,15 @@ def tile_list_modp_gelu_res_noneb_kernel(
 
         def wd_sc(tier, block):
             at = tier * (CHUNK + N) + CHUNK + block * P
-            return planes_late[:, at : at + P]
+            return planes_next[:, at : at + P]
 
         def v_sc(a, j0, width):
             if j0 < CHUNK:
                 planes, at = planes_first, a * (CHUNK + R) + j0
             elif j0 < 2 * CHUNK:
-                planes, at = planes_late, a * (CHUNK + N) + j0 - CHUNK
+                planes, at = planes_next, a * (CHUNK + N) + j0 - CHUNK
             else:
-                planes, at = planes_late, at_rest + a * REST + j0 - 2 * CHUNK
+                planes, at = rest, a * REST + j0 - 2 * CHUNK
             return planes[:, at : at + width]
 
         wu = [[sbuf([P, 2 * P], U32, "wu%d_%d" % (a, u)) for u in range(2)] for a in range(PASSES)]
@@ -150,7 +152,7 @@ def tile_list_modp_gelu_res_noneb_kernel(
                     wu_raw[a][:].rearrange("p (c i t) -> p c t i", t=PACK, i=4)[:, :, 2 * u : 2 * u + 2, :],
                 )
 
-        spread(nc.sync, planes_late[:, 0:at_rest], stage_next)
+        spread(nc.sync, planes_next[:], stage_next)
 
         def gather(picked, j0, width):
             nc.vector.tensor_copy(picked, tab[:].indirect(entries(j0, width)))
@@ -180,11 +182,14 @@ def tile_list_modp_gelu_res_noneb_kernel(
             return g_bytes + (c - 1) * (slices_bytes + 2 * g_bytes)
 
         h_first = placed("hidden", at_slices(1), [P, CHUNK], U32, "h_first")
-        h_rest = sbuf([P, J - CHUNK], U32, "h_rest")
+        h_next = sbuf([P, CHUNK], U32, "h_next")
         h_sc = sbuf([P, J], U8, "h_sc")
 
         def h_codes(j0, width):
-            return (h_first[:, j0 : j0 + width] if j0 < CHUNK else h_rest[:, j0 - CHUNK : j0 - CHUNK + width]).bitcast(FP8X4)
+            if j0 < 2 * CHUNK:
+                return (h_first, h_next)[j0 // CHUNK][:, j0 % CHUNK : j0 % CHUNK + width].bitcast(FP8X4)
+            at = 2 * REST + 4 * (j0 - 2 * CHUNK)
+            return rest[:, at : at + 4 * width].bitcast(FP8X4)
 
         def quantise(woven, j0, width):
             nc.vector.quantize_mx(out=h_codes(j0, width), scales=h_sc[:, j0 : j0 + width], in_=woven)
@@ -284,7 +289,7 @@ def tile_list_modp_gelu_res_noneb_kernel(
             nc.sync.dma_start(b_first[:], by_block[:, 0:1])
             nc.sync.dma_start(weight[:, 0:CHUNK], wgo[:, 0:CHUNK])
             nc.sync.dma_start(b_rest[:], by_block[:, 1:])
-        spread(nc.sync, planes_late[:, at_rest:], picked_sc_rest)
+        spread(nc.sync, rest[:, 0 : 2 * REST], picked_sc_rest)
         nc.sync.dma_start(weight[:, CHUNK:], wgo[:, CHUNK:])
 
         wovens = [placed("e", 0, [P, HALF * PACK], BF16, "woven0_0"), placed("f", 0, [P, HALF * PACK], BF16, "woven0_1")]

@@ -57,7 +57,7 @@ def tile_list_modp_gelu_res_noneb_kernel(
         nc.scalar.dma_start(tab_sc[ROWS0:P, :].bitcast(I32), tab_scales.rearrange("a q t -> q a t").bitcast(I32))
         stage_next = sbuf([P, CHUNK + N], U8, "stage_next")
         nc.sync.dma_start(stage_next[ROWS0:P:2, CHUNK:].bitcast(I32), wd4_scales[0].bitcast(I32))
-        wu_sc_raw = placed("d", 0, [P, R], U8, "wu_sc_raw")
+        wu_sc_raw = placed("d", 1472, [P, R], U8, "wu_sc_raw")
         nc.scalar.dma_start(wu_sc_raw[ROWS0:P, :].bitcast(I32), wu_scales.rearrange("a q r -> q a r").bitcast(I32))
         tab = sbuf([P, T], U32, "tab")
         nc.sync.dma_start(tab[:].bitcast(I32), tab_words[0].rearrange("p t i -> p (t i)").bitcast(I32))
@@ -81,13 +81,10 @@ def tile_list_modp_gelu_res_noneb_kernel(
         planes_first = sbuf([P, 2 * (CHUNK + R)], U8, "planes_first")
         clear_beside_gpsimd(planes_first[:].bitcast(I32))
         rest = sbuf([P, 2 * REST + 4 * REST], U8, "rest")
-        nc.gpsimd.memset(rest[:, 0 : 4 * R].bitcast(I32), 0)
-        planes_next = sbuf([P, 2 * (CHUNK + N)], U8, "planes_next")
-        nc.gpsimd.memset(planes_next[:].bitcast(I32), 0)
+        clear_beside_gpsimd(rest[:, 0 : 2 * R].bitcast(I32))
+        nc.gpsimd.memset(rest[:, 2 * R : 4 * R].bitcast(I32), 0)
         pages = [sbuf([P, T], F32, "page0")]
         nc.gpsimd.memset(pages[0][:].bitcast(I32), 0)
-        sm_t = sbuf([P, PACK], F32, "sm_t")
-        nc.gpsimd.dma_start(sm_t[:], sm.rearrange("(p t) -> p t", t=PACK))
 
         def gather_scales(picked, j0, width):
             nc.vector.tensor_copy(picked, tab_sc[:].indirect(entries(j0, width)))
@@ -108,6 +105,10 @@ def tile_list_modp_gelu_res_noneb_kernel(
         )
         nc.vector.tensor_copy(stage[:, 0:CHUNK].bitcast(I32), picked_sc0[:].bitcast(I32))
         spread(nc.scalar, planes_first[:], stage)
+        planes_next = placed("d", 0, [P, 2 * (CHUNK + N)], U8, "planes_next")
+        nc.gpsimd.memset(planes_next[:].bitcast(I32), 0)
+        sm_t = placed("d", 1536, [P, PACK], F32, "sm_t")
+        nc.gpsimd.dma_start(sm_t[:], sm.rearrange("(p t) -> p t", t=PACK))
 
         idle = psum.tile([P, R], F32, name="y_bank", tag="y_bank", bufs=4)
         for i in range(WARM_PASSES):
@@ -121,9 +122,9 @@ def tile_list_modp_gelu_res_noneb_kernel(
                 stop=True,
             )
 
-        picked_sc1 = placed("d", 0, [P, CHUNK], U8, "picked_sc1")
+        picked_sc1 = placed("d", 1600, [P, CHUNK], U8, "picked_sc1")
         gather_scales(picked_sc1[:], CHUNK, CHUNK)
-        picked_sc_rest = placed("d", CHUNK, [P, REST], U8, "picked_sc_rest")
+        picked_sc_rest = placed("d", 1856, [P, REST], U8, "picked_sc_rest")
         gather_scales(picked_sc_rest[:], 2 * CHUNK, REST)
         nc.vector.tensor_copy(stage_next[:, 0:CHUNK].bitcast(I32), picked_sc1[:].bitcast(I32))
 

@@ -25,7 +25,7 @@ QUARTER = 64
 REST = J - 2 * CHUNK
 BLOCKS = N // P
 ROWS0 = 96
-WARM_PASSES = 7
+WARM_PASSES = 6
 WARM_COLUMNS = 32
 PAGE_BYTES = 4 * T
 LAP = 64
@@ -55,13 +55,13 @@ def tile_list_modp_gelu_res_noneb_kernel(
         nc.sync.dma_start(offsets[:], offs)
         tab_sc = sbuf([P, T], U8, "tab_sc")
         nc.scalar.dma_start(tab_sc[ROWS0:P, :].bitcast(I32), tab_scales.rearrange("a q t -> q a t").bitcast(I32))
-        stage_next = sbuf([P, CHUNK + N], U8, "stage_next")
-        nc.sync.dma_start(stage_next[ROWS0:P:2, CHUNK:].bitcast(I32), wd4_scales[0].bitcast(I32))
-        wu_sc_raw = placed("d", 1472, [P, R], U8, "wu_sc_raw")
+        stage_next = sbuf([P, 2 * CHUNK + N], U8, "stage_next")
+        nc.sync.dma_start(stage_next[ROWS0:P:2, 2 * CHUNK :].bitcast(I32), wd4_scales[0].bitcast(I32))
+        wu_sc_raw = placed("d", 1984, [P, R], U8, "wu_sc_raw")
         nc.scalar.dma_start(wu_sc_raw[ROWS0:P, :].bitcast(I32), wu_scales.rearrange("a q r -> q a r").bitcast(I32))
         tab = sbuf([P, T], U32, "tab")
         nc.sync.dma_start(tab[:].bitcast(I32), tab_words[0].rearrange("p t i -> p (t i)").bitcast(I32))
-        nc.scalar.dma_start(stage_next[ROWS0 + 1 : P : 2, CHUNK:].bitcast(I32), wd8_scales[0].bitcast(I32))
+        nc.scalar.dma_start(stage_next[ROWS0 + 1 : P : 2, 2 * CHUNK :].bitcast(I32), wd8_scales[0].bitcast(I32))
         wu_raw = [sbuf([P, R], U32, "wu_raw%d" % a) for a in range(PASSES)]
         for a in range(PASSES):
             nc.sync.dma_start(wu_raw[a][:].bitcast(I32), wu_words[a].rearrange("p r i -> p (r i)").bitcast(I32))
@@ -80,7 +80,7 @@ def tile_list_modp_gelu_res_noneb_kernel(
         clear_beside_gpsimd(wu_sc_raw[0:ROWS0, :].bitcast(I32))
         planes_first = sbuf([P, 2 * (CHUNK + R)], U8, "planes_first")
         clear_beside_gpsimd(planes_first[:].bitcast(I32))
-        rest = sbuf([P, 2 * REST + 4 * REST], U8, "rest")
+        rest = sbuf([P, 2 * CHUNK + 4 * REST], U8, "rest")
         clear_beside_gpsimd(rest[:, 0 : 2 * R].bitcast(I32))
         nc.gpsimd.memset(rest[:, 2 * R : 4 * R].bitcast(I32), 0)
         pages = [sbuf([P, T], F32, "page0")]
@@ -105,9 +105,9 @@ def tile_list_modp_gelu_res_noneb_kernel(
         )
         nc.vector.tensor_copy(stage[:, 0:CHUNK].bitcast(I32), picked_sc0[:].bitcast(I32))
         spread(nc.scalar, planes_first[:], stage)
-        planes_next = placed("d", 0, [P, 2 * (CHUNK + N)], U8, "planes_next")
+        planes_next = placed("d", 0, [P, 2 * (2 * CHUNK + N)], U8, "planes_next")
         nc.gpsimd.memset(planes_next[:].bitcast(I32), 0)
-        sm_t = placed("d", 1536, [P, PACK], F32, "sm_t")
+        sm_t = placed("d", 2048, [P, PACK], F32, "sm_t")
         nc.gpsimd.dma_start(sm_t[:], sm.rearrange("(p t) -> p t", t=PACK))
 
         idle = psum.tile([P, R], F32, name="y_bank", tag="y_bank", bufs=4)
@@ -122,27 +122,25 @@ def tile_list_modp_gelu_res_noneb_kernel(
                 stop=True,
             )
 
-        picked_sc1 = placed("d", 1600, [P, CHUNK], U8, "picked_sc1")
-        gather_scales(picked_sc1[:], CHUNK, CHUNK)
-        picked_sc_rest = placed("d", 1856, [P, REST], U8, "picked_sc_rest")
-        gather_scales(picked_sc_rest[:], 2 * CHUNK, REST)
-        nc.vector.tensor_copy(stage_next[:, 0:CHUNK].bitcast(I32), picked_sc1[:].bitcast(I32))
+        picked_sc12 = placed("d", 2112, [P, 2 * CHUNK], U8, "picked_sc12")
+        gather_scales(picked_sc12[:], CHUNK, 2 * CHUNK)
+        nc.vector.tensor_copy(stage_next[:, 0 : 2 * CHUNK].bitcast(I32), picked_sc12[:].bitcast(I32))
 
         def wu_sc(a, t):
             at = a * (CHUNK + R) + CHUNK + t * P
             return planes_first[:, at : at + P]
 
         def wd_sc(tier, block):
-            at = tier * (CHUNK + N) + CHUNK + block * P
+            at = tier * (2 * CHUNK + N) + 2 * CHUNK + block * P
             return planes_next[:, at : at + P]
 
         def v_sc(a, j0, width):
             if j0 < CHUNK:
                 planes, at = planes_first, a * (CHUNK + R) + j0
-            elif j0 < 2 * CHUNK:
-                planes, at = planes_next, a * (CHUNK + N) + j0 - CHUNK
+            elif j0 < 3 * CHUNK:
+                planes, at = planes_next, a * (2 * CHUNK + N) + j0 - CHUNK
             else:
-                planes, at = rest, a * REST + j0 - 2 * CHUNK
+                planes, at = rest, a * CHUNK + j0 - 3 * CHUNK
             return planes[:, at : at + width]
 
         wu = [[sbuf([P, 2 * P], U32, "wu%d_%d" % (a, u)) for u in range(2)] for a in range(PASSES)]
@@ -189,7 +187,7 @@ def tile_list_modp_gelu_res_noneb_kernel(
         def h_codes(j0, width):
             if j0 < 2 * CHUNK:
                 return (h_first, h_next)[j0 // CHUNK][:, j0 % CHUNK : j0 % CHUNK + width].bitcast(FP8X4)
-            at = 2 * REST + 4 * (j0 - 2 * CHUNK)
+            at = 2 * CHUNK + 4 * (j0 - 2 * CHUNK)
             return rest[:, at : at + 4 * width].bitcast(FP8X4)
 
         def quantise(woven, j0, width):
@@ -276,6 +274,8 @@ def tile_list_modp_gelu_res_noneb_kernel(
         nc.gpsimd.memset(pages[1][:].bitcast(I32), 0)
         picked2 = placed("a", 8576, [P, CHUNK], U32, "picked2")
         gather(picked2[:], 2 * CHUNK, CHUNK)
+        picked_sc3 = placed("b", 3264, [P, CHUNK], U8, "picked_sc3")
+        gather_scales(picked_sc3[:], 3 * CHUNK, CHUNK)
 
         wd = placed("b", 0, [P, 6 * N], U8, "wd")
         wd8 = wd[:, 0 : 4 * N]
@@ -290,7 +290,7 @@ def tile_list_modp_gelu_res_noneb_kernel(
             nc.sync.dma_start(b_first[:], by_block[:, 0:1])
             nc.sync.dma_start(weight[:, 0:CHUNK], wgo[:, 0:CHUNK])
             nc.sync.dma_start(b_rest[:], by_block[:, 1:])
-        spread(nc.sync, rest[:, 0 : 2 * REST], picked_sc_rest)
+        spread(nc.sync, rest[:, 0 : 2 * CHUNK], picked_sc3)
         nc.sync.dma_start(weight[:, CHUNK:], wgo[:, CHUNK:])
 
         wovens = [placed("e", 0, [P, HALF * PACK], BF16, "woven0_0"), placed("f", 0, [P, HALF * PACK], BF16, "woven0_1")]

@@ -198,8 +198,8 @@ def tile_list_modp_gelu_res_noneb_kernel(
                 bank = up(v[half], c * CHUNK + half * HALF)
                 nc.scalar.activation(g[:, :, half * HALF : (half + 1) * HALF], bank[:], ACT.Gelu_apprx_tanh)
 
-        def smooth(slices, g):
-            for t in range(PACK):
+        def smooth(slices, g, ts=range(PACK)):
+            for t in ts:
                 nc.scalar.activation(slices[:, t * CHUNK : (t + 1) * CHUNK], g[:, t, :], ACT.Copy, scale=sm_t[:, t : t + 1])
             return slices
 
@@ -335,12 +335,13 @@ def tile_list_modp_gelu_res_noneb_kernel(
 
         g = next_g(1)
         gelu(2, g, v2)
-        slices = smooth(slices_of(2), g)
+        slices = smooth(slices_of(2), g, range(2))
         spent = g
         place(0, spent[:, 0, :], CHUNK)
+        smooth(slices, g, range(2, PACK))
+        place(1, spent[:, 2, :], CHUNK)
         weave(2, slices)
-        place(1, spent[:, 1, :], CHUNK)
-        place(2, spent[:, 2, :], CHUNK)
+        place(2, spent[:, 1, :], CHUNK)
 
         g = next_g(2)
         gelu(3, g, v3)

from contextlib import ExitStack

import concourse.mybir as mybir

K, R, N, T, J = 1024, 512, 512, 2048, 1024
FLOPS = 2 * K * R * J + 2 * 2 * R * N * J

F32 = mybir.dt.float32
BF16 = mybir.dt.bfloat16
I32 = mybir.dt.int32
U32 = mybir.dt.uint32
U16 = mybir.dt.uint16
U8 = mybir.dt.uint8
FP8X4 = mybir.dt.float8_e4m3fn_x4
FP4X4 = mybir.dt.float4_e2m1fn_x4
ACT = mybir.ActivationFunctionType
MULT = mybir.AluOpType.mult

P = 128
PACK = 4
PASSES = K // (P * PACK)
CHUNK = 256
HALF = 128
QUARTER = 64
REST = J - 2 * CHUNK
BLOCKS = N // P
ROWS0 = 96
WARM_PASSES = 6
WARM_COLUMNS = 32
PAGE_BYTES = 4 * T
LAP = 64
AT_FIRST_CODES = 4 * PACK * CHUNK


def tile_list_modp_gelu_res_noneb_kernel(
    tc, tab_words, tab_scales, wu_words, wu_scales, sm, wd4_words, wd4_scales, wd8_words, wd8_scales, b, wgo, offs, out
):
    nc = tc.nc
    with ExitStack() as ctx:
        lists = ctx.enter_context(tc.tile_pool(name="lists", bufs=1))
        free = ctx.enter_context(tc.tile_pool(name="free", bufs=1))
        psum = ctx.enter_context(tc.psum_pool(name="psum", bufs=1))
        arenas = {name: ctx.enter_context(tc.tile_pool(name=name, bufs=1)) for name in ("a", "b", "d", "e", "f", "hidden")}

        def sbuf(shape, dtype, name, tag=None):
            return free.tile(shape, dtype, name=name, tag=tag or name, align_bytes=64)

        def placed(arena, at, shape, dtype, name):
            return arenas[arena].tile(shape, dtype, name=name, offset=at, align_bytes=64)

        def entries(j0, width):
            return offsets[:, j0 // 16 : (j0 + width) // 16]

        offsets = lists.tile([P, J // 16], U16, name="offsets")
        nc.sync.dma_start(offsets[:], offs)
        tab_sc = sbuf([P, T], U8, "tab_sc")
        nc.scalar.dma_start(tab_sc[ROWS0:P, :].bitcast(I32), tab_scales.rearrange("a q t -> q a t").bitcast(I32))
        stage_next = sbuf([P, 2 * CHUNK + N], U8, "stage_next")
        nc.sync.dma_start(stage_next[ROWS0:P:2, 2 * CHUNK :].bitcast(I32), wd4_scales[0].bitcast(I32))
        wu_sc_raw = placed("d", 1984, [P, R], U8, "wu_sc_raw")
        nc.scalar.dma_start(wu_sc_raw[ROWS0:P, :].bitcast(I32), wu_scales.rearrange("a q r -> q a r").bitcast(I32))
        tab = sbuf([P, T], U32, "tab")
        nc.sync.dma_start(tab[:].bitcast(I32), tab_words[0].rearrange("p t i -> p (t i)").bitcast(I32))
        nc.scalar.dma_start(stage_next[ROWS0 + 1 : P : 2, 2 * CHUNK :].bitcast(I32), wd8_scales[0].bitcast(I32))
        wu_raw = [sbuf([P, R], U32, "wu_raw%d" % a) for a in range(PASSES)]
        for a in range(PASSES):
            nc.sync.dma_start(wu_raw[a][:].bitcast(I32), wu_words[a].rearrange("p r i -> p (r i)").bitcast(I32))

        zero = placed("hidden", AT_FIRST_CODES, [P, 1], F32, "zero")
        nc.vector.memset(zero[:], 0.0)
        unread = sbuf([P, 1], F32, "unread")
        nc.scalar.activation(unread[:], zero[:], ACT.Gelu_apprx_tanh)

        def clear_beside_gpsimd(words):
            cut = words.shape[1] // 2 - 1
            nc.vector.memset(words[:, 0:cut], 0)
            nc.vector.memset(words[:, cut:], 0)

        clear_beside_gpsimd(tab_sc[0:ROWS0, :].bitcast(I32))
        clear_beside_gpsimd(wu_sc_raw[0:ROWS0, :].bitcast(I32))
        planes_first = sbuf([P, 2 * (CHUNK + R)], U8, "planes_first")
        clear_beside_gpsimd(planes_first[:].bitcast(I32))
        rest = sbuf([P, 2 * CHUNK + 4 * REST], U8, "rest")
        clear_beside_gpsimd(rest[:, 0 : 2 * R].bitcast(I32))
        nc.gpsimd.memset(rest[:, 2 * R : 4 * R].bitcast(I32), 0)
        pages = [sbuf([P, T], F32, "page0")]
        nc.gpsimd.memset(pages[0][:].bitcast(I32), 0)

        def gather_scales(picked, j0, width):
            nc.vector.tensor_copy(picked, tab_sc[:].indirect(entries(j0, width)))

        def spread(queue, planes, rows):
            for q in (0, 2, 1, 3):
                queue.dma_start(
                    planes[32 * q : 32 * q + 4, :].bitcast(I32).rearrange("p (a n) -> p a n", a=2),
                    rows[ROWS0 + 8 * q : ROWS0 + 8 * q + 8, :].bitcast(I32),
                )

        stage = sbuf([P, CHUNK + R], U8, "stage")
        picked_sc0 = sbuf([P, CHUNK], U8, "picked_sc0")
        gather_scales(picked_sc0[:], 0, CHUNK)
        nc.vector.tensor_copy(
            stage[:, CHUNK : CHUNK + R].rearrange("p (t c i) -> p c t i", t=PACK, i=16),
            wu_sc_raw[:].rearrange("p (c i t) -> p c t i", t=PACK, i=16),
        )
        nc.vector.tensor_copy(stage[:, 0:CHUNK].bitcast(I32), picked_sc0[:].bitcast(I32))
        spread(nc.scalar, planes_first[:], stage)
        planes_next = placed("d", 0, [P, 2 * (2 * CHUNK + N)], U8, "planes_next")
        nc.gpsimd.memset(planes_next[:].bitcast(I32), 0)
        sm_t = placed("d", 2048, [P, PACK], F32, "sm_t")
        nc.gpsimd.dma_start(sm_t[:], sm.rearrange("(p t) -> p t", t=PACK))

        idle = psum.tile([P, R], F32, name="y_bank", tag="y_bank", bufs=4)
        for i in range(WARM_PASSES):
            nc.tensor.matmul_mx(
                out=idle[0:WARM_COLUMNS, :],
                lhsT=rest[:, 0 : 4 * WARM_COLUMNS].bitcast(FP8X4),
                lhsT_scale=picked_sc0[:, 0:WARM_COLUMNS],
                rhs=rest[:, 0 : 4 * R].bitcast(FP8X4),
                rhs_scale=tab_sc[:, 0:R],
                start=True,
                stop=True,
            )

        picked_sc12 = placed("d", 2112, [P, 2 * CHUNK], U8, "picked_sc12")
        gather_scales(picked_sc12[:], CHUNK, 2 * CHUNK)
        nc.vector.tensor_copy(stage_next[:, 0 : 2 * CHUNK].bitcast(I32), picked_sc12[:].bitcast(I32))

        def wu_sc(a, t):
            at = a * (CHUNK + R) + CHUNK + t * P
            return planes_first[:, at : at + P]

        def wd_sc(tier, block):
            at = tier * (2 * CHUNK + N) + 2 * CHUNK + block * P
            return planes_next[:, at : at + P]

        def v_sc(a, j0, width):
            if j0 < CHUNK:
                planes, at = planes_first, a * (CHUNK + R) + j0
            elif j0 < 3 * CHUNK:
                planes, at = planes_next, a * (2 * CHUNK + N) + j0 - CHUNK
            else:
                planes, at = rest, a * CHUNK + j0 - 3 * CHUNK
            return planes[:, at : at + width]

        wu = [[sbuf([P, 2 * P], U32, "wu%d_%d" % (a, u)) for u in range(2)] for a in range(PASSES)]
        for a in range(PASSES):
            for u in range(2):
                nc.scalar.copy(
                    wu[a][u][:].rearrange("p (t c i) -> p c t i", t=2, i=4),
                    wu_raw[a][:].rearrange("p (c i t) -> p c t i", t=PACK, i=4)[:, :, 2 * u : 2 * u + 2, :],
                )

        spread(nc.sync, planes_next[:], stage_next)

        def gather(picked, j0, width):
            nc.vector.tensor_copy(picked, tab[:].indirect(entries(j0, width)))

        def part(v, picked):
            nc.vector.tensor_copy(v.bitcast(U16), picked.bitcast(U16).rearrange("p (j a) -> p a j", a=PASSES))

        def up(v, j0):
            bank = psum.tile([P, PACK, HALF], F32, name="a_bank", tag="a_bank", bufs=4)
            for a in range(PASSES):
                for t in range(PACK):
                    nc.tensor.matmul_mx(
                        out=bank[:, t, :],
                        lhsT=wu[a][t // 2][:, t % 2 * P : (t % 2 + 1) * P].bitcast(FP8X4),
                        lhsT_scale=wu_sc(a, t),
                        rhs=v[:, a, :].bitcast(FP4X4),
                        rhs_scale=v_sc(a, j0, HALF),
                        start=(a == 0 and t == 0),
                        stop=(a == PASSES - 1 and t == PACK - 1),
                    )
            return bank

        slices_bytes = 2 * PACK * CHUNK
        g_bytes = 4 * PACK * CHUNK

        def at_slices(c):
            return g_bytes + (c - 1) * (slices_bytes + 2 * g_bytes)

        h_first = placed("hidden", at_slices(1), [P, CHUNK], U32, "h_first")
        h_next = sbuf([P, CHUNK], U32, "h_next")
        h_sc = sbuf([P, J], U8, "h_sc")

        def h_codes(j0, width):
            if j0 < 2 * CHUNK:
                return (h_first, h_next)[j0 // CHUNK][:, j0 % CHUNK : j0 % CHUNK + width].bitcast(FP8X4)
            at = 2 * CHUNK + 4 * (j0 - 2 * CHUNK)
            return rest[:, at : at + 4 * width].bitcast(FP8X4)

        def quantise(woven, j0, width):
            nc.vector.quantize_mx(out=h_codes(j0, width), scales=h_sc[:, j0 : j0 + width], in_=woven)

        def gelu(c, g, v):
            for half in range(2):
                bank = up(v[half], c * CHUNK + half * HALF)
                nc.scalar.activation(g[:, :, half * HALF : (half + 1) * HALF], bank[:], ACT.Gelu_apprx_tanh)

        def smooth(slices, g, ts=range(PACK)):
            for t in ts:
                nc.scalar.activation(slices[:, t * CHUNK : (t + 1) * CHUNK], g[:, t, :], ACT.Copy, scale=sm_t[:, t : t + 1])
            return slices

        def slices_of(c):
            return placed("hidden", at_slices(c), [P, PACK * CHUNK], BF16, "slices%d" % c)

        def weave(c, slices):
            woven = sbuf([P, CHUNK * PACK], BF16, "woven%d" % c)
            nc.scalar.copy(
                woven[:].rearrange("p (c i t) -> p c t i", t=PACK, i=4),
                slices[:].rearrange("p (t c i) -> p c t i", t=PACK, i=4),
            )
            quantise(woven[:], c * CHUNK, CHUNK)

        def next_g(c):
            return placed("hidden", at_slices(c) + LAP - g_bytes, [P, PACK, CHUNK], F32, "g%d" % (c + 1))

        def cover_y(c, i):
            return placed("hidden", at_slices(c) + LAP + 4 * CHUNK * i, [P, CHUNK], F32, "y_cover%d_%d" % (c, i))

        def down(block, j0, width):
            bank = psum.tile([P, width], F32, name="y_bank", tag="y_bank", bufs=4)
            nc.tensor.matmul_mx(
                out=bank[:],
                lhsT=wd8[:, 4 * block * P : 4 * (block + 1) * P].bitcast(FP8X4),
                lhsT_scale=wd_sc(1, block),
                rhs=h_codes(j0, width),
                rhs_scale=h_sc[:, j0 : j0 + width],
                start=True,
                stop=False,
            )
            nc.tensor.matmul_mx(
                out=bank[:],
                lhsT=wd4[:, 2 * block * P : 2 * (block + 1) * P].bitcast(FP4X4),
                lhsT_scale=wd_sc(0, block),
                rhs=h_codes(j0, width),
                rhs_scale=h_sc[:, j0 : j0 + width],
                start=False,
                stop=True,
            )
            return bank

        def add_bias(y, bank, block):
            nc.scalar.activation(y, bank[:], ACT.Identity, bias=b_first[:] if block == 0 else b_rest[:, block - 1 : block])

        def scatter(block, y, j0, width):
            page = pages[block]
            nc.vector.tensor_tensor(page[:].indirect(entries(j0, width)), y, weight[:, j0 : j0 + width], MULT)
            if j0 + width == J:
                nc.sync.dma_start(out[block * P : (block + 1) * P, :], page[:])

        def place(block, y, j0, width=CHUNK, bank=None):
            add_bias(y, down(block, j0, width) if bank is None else bank, block)
            scatter(block, y, j0, width)

        def halves_of(v):
            return [v[:, :, 2 * half * HALF : 2 * (half + 1) * HALF] for half in range(2)]

        picked0 = [placed("a", 7872, [P, HALF], U32, "picked0_0"), placed("b", 3008, [P, HALF], U32, "picked0_1")]
        v0 = [sbuf([P, PASSES, 2 * HALF], U8, "v0_%d" % half) for half in range(2)]
        for half in range(2):
            gather(picked0[half][:], half * HALF, HALF)
        for half in range(2):
            part(v0[half][:], picked0[half][:])
        picked1 = [placed("a", 8128, [P, HALF], U32, "picked1_0"), placed("b", 3456, [P, HALF], U32, "picked1_1")]
        v1 = [sbuf([P, PASSES, 2 * HALF], U8, "v1_%d" % half)[:] for half in range(2)]
        for half in range(2):
            gather(picked1[half][:], CHUNK + half * HALF, HALF)
        for half in range(2):
            part(v1[half], picked1[half][:])
        pages.append(placed("a", 0, [P, T], F32, "page1"))
        nc.gpsimd.memset(pages[1][:].bitcast(I32), 0)
        picked2 = placed("a", 8576, [P, CHUNK], U32, "picked2")
        gather(picked2[:], 2 * CHUNK, CHUNK)
        picked_sc3 = placed("b", 3264, [P, CHUNK], U8, "picked_sc3")
        gather_scales(picked_sc3[:], 3 * CHUNK, CHUNK)

        wd = placed("b", 0, [P, 6 * N], U8, "wd")
        wd8 = wd[:, 0 : 4 * N]
        wd4 = wd[:, 4 * N : 6 * N]
        nc.sync.dma_start(wd8.bitcast(I32), wd8_words[0].rearrange("p n i -> p (n i)").bitcast(I32))
        nc.sync.dma_start(wd4.bitcast(I32), wd4_words[0].bitcast(I32))
        b_first = placed("b", 3584, [P, 1], F32, "b_first")
        b_rest = placed("b", 3648, [P, BLOCKS - 1], F32, "b_rest")
        weight = placed("b", 3904, [P, J], F32, "weight")
        by_block = b.rearrange("(c p) -> p c", p=P)
        with nc.allow_non_contiguous_dma(reason="one bias value a partition and block"):
            nc.sync.dma_start(b_first[:], by_block[:, 0:1])
            nc.sync.dma_start(weight[:, 0:CHUNK], wgo[:, 0:CHUNK])
            nc.sync.dma_start(b_rest[:], by_block[:, 1:])
        spread(nc.sync, rest[:, 0 : 2 * CHUNK], picked_sc3)
        nc.sync.dma_start(weight[:, CHUNK:], wgo[:, CHUNK:])

        wovens = [placed("e", 0, [P, HALF * PACK], BF16, "woven0_0"), placed("f", 0, [P, HALF * PACK], BF16, "woven0_1")]
        for half in range(2):
            bank = up(v0[half][:], half * HALF)
            for i in range(2):
                g = sbuf([P, QUARTER, PACK], F32, "g0_%d%d" % (half, i))
                sums = bank[:, :, i * QUARTER : (i + 1) * QUARTER].rearrange("p t j -> p j t")
                nc.scalar.activation(g[:], sums, ACT.Gelu_apprx_tanh, bias=zero[:])
                nc.vector.tensor_tensor(
                    wovens[half][:, i * QUARTER * PACK : (i + 1) * QUARTER * PACK].rearrange("p (j t) -> p j t", t=PACK),
                    g[:],
                    sm_t[:].unsqueeze(1).to_broadcast([P, QUARTER, PACK]),
                    MULT,
                )
        for half in range(2):
            quantise(wovens[half][:], half * HALF, HALF)
        picked3 = placed("e", 0, [P, CHUNK], U32, "picked3")
        gather(picked3[:], 3 * CHUNK, CHUNK)
        whole2 = placed("f", 960, [P, PASSES, 2 * CHUNK], U8, "v2")
        part(whole2[:], picked2[:])
        whole3 = sbuf([P, PASSES, 2 * CHUNK], U8, "v3")
        part(whole3[:], picked3[:])
        v2, v3 = halves_of(whole2), halves_of(whole3)
        pages.append(placed("a", 9536, [P, T], F32, "page2"))
        pages.append(placed("e", 960, [P, T], F32, "page3"))
        for block in range(2, BLOCKS):
            nc.gpsimd.memset(pages[block][:].bitcast(I32), 0)

        g = sbuf([P, PACK, CHUNK], F32, "g1")
        gelu(1, g, v1)
        y = sbuf([P, CHUNK], F32, "y_first")
        for half in range(2):
            add_bias(y[:, half * HALF : (half + 1) * HALF], down(0, half * HALF, HALF), 0)
        scatter(0, y[:], 0, CHUNK)
        sums = [down(block, 0, CHUNK) for block in range(1, BLOCKS)]
        place(1, sbuf([P, CHUNK], F32, "y0_1")[:], 0, bank=sums[0])
        slices = smooth(slices_of(1), g)
        place(2, sbuf([P, CHUNK], F32, "y0_2")[:], 0, bank=sums[1])
        weave(1, slices)
        place(3, cover_y(1, 0)[:], 0, bank=sums[2])

        g = next_g(1)
        gelu(2, g, v2)
        slices = smooth(slices_of(2), g, range(2))
        spent = g
        place(0, spent[:, 0, :], CHUNK)
        smooth(slices, g, range(2, PACK))
        place(1, spent[:, 2, :], CHUNK)
        weave(2, slices)
        place(2, spent[:, 1, :], CHUNK)

        g = next_g(2)
        gelu(3, g, v3)
        place(3, spent[:, 3, :], CHUNK)
        weave(3, smooth(slices_of(3), g))
        for block in range(2):
            place(block, cover_y(3, block)[:], 2 * CHUNK)
        for block in range(2):
            place(block, g[:, block, :], 3 * CHUNK)
        for block in range(2, BLOCKS):
            place(block, sbuf([P, 2 * CHUNK], F32, "y_wide%d" % block)[:], 2 * CHUNK, 2 * CHUNK)
